import numpy as np, ml_dtypes
CORES = [78,86,94,102,110,118]
N = 6
BF = ml_dtypes.bfloat16
B, LE, LP, M, ST, RO, TH = 1920, 208, 48, 144, 3, 2, 49152
E = RO * LE + LP
W = B + RO * ST * M
def parts(rng):
    c = (65536 * rng.random((N, 8, 16, B)) * np.exp2(-1.0 * rng.integers(0, 7, (N, 8, 1, B)))).astype(np.int64)
    return c, rng.integers(0, B, (N, 8, 16, B))
def starts(rng, c, share):
    e = np.where(rng.random((N, 8, 1, E)) < share, rng.integers(0, 3, (N, 8, 1, E)), rng.integers(4, 9, (N, 8, 1, E)))
    c[..., B - E:] = (65536 * rng.random((N, 8, 16, E)) * np.exp2(-1.0 * e)).astype(np.int64)
    return c
def pack(c, s):
    return {"c0": np.ascontiguousarray(c.reshape(N, 128, B)).astype(np.int32), "s0": np.ascontiguousarray(s.reshape(N, 128, B)).astype(np.int32)}
def setup_inputs(rng):
    c, s = parts(rng)
    return pack(starts(rng, c, rng.choice(np.array([0.4, 0.7, 0.9, 1.0]), (N, 8, 1, 1))), s)
def setup_inputs_room(rng):
    c, s = parts(rng); c = starts(rng, c, 0.8)
    for q in range(N):
        for g in range(8):
            n = int(rng.choice(np.array([0, 1, M - 1, M, M + 1, LE]))); z = int(rng.choice(np.array([0, 1, LP - 1, LP, LP + 1, M])))
            if q == 0: n = (M, M + 1, LE, M - 1, M, 1, 0, M)[g]; z = (LP, LP + 1, M, LP - 1, 0, 1, 0, 1)[g]
            live = min(n, M); z = min(z, live)
            pool = rng.permutation(B - E); ch = pool[:ST * LE].reshape(ST, LE); nil = pool[ST * LE:ST * LE + 64]; ent = B - E + np.arange(LE)
            who = np.sort(rng.permutation(LE)[:n]); drop = np.delete(who[:M], rng.permutation(live)[:z])
            c[q, g][:, ent] = 0; c[q, g][:, ent[who]] = rng.integers(30000, 65536, (16, n))
            c[q, g][:, ch.reshape(-1)] = rng.integers(20000, 65536, (16, ST * LE)); c[q, g][:, nil] = 0
            c[q, g][:, ch[ST - 1][drop]] = 0
            prev = ent
            for st in range(ST):
                own = np.where(rng.random((16, LE)) < 0.4, ch[st][None, :], rng.choice(nil, (16, LE)))
                own[rng.integers(0, 16, LE), np.arange(LE)] = ch[st]
                s[q, g][:, prev] = own; prev = ch[st]
    return pack(c, s)
def setup_inputs_ties(rng):
    c, s = parts(rng); u = TH // 16
    one = (np.arange(16).reshape(1, 1, 16, 1) == rng.integers(0, 16, (N, 8, 1, B))).astype(np.int64)
    full = rng.random((N, 8, 1, B)) < np.array([0.05, 0.1, 0.2, 0.5, 0.05, 0.1, 0.2, 0.5]).reshape(1, 8, 1, 1)
    c = np.where(full, u, u - one); c = np.where(rng.random((N, 8, 1, B)) < 0.1, 0, c)
    big = rng.random((N, 8, 1, B)) < 0.1; big[:, :4] = False; c = np.where(big, 65535, c)
    c[..., B - E:] = np.where(rng.random((N, 8, 1, E)) < 0.7, 65535, u - one[..., B - E:] * rng.integers(0, 2, (N, 8, 1, E)))
    s[:, :4] = rng.integers(0, B - E, (N, 4, 16, B))
    return pack(c, s)
def setup_inputs_alike(rng):
    c, s = parts(rng); c = starts(rng, c, 0.85)
    for q in range(N):
        for g in range(8):
            h = (1, 2, 17, 64, 160, 300, B // 4, B)[(g + q) % 8]
            s[q, g] = rng.permutation(B)[:h][rng.integers(0, h, (16, B))]
    s = np.where(rng.random(s.shape) < 0.1, np.arange(B), s)
    ends = rng.random(s.shape) < 0.05; ends[:, ::2] = False
    s = np.where(ends, rng.choice(np.array([0, B - 1]), s.shape), s); c[:, 1::2, :, 0] = 65535; c[:, 1::2, :, B - 1] = 65535
    return pack(c, s)
def setup_inputs_links(rng):
    c, s = parts(rng); c = c >> 3; c = starts(rng, c, 0.9)
    near = rng.random(s.shape) < 0.5; near[:, ::2] = True
    return pack(c, np.where(near, rng.integers(B - E, B, s.shape), s))
def setup_inputs_spread(rng):
    c, s = parts(rng); lo = rng.choice(np.array([0.0, 6.0, 10.0]), (N, 8, 1, 1))
    c = np.minimum((np.exp2(lo + (16.0 - lo) * rng.random((N, 8, 1, B))) * rng.random((N, 8, 16, B))).astype(np.int64), 65535)
    c[:, :, :, B - E::7] = rng.integers(0, 65536, c[:, :, :, B - E::7].shape)
    v = rng.random((N, 4, 16, B)); s[:, 1::2] = np.minimum((B * v * v).astype(np.int64), B - 1)
    return pack(c, s)
def check_inputs(d):
    bad = []
    for k, hi in (("c0", 65535), ("s0", B - 1)):
        if np.min(d[k]) < 0 or np.max(d[k]) > hi: bad.append("range of " + k)
    return bad
def reference(c0, s0):
    C = np.zeros((N, 8, 16, W), np.int64); S = np.zeros((N, 8, 16, W), np.int64)
    C[..., :B] = c0.reshape(N, 8, 16, B); S[..., :B] = s0.reshape(N, 8, 16, B)
    port = np.zeros((N, 8, 16, LP), np.int64)
    for rnd in range(RO):
        x = np.concatenate([B - E + rnd * LE + np.arange(LE), B - LP + np.arange(LP)])
        c = np.concatenate([C[..., x[:LE]], port], axis=3)
        for st in range(ST):
            b = B + (rnd * ST + st) * M
            sx = S[..., x]
            score = np.stack([np.add.reduce(np.minimum(c, np.take_along_axis(C, sx[:, :, i][:, :, None, :], 3)), axis=2) for i in range(16)], axis=2)
            k = np.argmax(score, axis=2); best = np.max(score, axis=2)
            y = np.take_along_axis(sx, k[:, :, None, :], 2)[:, :, 0]
            for a in range(N):
                for g in range(8):
                    l = np.flatnonzero(best[a, g] >= TH)
                    l = l[np.sort(np.unique(y[a, g, l], return_index=True)[1])][:M]
                    n = b + np.arange(l.size); yy = y[a, g, l]
                    m = np.minimum(c[a, g][:, l], C[a, g][:, yy]); old = S[a, g][:, yy]
                    C[a, g][:, yy] -= m
                    C[a, g][:, n] = m; S[a, g][:, n] = old
                    S[a, g][k[a, g, l], x[l]] = n
            x = b + np.arange(M); c = np.array(C[..., b:b + M])
        port = np.roll(c[..., :LP], 1, axis=0)
    return {"yc": C.reshape(N, 128, W).astype(np.float32), "ys": np.ascontiguousarray(S[..., B - E:]).reshape(N, 128, W - B + E).astype(np.float32)}

@@ -1,0 +1,533 @@
+from concourse.mybir import dt, AluOpType, AxisListType, ActivationFunctionType
+
+B, LE, LP, M, ST, RO, TH = 1920, 208, 48, 144, 3, 2, 49152
+U = RO * ST
+E0 = B - RO * LE - LP
+N0 = B + 1
+WIN = N0 + U * M
+DUMP = WIN
+CW = 3168
+T16 = float(16 * TH)
+BIG = 33554432.0
+FAR = 4000.0
+SPW = 14080
+MC = 112
+
+SCRATCH = {
+    "CI": ("sbuf", [128, B], "int32"), "SI": ("sbuf", [128, B], "int32"),
+    "Cw": ("sbuf", [128, CW], "float32"), "Sw": ("sbuf", [128, 2800], "float32"),
+    "SP": ("sbuf", [128, SPW], "float32"), "SQ": ("sbuf", [128, SPW], "float32"), "HM": ("sbuf", [128, 1280], "bfloat16"),
+    "CR": ("sbuf", [128, 4096], "float32"), "MG": ("sbuf", [128, 4096], "float32"),
+    "RB": ("sbuf", [128, 256], "float32"), "RK": ("sbuf", [128, 128], "float32"),
+    "PT": ("sbuf", [128, 256], "float16"), "WF": ("sbuf", [128, 256], "float32"),
+    "YW": ("sbuf", [128, 18], "uint16"), "YP": ("sbuf", [128, 16], "float32"),
+    "WS": ("sbuf", [128, 16], "float32"), "WX": ("sbuf", [128, 16], "float32"),
+    "EQ": ("sbuf", [128, 4096], "bfloat16"),
+    "CY": ("sbuf", [128, 256], "float32"), "SY": ("sbuf", [128, 256], "float32"), "MM": ("sbuf", [128, 256], "float32"),
+    "FK": ("sbuf", [128, 256], "float32"), "AW": ("sbuf", [128, 16], "bfloat16"), "EX": ("sbuf", [128, 24], "bfloat16"),
+    "AL": ("sbuf", [128, 16], "float16"), "CN": ("sbuf", [128, 16], "float32"), "TN": ("sbuf", [128, 16], "float32"),
+    "TO": ("sbuf", [128, 16], "float32"), "OFM": ("sbuf", [128, 16], "uint16"),
+    "OFY": ("sbuf", [128, 16], "uint16"), "LV": ("sbuf", [128, 16], "bfloat16"),
+    "P1": ("sbuf", [128, 16], "bfloat16"), "P2": ("sbuf", [128, 16], "bfloat16"),
+    "T1": ("sbuf", [128, 256], "float32"), "T2": ("sbuf", [128, 1328], "float32"), "YS": ("sbuf", [128, 1328], "float32"),
+    "PORT": ("sbuf", [128, LP], "float32"), "PS": ("sbuf", [128, LP], "float32"),
+    "ON": ("sbuf", [128, 512], "float32"), "FR": ("sbuf", [128, 256], "float32"), "ONB": ("sbuf", [128, 2048], "bfloat16"),
+    "ONK": ("sbuf", [128, 128], "bfloat16"), "KC": ("sbuf", [128, 128], "bfloat16"),
+    "IDF": ("sbuf", [128, 128], "float32"), "IDB": ("sbuf", [128, 128], "bfloat16"), "IDH": ("sbuf", [128, 128], "float16"),
+    "BOX": ("sbuf", [128, 128], "float32"), "BOF": ("sbuf", [128, 128], "float32"), "BOB": ("sbuf", [128, 128], "bfloat16"),
+    "BOH": ("sbuf", [128, 128], "float16"), "BG": ("sbuf", [128, 8], "float32"),
+    "TSF": ("sbuf", [128, 128], "float32"), "TSB": ("sbuf", [128, 128], "bfloat16"),
+    "TIF": ("sbuf", [128, 128], "float32"), "TIB": ("sbuf", [128, 128], "bfloat16"),
+    "DL": ("sbuf", [128, 128], "bfloat16"), "DC": ("sbuf", [128, 256], "bfloat16"),
+    "DLF": ("sbuf", [128, 128], "float32"), "DCF": ("sbuf", [128, 256], "float32"),
+    "LIF": ("sbuf", [128, 16], "float32"), "LIH": ("sbuf", [128, 16], "float16"), "NLI": ("sbuf", [128, 16], "float32"),
+    "D2": ("sbuf", [128, 16], "float32"), "ON16": ("sbuf", [128, 16], "float32"), "BS": ("sbuf", [128, 2048], "bfloat16"),
+    "KP0": ("psum", [128, 512], "float32"), "KP1": ("psum", [128, 512], "float32"), "OT": ("psum", [128, 512], "float32"),
+    "YB": ("psum", [128, 512], "float32"), "YD": ("psum", [128, 512], "float32"), "KL": ("psum", [128, 512], "float32"),
+    "RR": ("psum", [128, 512], "float32"), "NB": ("psum", [128, 512], "float32"),
+}
+for _i in range(2):
+    SCRATCH["FF%d" % _i] = ("sbuf", [128, 128], "float32")
+    SCRATCH["SK%d" % _i] = ("sbuf", [128, 128], "float32")
+    SCRATCH["MX%d" % _i] = ("sbuf", [128, 128], "float32")
+    SCRATCH["OH%d" % _i] = ("sbuf", [128, 128], "bfloat16")
+    SCRATCH["OS%d" % _i] = ("sbuf", [128, 256], "float32")
+for _i in range(U):
+    SCRATCH["SU%d" % _i] = ("sbuf", [128, 256], "uint16")
+    SCRATCH["SF%d" % _i] = ("sbuf", [128, 256], "float16")
+NDMA = 24
+SEMAPHORES = ["qv", "qt", "qa", "qg", "arr", "left"] + ["d%d" % i for i in range(NDMA)]
+
+
+def rank_program(g, core, T, topo):
+    rank = T.rank_of(core)
+    if rank is None:
+        return
+    Op, Act = AluOpType, ActivationFunctionType
+    eng = {"v": g.vector, "t": g.tensor, "a": g.scalar, "g": g, "y": g.sync}
+    cnt, known, clock, hist, inc = {}, {q: {} for q in eng}, {}, {}, {}
+    psum = {n for n in SCRATCH if SCRATCH[n][0] == "psum"}
+
+    def X(name, c0, c1, step=1, p=128):
+        ap = T[name][0:p, c0:c1] if step == 1 else T[name][0:p, c0:c1:step]
+        return (name, c0, c1, step, ap, None)
+
+    def IND(x, off):
+        return (x[0], x[1], x[2], 1, x[4].indirect(off[4]), off)
+
+    def semname(q):
+        return {"v": "qv", "t": "qt", "a": "qa", "g": "qg"}.get(q, q)
+
+    def emit(q, call, outs, ins, sem=None, n=1):
+        acc = [(o, True) for o in outs] + [(i, False) for i in ins]
+        acc += [(o[5], False) for o in list(outs) + list(ins) if o[5] is not None]
+        need = {}
+        for (o, w) in acc:
+            name, c0, c1, st = o[0:4]
+            for (q2, n2, d0, d1, s2, w2) in hist.get(name, []):
+                if name in psum and q2 != q:
+                    pass
+                elif name in psum and q == "t":
+                    continue
+                elif not (w or w2) or d1 <= c0 or c1 <= d0:
+                    continue
+                elif st == s2 and st > 1 and c0 % st != d0 % st:
+                    continue
+                need[q2] = max(need.get(q2, 0), n2)
+        kn = known[q]
+        todo = [(q2, n2) for q2, n2 in need.items() if kn.get(q2, 0) < n2]
+        todo = [(q2, n2) for q2, n2 in todo
+                if not any((q3, n3) != (q2, n2) and clock[(q3, n3)].get(q2, 0) >= n2 for q3, n3 in todo)]
+        for q2, n2 in todo:
+            eng[q].wait_ge(T.sem[semname(q2)], n2 * inc[q2])
+            for k, v in clock[(q2, n2)].items():
+                kn[k] = max(kn.get(k, 0), v)
+        me = q if sem is None else sem
+        cnt[me] = cnt.get(me, 0) + 1
+        inc[me] = n
+        c = dict(kn)
+        c[me] = cnt[me]
+        clock[(me, cnt[me])] = c
+        for (o, w) in acc:
+            hist.setdefault(o[0], []).append((me, cnt[me], o[1], o[2], o[3], w))
+        inst = call()
+        if sem != "arr":
+            inst.then_inc(T.sem[semname(me)], n)
+
+    def act(out, in_, func, **kw):
+        emit("a", lambda: g.scalar.activation(out[4], in_[4], func, **kw), [out], [in_])
+
+    def copy(q, out, in_):
+        if q == "v":
+            emit("v", lambda: g.vector.tensor_copy(out[4], in_[4]), [out], [in_])
+        else:
+            act(out, in_, Act.Copy)
+
+    def tt(out, a, b, op):
+        emit("v", lambda: g.vector.tensor_tensor(out[4], a[4], b[4], op), [out], [a, b])
+
+    def ts(out, a, s1, op0, s2=None, op1=None):
+        col = isinstance(s1, tuple)
+        k = s1[4] if col else s1
+        ins = [a, s1] if col else [a]
+        if op1 is None:
+            emit("v", lambda: g.vector.tensor_scalar(out[4], a[4], k, None, op0), [out], ins)
+        else:
+            emit("v", lambda: g.vector.tensor_scalar(out[4], a[4], k, s2, op0, op1), [out], ins)
+
+    def scan(out, d0, d1, init, op0, op1):
+        emit("v", lambda: g.vector.tensor_tensor_scan(out[4], d0[4], d1[4], init, op0, op1), [out], [d0, d1])
+
+    def minima(out, d):
+        scan(out, X("RB", 0, out[2] - out[1]), d, 0.0, Op.max, Op.min)
+
+    def fill(out, c):
+        emit("v", lambda: g.vector.memset(out[4], c), [out], [])
+
+    def zero_a(out, like):
+        act(out, like, Act.Copy, scale=0.0)
+
+    def mm(out, lhsT, rhs, start, stop):
+        emit("t", lambda: g.tensor.matmul(out[4], lhsT[4], rhs[4], start, stop), [out], [lhsT, rhs])
+
+    def aff(out, in_, pattern, op, f, base, cm):
+        emit("g", lambda: g.affine_select(out[4], in_[4], pattern, op, f, base, cm), [out], [in_])
+
+    def copy_g(out, in_, n):
+        aff(out, in_, [[0, n]], Op.is_gt, 0.0, 1, 0)
+
+    def iota(out, pattern, base, cm):
+        emit("g", lambda: g.iota(out[4], pattern, base, cm, allow_small_or_imprecise_dtypes=True), [out], [])
+
+    ndma = [0]
+
+    def dma(q, out, in_):
+        s = "d%d" % ndma[0]
+        ndma[0] += 1
+        emit(q, lambda: eng[q].dma_start(out[4], in_[4]), [out], [in_], sem=s, n=16)
+
+    def D(name, c0, c1):
+        return (name, c0, c1, 1, T[name][:, c0:c1], None)
+
+    dma("a", X("CI", E0, B), D("c0", E0, B))
+    dma("y", X("SI", E0, B), D("s0", E0, B))
+    dma("a", X("CI", 736, E0), D("c0", 736, E0))
+    dma("y", X("CI", 0, 736), D("c0", 0, 736))
+    dma("y", X("SI", 0, E0), D("s0", 0, E0))
+
+    fill(X("ON", 0, 512), 1.0)
+    fill(X("HM", 0, 1280), 1.0)
+    fill(X("HM", 0, 1280, 16), 0.0)
+    fill(X("RK", 0, 128), BIG)
+    fill(X("RK", 0, 128, 16), T16)
+    fill(X("RB", 0, 256), -BIG)
+    fill(X("RB", 0, 256, 16), BIG)
+    fill(X("SK1", 0, 128), 0.0)
+    fill(X("SK0", 0, 128), 0.0)
+    fill(X("ON16", 0, 16), 1.0)
+    aff(X("BOX", 0, 128), X("ON", 0, 128), [[-16, 8], [0, 16]], Op.is_ge, 0.0, 0, 1)
+    aff(X("BOF", 0, 128), X("BOX", 0, 128), [[16, 8], [0, 16]], Op.is_ge, 0.0, 15, -1)
+    iota(X("KC", 0, 128, p=1), [[0, 8], [-1, 16]], 15, 0)
+    iota(X("ONK", 0, 128, p=1), [[0, 128]], 1, 0)
+    iota(X("FR", 0, 256, p=16), [[0, 256]], int(FAR), 0)
+    aff(X("IDF", 0, 128), X("ON", 0, 128), [[-1, 128]], Op.is_equal, 0.0, 0, 1)
+    aff(X("DLF", 0, 128, p=16), X("ON", 0, 128, p=16), [[0, 8], [1, 16]], Op.is_equal, 0.0, 0, -1)
+    aff(X("DCF", 0, 256, p=16), X("FR", 0, 256, p=16), [[0, 16], [1, 16]], Op.not_equal, 0.0, 0, -1)
+    aff(X("TSF", 0, 128), X("BOF", 0, 128), [[1, 128]], Op.is_gt, 0.0, 0, -1)
+    aff(X("TIF", 0, 128), X("BOF", 0, 128), [[1, 128]], Op.is_ge, 0.0, 0, -1)
+    iota(X("LIF", 0, 16), [[16, 16]], 256, 1)
+    iota(X("NLI", 0, 16), [[-16, 16]], -256, -1)
+    iota(X("D2", 0, 16), [[16, 16]], DUMP, 1)
+    copy_g(X("Cw", 0, E0), X("CI", 0, E0), E0)
+    copy_g(X("Sw", E0, B), X("SI", E0, B), B - E0)
+    copy_g(X("Sw", 0, E0), X("SI", 0, E0), E0)
+    iota(X("SQ", 0, 16 * M, 16), [[0, M]], 0, 0)
+    iota(X("ONB", 0, 2048), [[0, 2048]], 1, 0)
+    aff(X("BS", 0, 2048), X("ONB", 0, 2048), [[1, 16], [16, 8], [0, 16]], Op.is_equal, 0.0, 0, -1)
+    for a in range(0, 16 * M, 512):
+        zero_a(X("SP", a, min(a + 512, 16 * M)), X("ON", 0, min(512, 16 * M - a)))
+    zero_a(X("Cw", B, B + 512), X("ON", 0, 512))
+    zero_a(X("Cw", B + 512, WIN), X("ON", 0, WIN - B - 512))
+
+    copy("v", X("Cw", E0, B), X("CI", E0, B))
+
+    fillers = []
+    spare = []
+
+    def pop(n=1, more=False):
+        for _ in range(n):
+            if fillers:
+                fillers.pop(0)()
+            elif more and spare:
+                spare.pop(0)()
+
+    def ys_conv(c0, c1, src=None):
+        o = c0 - E0 if c1 <= B else c0 - 1 - E0
+        n = c1 - c0
+        s = src if src is not None else X("Sw", c0, c1)
+
+        def second():
+            tt(X("YS", o, o + n), s, X("T2", o, o + n), Op.subtract)
+            dma("y", D("ys", o, o + n), X("YS", o, o + n))
+        return [lambda: ts(X("T2", o, o + n), s, float(B) + 0.5, Op.is_gt), second]
+
+    def xcols(u):
+        t, e = divmod(u, ST)
+        if e:
+            return [(0, M, N0 + M * (u - 1))]
+        r = [(0, LE, E0 + LE * t)]
+        return r + [(LE, LP, B - LP)] if t else r
+
+    def s_update(u):
+        L = sum(n for _, n, _ in xcols(u))
+        r = [lambda: tt(X("T1", 0, L), X("OS%d" % (u % 2), 0, L), X("NB", 0, L), Op.mult)]
+        for l0, n, c in xcols(u):
+            r.append(lambda l0=l0, n=n, c=c: tt(X("Sw", c, c + n), X("Sw", c, c + n), X("T1", l0, l0 + n), Op.max))
+        return r
+
+    def src_c(u, l0, l1, rep=False):
+        t, e = divmod(u, ST)
+        if e:
+            if rep:
+                return [(l0, l1, X("SP", 16 * l0, 16 * l1, 16))]
+            return [(l0, l1, X("Cw", N0 + M * (u - 1) + l0, N0 + M * (u - 1) + l1))]
+        r = []
+        if l0 < LE:
+            a = min(l1, LE)
+            r.append((l0, a, X("Cw", E0 + LE * t + l0, E0 + LE * t + a)))
+        if l1 > LE:
+            a = max(l0, LE)
+            r.append((a, l1, X("PORT", a - LE, l1 - LE)))
+        return r
+
+    def repeat(u, l0, l1, q, slot=0):
+        for a, b, s in src_c(u, l0, l1, True):
+            if q == "v":
+                d0 = 16 * a
+                if u % ST == 0:
+                    d0 = 16 * slot
+                    copy("v", X("SP", d0, d0 + 16 * (b - a), 16), s)
+                scan(X("CR", 16 * a, 16 * b), X("HM", 0, 16 * (b - a)), X("SP", d0, d0 + 16 * (b - a)), 0.0, Op.mult, Op.add)
+            elif q == "g":
+                for k in range(16):
+                    copy_g(X("CR", 16 * a + k, 16 * b, 16), s, b - a)
+            else:
+                for k in range(16):
+                    copy("a", X("CR", 16 * a + k, 16 * b, 16), s)
+
+    def gather(u, l0, l1):
+        win = X("Cw", 0, WIN) if u else X("CI", 0, B)
+        tt(X("MG", 16 * l0, 16 * l1), IND(win, X("SU%d" % u, l0, l1)), X("CR", 16 * l0, 16 * l1), Op.min)
+
+    def keys(ch, l0, n, k0=0, k1=16):
+        kp = "KP%d" % ch
+        if k0 == 0:
+            mm(X(kp, 0, 128, p=n), X("ONK", 0, n, p=1), X("KC", 0, 128, p=1), True, False)
+        for k in range(k0, k1):
+            mm(X(kp, k, 128, 16, p=n), X("MG", 16 * l0 + k, 16 * (l0 + n), 16), X("BG", 0, 8), False, k == 15)
+
+    def best(u, ch, l0, n, other):
+        kp, ff, sk, mx, oh = ["%s%d" % (b, ch) for b in ("KP", "FF", "SK", "MX", "OH")]
+        scan(X(ff, 0, 128, p=n), X("RK", 0, 128, p=n), X(kp, 0, 128, p=n), T16, Op.min, Op.max)
+        pop()
+        copy("v", X(sk, 0, 128, 16, p=n), X(ff, 15, 128, 16, p=n))
+        pop()
+        scan(X(mx, 0, 128, p=n), X("HM", 0, 128, p=n), X(sk, 0, 128, p=n), 0.0, Op.mult, Op.add)
+        pop()
+        tt(X(oh, 0, 128, p=n), X(kp, 0, 128, p=n), X(mx, 0, 128, p=n), Op.is_equal)
+        pop(2 if other else 1, other)
+        mm(X("OT", l0, l0 + n), X(oh, 0, 128, p=n), X("IDB", 0, n, p=n), True, True)
+        mm(X("YD", l0, l0 + n), X("DL", 0, 128, p=16), X("DC", 0, n, p=16), True, False)
+        if other:
+            other(7, 9)
+        tt(X("PT", l0, l0 + n), X("SF%d" % u, l0, l0 + n), X("OT", l0, l0 + n), Op.mult)
+        pop(2 if other else 1, other)
+        mm(X("YD", l0, l0 + n), X("BOH", 0, 128), X("PT", l0, l0 + n), False, True)
+        mm(X("YB", l0, l0 + n), X("BOH", 0, 128), X("PT", l0, l0 + n), True, True)
+        if other:
+            other(9, 16)
+        minima(X("WF", l0, l0 + n), X("YD", l0, l0 + n))
+        pop(99)
+        q0 = l0 // 16 + l0 // 16 % 2
+        q1 = q0 + n // 16
+        ts(X("YW", q0, q1), X("WF", l0 + 15, l0 + n, 16), float(B), Op.add)
+        copy("a", X("OS%d" % (u % 2), l0, l0 + n), X("OT", l0, l0 + n))
+        copy("a", X("CY", l0, l0 + n), IND(X("Cw", 0, WIN), X("YW", q0, q1)))
+        copy("a", X("SY", l0, l0 + n), IND(X("Sw", 0, WIN), X("YW", q0, q1)))
+
+    def pairs(q, c0, c1, last):
+        d = 16 * q
+        e = 256 * q - d
+        ts(X("EQ", e + c0, e + c1), X("YB", c0, c1), X("WF", d + 15, d + 16), Op.is_equal)
+        if c0 == d:
+            c0 += 16
+            mm(X("KL", d, c0), X("TSB", 0, 128), X("EQ", e + d, e + c0), False, last and c0 == c1)
+        if c0 < c1:
+            mm(X("KL", c0, c1), X("BOB", 0, 128), X("EQ", e + c0, e + c1), False, last)
+
+    def lane_min(u, l0, n):
+        q0, q1 = l0 // 16, (l0 + n) // 16
+        act(X("WS", q0, q1), X("WF", l0 + 15, l0 + n, 16), Act.Sign)
+        act(X("WX", q0, q1), X("WS", q0, q1), Act.Square)
+        act(X("YP", q0, q1), X("WF", l0 + 15, l0 + n, 16), Act.Identity, bias=float(B))
+        for a, b, s in src_c(u, l0, l0 + n):
+            tt(X("MM", a, b), X("CY", a, b), s, Op.min)
+
+    def new_succ(L, Q):
+        copy("v", IND(X("SQ", 0, SPW), X("OFM", 0, Q)), X("SY", 0, L))
+
+    SQM = X("SQ", 0, 16 * M, 16)
+    for u in range(U):
+        t, e = divmod(u, ST)
+        L = M if e else (LE + LP if t else LE)
+        Q = L // 16
+        last = u == U - 1
+        main = (0, MC if e else 128)
+        aux = (main[1], L - main[1])
+
+        def starts():
+            mm(X("KL", 0, L), X("DL", 0, 128, p=16), X("DC", 0, L, p=16), True, False)
+            mm(X("RR", 0, Q), X("IDH", 0, 128), X("LIH", 0, Q), True, False)
+
+        if u == 0:
+            repeat(u, 48, 128, "a")
+            repeat(u, 128, 208, "v", 0)
+            repeat(u, 0, 48, "v", 80)
+            ts(X("BG", 0, 8), X("BOF", 0, 128, 16), 16.0, Op.mult)
+            copy("v", X("BOH", 0, 128), X("BOF", 0, 128))
+            copy("v", X("IDH", 0, 128), X("IDF", 0, 128))
+            copy("v", X("LIH", 0, 16), X("LIF", 0, 16))
+            copy("v", X("EX", 0, 1), X("SP", 1, 2))
+            copy("v", X("SU0", 0, LE), X("SI", E0, E0 + LE))
+            gather(u, 128, 208)
+            keys(1, *aux)
+            gather(u, 0, 48)
+            gather(u, 48, 128)
+            fillers += [lambda: ts(X("SF0", 0, LE), X("SI", E0, E0 + LE), float(-B), Op.add)]
+            copy("a", X("IDB", 0, 128), X("IDF", 0, 128))
+            copy("a", X("DL", 0, 128, p=16), X("DLF", 0, 128, p=16))
+            copy("a", X("DC", 0, 256, p=16), X("DCF", 0, 256, p=16))
+            copy("a", X("BOB", 0, 128), X("BOF", 0, 128))
+            copy("a", X("TSB", 0, 128), X("TSF", 0, 128))
+            copy("a", X("TIB", 0, 128), X("TIF", 0, 128))
+            zero_a(X("Sw", B, B + 512), X("ON", 0, 512))
+            zero_a(X("Sw", B + 512, WIN), X("ON", 0, WIN - B - 512))
+            starts()
+        else:
+            starts()
+            if e:
+                repeat(u, 0, 80, "a")
+                repeat(u, 80, MC, "g")
+                repeat(u, MC, M, "v")
+                gather(u, MC, M)
+                keys(1, *aux)
+                gather(u, 0, 80)
+                gather(u, 80, MC)
+            else:
+                repeat(u, 48, 128, "a")
+                repeat(u, LE, LE + LP, "a")
+                repeat(u, 176, LE, "g")
+                repeat(u, 0, 48, "v", 0)
+                gather(u, 0, 48)
+                repeat(u, 128, 176, "v", 48)
+                gather(u, 48, 128)
+                keys(0, *main)
+                gather(u, 128, LE)
+                gather(u, LE, LE + LP)
+                new_succ(M, M // 16)
+            copy("a", X("Sw", N0 + M * (u - 1), N0 + M * u), SQM)
+            fillers += s_update(u - 1)
+            if e:
+                fillers.insert(1, lambda u=u: ts(X("SF%d" % u, 0, M), SQM, float(-B), Op.add))
+        zero_a(X("SP", 0, 16 * M, 16), X("SP", 0, 16 * M, 16))
+        if u == 1:
+            fillers += [lambda: copy("v", X("SU3", 0, LE), X("Sw", E0 + LE, E0 + 2 * LE)),
+                        lambda: copy("v", X("SU3", LE, LE + LP), X("Sw", B - LP, B))]
+        if u == 2:
+            fillers += [lambda: ts(X("SF3", 0, LE), X("Sw", E0 + LE, E0 + 2 * LE), float(-B), Op.add),
+                        lambda: ts(X("SF3", LE, LE + LP), X("Sw", B - LP, B), float(-B), Op.add)]
+            spare += ys_conv(E0, E0 + LE)
+        if u == 3:
+            spare += ys_conv(N0, N0 + M)
+        if u == 4:
+            spare += ys_conv(N0 + M, N0 + 2 * M) + ys_conv(E0 + LE, B)
+        if u == 5:
+            spare += ys_conv(N0 + 2 * M, N0 + 3 * M) + ys_conv(N0 + 3 * M, N0 + 4 * M)
+        (c1, k1), (c2, k2) = ((main, 0), (aux, 1)) if u == ST else ((aux, 1), (main, 0))
+        if u == ST:
+            pop(2)
+        keys(k2, c2[0], c2[1], 0, 7)
+        best(u, k1, c1[0], c1[1], lambda a, b: keys(k2, c2[0], c2[1], a, b))
+        if u:
+            zero_a(SQM, SQM)
+        for q in range(c1[0] // 16, (c1[0] + c1[1]) // 16):
+            pairs(q, 16 * q, c1[0] + c1[1], False)
+        lane_min(u, *c1)
+        while spare:
+            spare.pop(0)()
+        best(u, k2, c2[0], c2[1], None)
+        if u == ST:
+            for q in range(8):
+                pairs(q, 128, L, False)
+            for q in range(8, Q):
+                pairs(q, 16 * q, L, q == Q - 1)
+        else:
+            for q in range(c2[1] // 16):
+                pairs(q, 16 * q, L, q == c2[1] // 16 - 1)
+        lane_min(u, *c2)
+        minima(X("FK", 0, L), X("KL", 0, L))
+        fk = X("FK", 15, L, 16)
+        tt(X("AW", 0, Q), fk, X("WX", 0, Q), Op.is_lt)
+        mm(X("RR", 0, Q), X("TIB", 0, 128), X("AW", 0, Q), False, False)
+        if e:
+            tt(X("CN", 0, Q), fk, X("WX", 0, Q), Op.is_ge)
+        scan(X("EX", 1, Q + 1), X("ON16", 0, Q), X("AW", 0, Q), 0.0, Op.mult, Op.add)
+        if e:
+            tt(X("TN", 0, Q), X("CN", 0, Q), X("D2", 0, Q), Op.mult)
+        tt(X("AL", 0, Q), X("AW", 0, Q), X("NLI", 0, Q), Op.mult)
+        mm(X("RR", 0, Q), X("BOB", 0, 128), X("EX", 0, Q), False, False)
+        mm(X("RR", 0, Q), X("IDH", 0, 128), X("AL", 0, Q), False, True)
+
+        places = [lambda: tt(X("TN", 0, Q), X("CN", 0, Q), X("D2", 0, Q), Op.mult),
+                  lambda: tt(X("TO", 0, Q), X("TN", 0, Q), X("YP", 0, Q), Op.max),
+                  lambda: copy("v", X("OFY", 0, Q), X("TO", 0, Q))]
+
+        def p1():
+            tt(X("P1", 0, Q), X("AW" if e else "LV", 0, Q), X("RR", 0, Q), Op.mult)
+
+        def p2():
+            if e:
+                act(X("P2", 0, Q), X("AW", 0, Q), Act.Copy, scale=float(B + M * u))
+            else:
+                ts(X("P2", 0, Q), X("LV", 0, Q), float(B + M * u), Op.mult)
+
+        def sub():
+            tt(IND(X("Cw", 0, CW), X("OFY", 0, Q)), X("CY", 0, L), X("MM", 0, L), Op.subtract)
+
+        def send():
+            nxt = T.cores[(rank + 1) % len(T.cores)]
+            rid, pid, _ = topo.addr(nxt)
+            en = topo.engines(core, nxt)[0:4]
+            src, dst = X("PS", 0, LP), X("PORT", 0, LP)
+            emit("g", lambda: g.remote_dma(dst[4], src[4], T.sem["arr"], T.sem["left"], pid, rid, sum(1 << x for x in en)),
+                 [dst], [src], sem="arr", n=len(en))
+
+        def place_m():
+            ts(X("OFM", 0, Q), X("RR", 0, Q), 16.0, Op.mult, -16.0, Op.add)
+            if not e:
+                ts(X("CN", 0, Q), X("RR", 0, Q), M + 0.5, Op.is_gt)
+            copy("v", IND(X("SP", 0, SPW), X("OFM", 0, Q)), X("MM", 0, L))
+            if u == ST - 1:
+                copy("a", X("PS", 0, LP), X("SP", 0, 16 * LP, 16))
+                send()
+            copy("a", X("Cw", N0 + M * u, N0 + M * (u + 1)), X("SP", 0, 16 * M, 16))
+
+        if not e:
+            place_m()
+            places[0]()
+            new_succ(L, Q)
+            places[1]()
+            ts(X("LV", 0, Q), X("RR", 0, Q), M + 0.5, Op.is_lt)
+            places[2]()
+            p1()
+            copy("v", X("SU%d" % (u + 1), 0, M), SQM)
+            p2()
+            sub()
+        else:
+            places[1]()
+            places[2]()
+            if e == ST - 1:
+                sub()
+            if last:
+                dma("y", D("yc", 0, 720), X("Cw", 0, 720))
+                dma("a", D("yc", 720, 1440), X("Cw", 720, 1440))
+                dma("y", D("yc", 1440, B), X("Cw", 1440, B))
+                dma("a", D("yc", B, WIN - 1 - M), X("Cw", N0, WIN - M))
+                p1()
+                p2()
+                place_m()
+                dma("y", D("yc", WIN - 1 - M, WIN - 1), X("Cw", WIN - M, WIN))
+                new_succ(L, Q)
+            elif e == ST - 1:
+                place_m()
+                p1()
+                p2()
+            else:
+                place_m()
+                new_succ(L, Q)
+                p1()
+                copy("v", X("SU%d" % (u + 1), 0, M), SQM)
+                p2()
+                sub()
+        for i in range(16):
+            mm(X("NB", i, L, 16), X("BS", 128 * i, 128 * i + 128), X("P1", 0, Q), True, False)
+            mm(X("NB", i, L, 16), X("BS", 128 * i, 128 * i + 128), X("P2", 0, Q), False, True)
+    fillers += s_update(U - 1)
+    for f in ys_conv(N0 + 5 * M, WIN, SQM):
+        f()
+    pop(99)
+    for f in ys_conv(N0 + 4 * M, N0 + 5 * M):
+        f()
+    g.wait_ge(T.sem["left"], inc["arr"])
+    for q in cnt:
+        g.wait_ge(T.sem[semname(q)], cnt[q] * inc[q])

@@ -3,58 +3,32 @@ from concourse.mybir import dt, AluOpType, AxisListType, ActivationFunctionType
 B, LE, LP, M, ST, RO, TH = 1920, 208, 48, 144, 3, 2, 49152
 U = RO * ST
 E0 = B - RO * LE - LP
-N0 = B + 1
-WIN = N0 + U * M
-DUMP = WIN
-CW = 3168
+W = B + U * M
+DUMP = W + 8
+CW = DUMP + 256
 T16 = float(16 * TH)
 BIG = 33554432.0
-FAR = 4000.0
-SPW = 14080
-MC = 112
+LOW = 2097152.0
+RG = 264
+NA = {0: 96, 1: 112, 2: 112, 3: 128, 4: 112, 5: 112}
 
-SCRATCH = {
-    "CI": ("sbuf", [128, B], "int32"), "SI": ("sbuf", [128, B], "int32"),
-    "Cw": ("sbuf", [128, CW], "float32"), "Sw": ("sbuf", [128, 2800], "float32"),
-    "SP": ("sbuf", [128, SPW], "float32"), "SQ": ("sbuf", [128, SPW], "float32"), "HM": ("sbuf", [128, 1280], "bfloat16"),
-    "CR": ("sbuf", [128, 4096], "float32"), "MG": ("sbuf", [128, 4096], "float32"),
-    "RB": ("sbuf", [128, 256], "float32"), "RK": ("sbuf", [128, 128], "float32"),
-    "PT": ("sbuf", [128, 256], "float16"), "WF": ("sbuf", [128, 256], "float32"),
-    "YW": ("sbuf", [128, 18], "uint16"), "YP": ("sbuf", [128, 16], "float32"),
-    "WS": ("sbuf", [128, 16], "float32"), "WX": ("sbuf", [128, 16], "float32"),
-    "EQ": ("sbuf", [128, 4096], "bfloat16"),
-    "CY": ("sbuf", [128, 256], "float32"), "SY": ("sbuf", [128, 256], "float32"), "MM": ("sbuf", [128, 256], "float32"),
-    "FK": ("sbuf", [128, 256], "float32"), "AW": ("sbuf", [128, 16], "bfloat16"), "EX": ("sbuf", [128, 24], "bfloat16"),
-    "AL": ("sbuf", [128, 16], "float16"), "CN": ("sbuf", [128, 16], "float32"), "TN": ("sbuf", [128, 16], "float32"),
-    "TO": ("sbuf", [128, 16], "float32"), "OFM": ("sbuf", [128, 16], "uint16"),
-    "OFY": ("sbuf", [128, 16], "uint16"), "LV": ("sbuf", [128, 16], "bfloat16"),
-    "P1": ("sbuf", [128, 16], "bfloat16"), "P2": ("sbuf", [128, 16], "bfloat16"),
-    "T1": ("sbuf", [128, 256], "float32"), "T2": ("sbuf", [128, 1328], "float32"), "YS": ("sbuf", [128, 1328], "float32"),
-    "PORT": ("sbuf", [128, LP], "float32"), "PS": ("sbuf", [128, LP], "float32"),
-    "ON": ("sbuf", [128, 512], "float32"), "FR": ("sbuf", [128, 256], "float32"), "ONB": ("sbuf", [128, 2048], "bfloat16"),
-    "ONK": ("sbuf", [128, 128], "bfloat16"), "KC": ("sbuf", [128, 128], "bfloat16"),
-    "IDF": ("sbuf", [128, 128], "float32"), "IDB": ("sbuf", [128, 128], "bfloat16"), "IDH": ("sbuf", [128, 128], "float16"),
-    "BOX": ("sbuf", [128, 128], "float32"), "BOF": ("sbuf", [128, 128], "float32"), "BOB": ("sbuf", [128, 128], "bfloat16"),
-    "BOH": ("sbuf", [128, 128], "float16"), "BG": ("sbuf", [128, 8], "float32"),
-    "TSF": ("sbuf", [128, 128], "float32"), "TSB": ("sbuf", [128, 128], "bfloat16"),
-    "TIF": ("sbuf", [128, 128], "float32"), "TIB": ("sbuf", [128, 128], "bfloat16"),
-    "DL": ("sbuf", [128, 128], "bfloat16"), "DC": ("sbuf", [128, 256], "bfloat16"),
-    "DLF": ("sbuf", [128, 128], "float32"), "DCF": ("sbuf", [128, 256], "float32"),
-    "LIF": ("sbuf", [128, 16], "float32"), "LIH": ("sbuf", [128, 16], "float16"), "NLI": ("sbuf", [128, 16], "float32"),
-    "D2": ("sbuf", [128, 16], "float32"), "ON16": ("sbuf", [128, 16], "float32"), "BS": ("sbuf", [128, 2048], "bfloat16"),
-    "KP0": ("psum", [128, 512], "float32"), "KP1": ("psum", [128, 512], "float32"), "OT": ("psum", [128, 512], "float32"),
-    "YB": ("psum", [128, 512], "float32"), "YD": ("psum", [128, 512], "float32"), "KL": ("psum", [128, 512], "float32"),
-    "RR": ("psum", [128, 512], "float32"), "NB": ("psum", [128, 512], "float32"),
-}
-for _i in range(2):
-    SCRATCH["FF%d" % _i] = ("sbuf", [128, 128], "float32")
-    SCRATCH["SK%d" % _i] = ("sbuf", [128, 128], "float32")
-    SCRATCH["MX%d" % _i] = ("sbuf", [128, 128], "float32")
-    SCRATCH["OH%d" % _i] = ("sbuf", [128, 128], "bfloat16")
-    SCRATCH["OS%d" % _i] = ("sbuf", [128, 256], "float32")
-for _i in range(U):
-    SCRATCH["SU%d" % _i] = ("sbuf", [128, 256], "uint16")
-    SCRATCH["SF%d" % _i] = ("sbuf", [128, 256], "float16")
+f32, b16, f16, u16, i32 = "float32", "bfloat16", "float16", "uint16", "int32"
+SCRATCH = {n: ("sbuf", [128, c], d) for n, c, d in [
+    ("CI", B + 8, i32), ("SI", B + 8, i32), ("Cw", CW, f32), ("Sw", W + 8, f32), ("CR", 1024, f32), ("MG", 4096, f32),
+    ("SF", 256 * U, f16), ("SU", 256 * U, u16), ("MM", RG * U, f32), ("SY", RG * U, f32), ("INV", 16 * U, u16),
+    ("FF0", 128, f32), ("FF1", 128, f32), ("MX0", 128, f32), ("MX1", 128, f32), ("OH0", 128, b16), ("OH1", 128, b16),
+    ("OS", 256, b16), ("PT", 256, f16), ("WF", 256, f32), ("YW", 18, u16), ("EQ", 4096, b16), ("CY", 256, f32),
+    ("FK", 256, f32), ("OFY", 16, u16), ("SG", 256, b16), ("RS", 256, f32), ("RW", 256, f32), ("TO", 16, f32),
+    ("ACC", 16, f32), ("JK", 2304, b16), ("IV", 16, f32), ("RKB", 256, b16), ("OV", 256, b16),
+    ("PORT", LP, f32), ("PS", LP, f32),
+    ("ON", 512, f32), ("RK", 128, f32), ("RB", 256, f32), ("RM", 256, f32), ("DG", 256, f32), ("LM", 256, f32), ("LR", 256, f32),
+    ("BOX", 128, f32), ("BOF", 128, f32), ("TSF", 128, f32), ("IDW", 160, f32), ("WS", 640, f16),
+    ("PI", 2, i32), ("PR", 2, i32), ("PF", 2, f32), ("I4", 4, f32), ("MK4", 4, f32), ("Q16", 16, f32), ("JB", 16, f32),
+    ("BG", 8, f32), ("BOH", 128, f16), ("IDB", 128, b16), ("IP", 128, b16), ("IN", 128, b16), ("BN", 128, b16),
+    ("BP", 128, b16), ("BH", 128, b16), ("BD", 128, b16), ("TP", 128, b16), ("MY", 256, b16), ("MK", 256, b16),
+    ("KC", 128, b16), ("ONK", 256, b16), ("C14", 128, b16), ("RH", 256, b16), ("RA", 256, b16), ("CZ", 128 * U, b16)]}
+for _n in ("KP0", "KP1", "OT", "O2", "YD", "YB", "KL", "SH"):
+    SCRATCH[_n] = ("psum", [128, 512], f32)
 NDMA = 24
 SEMAPHORES = ["qv", "qt", "qa", "qg", "arr", "left"] + ["d%d" % i for i in range(NDMA)]
 
@@ -71,6 +45,9 @@ def rank_program(g, core, T, topo):
     def X(name, c0, c1, step=1, p=128):
         ap = T[name][0:p, c0:c1] if step == 1 else T[name][0:p, c0:c1:step]
         return (name, c0, c1, step, ap, None)
+
+    def REV(name, p):
+        return (name, 0, 128, 1, T[name][0:p, ::-1], None)
 
     def IND(x, off):
         return (x[0], x[1], x[2], 1, x[4].indirect(off[4]), off)
@@ -114,8 +91,17 @@ def rank_program(g, core, T, topo):
         if sem != "arr":
             inst.then_inc(T.sem[semname(me)], n)
 
-    def act(out, in_, func, **kw):
-        emit("a", lambda: g.scalar.activation(out[4], in_[4], func, **kw), [out], [in_])
+    def act(out, in_, func, bias=None, scale=None, acc=None):
+        kw, ins, outs = {}, [in_], [out]
+        if bias is not None:
+            kw["bias"] = bias[4] if isinstance(bias, tuple) else bias
+            ins += [bias] if isinstance(bias, tuple) else []
+        if scale is not None:
+            kw["scale"] = scale
+        if acc is not None:
+            kw["accum_out"] = acc[4]
+            outs.append(acc)
+        emit("a", lambda: g.scalar.activation(out[4], in_[4], func, **kw), outs, ins)
 
     def copy(q, out, in_):
         if q == "v":
@@ -138,14 +124,11 @@ def rank_program(g, core, T, topo):
     def scan(out, d0, d1, init, op0, op1):
         emit("v", lambda: g.vector.tensor_tensor_scan(out[4], d0[4], d1[4], init, op0, op1), [out], [d0, d1])
 
-    def minima(out, d):
-        scan(out, X("RB", 0, out[2] - out[1]), d, 0.0, Op.max, Op.min)
-
     def fill(out, c):
         emit("v", lambda: g.vector.memset(out[4], c), [out], [])
 
-    def zero_a(out, like):
-        act(out, like, Act.Copy, scale=0.0)
+    def zero_a(out):
+        act(out, X("ON", 0, out[2] - out[1]), Act.Copy, scale=0.0)
 
     def mm(out, lhsT, rhs, start, stop):
         emit("t", lambda: g.tensor.matmul(out[4], lhsT[4], rhs[4], start, stop), [out], [lhsT, rhs])
@@ -156,8 +139,11 @@ def rank_program(g, core, T, topo):
     def copy_g(out, in_, n):
         aff(out, in_, [[0, n]], Op.is_gt, 0.0, 1, 0)
 
-    def iota(out, pattern, base, cm):
-        emit("g", lambda: g.iota(out[4], pattern, base, cm, allow_small_or_imprecise_dtypes=True), [out], [])
+    def iota(out, pattern, base, cm, whole=False):
+        if whole:
+            emit("g", lambda: g.iota(out[4], pattern, base, cm), [out], [])
+        else:
+            emit("g", lambda: g.iota(out[4], pattern, base, cm, allow_small_or_imprecise_dtypes=True), [out], [])
 
     ndma = [0]
 
@@ -169,365 +155,370 @@ def rank_program(g, core, T, topo):
     def D(name, c0, c1):
         return (name, c0, c1, 1, T[name][:, c0:c1], None)
 
-    dma("a", X("CI", E0, B), D("c0", E0, B))
+    def mat(name):
+        return X(name, 0, 128)
+
+    def lanes(u):
+        return M if u % ST else (LE + LP if u else LE)
+
+    def reg(name, u, l0=0, l1=None):
+        a = RG * u + 256 - lanes(u)
+        return X(name, a + l0, a + (lanes(u) if l1 is None else l1))
+
+    def regw(name, u):
+        return reg(name, u, 0, lanes(u) + 1)
+
+    def sf(u, l0=0, l1=None, step=1):
+        return X("SF", 256 * u + l0, 256 * u + (lanes(u) if l1 is None else l1), step)
+
+    def new(name, u):
+        return X(name, B + M * u, B + M * (u + 1))
+
+    def ys_out(c0, c1, q="y"):
+        dma(q, D("ys", c0 - E0, c1 - E0), X("Sw", c0, c1))
+
     dma("y", X("SI", E0, B), D("s0", E0, B))
-    dma("a", X("CI", 736, E0), D("c0", 736, E0))
+    dma("a", X("CI", E0, B), D("c0", E0, B))
     dma("y", X("CI", 0, 736), D("c0", 0, 736))
+    dma("a", X("CI", 736, E0), D("c0", 736, E0))
     dma("y", X("SI", 0, E0), D("s0", 0, E0))
 
     fill(X("ON", 0, 512), 1.0)
-    fill(X("HM", 0, 1280), 1.0)
-    fill(X("HM", 0, 1280, 16), 0.0)
-    fill(X("RK", 0, 128), BIG)
-    fill(X("RK", 0, 128, 16), T16)
-    fill(X("RB", 0, 256), -BIG)
-    fill(X("RB", 0, 256, 16), BIG)
-    fill(X("SK1", 0, 128), 0.0)
-    fill(X("SK0", 0, 128), 0.0)
-    fill(X("ON16", 0, 16), 1.0)
-    aff(X("BOX", 0, 128), X("ON", 0, 128), [[-16, 8], [0, 16]], Op.is_ge, 0.0, 0, 1)
-    aff(X("BOF", 0, 128), X("BOX", 0, 128), [[16, 8], [0, 16]], Op.is_ge, 0.0, 15, -1)
+    iota(X("PI", 0, 1), [[0, 1]], 0, 1, True)
+    iota(X("I4", 0, 4), [[1, 4]], 0, 0)
+    aff(X("IDW", 0, 160), X("ON", 0, 160), [[-1, 160]], Op.is_equal, 0.0, 12, 1)
+    aff(mat("BOX"), mat("ON"), [[-16, 8], [0, 16]], Op.is_ge, 0.0, 0, 1)
+    aff(mat("BOF"), mat("BOX"), [[16, 8], [0, 16]], Op.is_ge, 0.0, 15, -1)
     iota(X("KC", 0, 128, p=1), [[0, 8], [-1, 16]], 15, 0)
-    iota(X("ONK", 0, 128, p=1), [[0, 128]], 1, 0)
-    iota(X("FR", 0, 256, p=16), [[0, 256]], int(FAR), 0)
-    aff(X("IDF", 0, 128), X("ON", 0, 128), [[-1, 128]], Op.is_equal, 0.0, 0, 1)
-    aff(X("DLF", 0, 128, p=16), X("ON", 0, 128, p=16), [[0, 8], [1, 16]], Op.is_equal, 0.0, 0, -1)
-    aff(X("DCF", 0, 256, p=16), X("FR", 0, 256, p=16), [[0, 16], [1, 16]], Op.not_equal, 0.0, 0, -1)
-    aff(X("TSF", 0, 128), X("BOF", 0, 128), [[1, 128]], Op.is_gt, 0.0, 0, -1)
-    aff(X("TIF", 0, 128), X("BOF", 0, 128), [[1, 128]], Op.is_ge, 0.0, 0, -1)
-    iota(X("LIF", 0, 16), [[16, 16]], 256, 1)
-    iota(X("NLI", 0, 16), [[-16, 16]], -256, -1)
-    iota(X("D2", 0, 16), [[16, 16]], DUMP, 1)
-    copy_g(X("Cw", 0, E0), X("CI", 0, E0), E0)
+    iota(X("LM", 0, 256), [[0, 16], [1, 16]], 0, 0)
+    iota(X("Q16", 0, 16), [[16, 16]], 0, 0)
+    iota(X("LR", 0, 256), [[1, 256]], DUMP - B + int(LOW), 0)
+    aff(mat("TSF"), mat("BOF"), [[1, 128]], Op.is_gt, 0.0, 0, -1)
+    for u in range(U):
+        c = B - 1 + M * u - 8192 + 14 * 4096
+        iota(X("CZ", 128 * u, 128 * u + 128, p=2), [[0, 128]], c - c % 256, c % 256 - (c - c % 256))
+    fill(mat("RK"), BIG)
+    fill(X("RB", 0, 256), -LOW)
+    fill(X("ONK", 0, 256, p=2), 1.0)
+    fill(X("RK", 0, 128, 16), T16)
+    fill(X("C14", 0, 128, p=1), 14.0 * 16777216.0)
+    fill(X("RH", 0, 256, p=1), float(W - B))
+    fill(X("RA", 0, 256, p=1), 65536.0)
+    fill(X("MM", 256, RG * U, RG), 0.0)
+    fill(X("SY", 256, RG * U, RG), 0.0)
+    fill(X("CI", B, B + 8), 0)
+    fill(X("SI", B, B + 8), 0)
+    ts(X("PR", 0, 1), X("PI", 0, 1), 15, Op.bitwise_and)
+    ts(X("PR", 1, 2), X("PR", 0, 1), 2, Op.arith_shift_right)
+    copy("v", X("PF", 0, 2), X("PR", 0, 2))
+    ts(X("MK4", 0, 4), X("I4", 0, 4), X("PF", 1, 2), Op.is_equal)
+    for kq in range(4):
+        ts(X("WS", 160 * kq, 160 * kq + 160), X("IDW", 0, 160), X("MK4", kq, kq + 1), Op.mult)
+    zero_a(X("Cw", B, B + 512))
+    zero_a(X("Cw", B + 512, W + 8))
+    zero_a(X("Sw", B, B + 512))
+    zero_a(X("Sw", B + 512, W + 8))
+    idf = X("IDW", 12, 140)
+    for name, src, s in (("IDB", idf, 1.0), ("BH", mat("BOF"), float(B - W)), ("BN", mat("BOF"), -4096.0),
+                         ("BP", mat("BOF"), 4096.0), ("TP", mat("TSF"), 4096.0), ("IP", idf, 8192.0),
+                         ("IN", idf, -8192.0), ("BD", mat("BOF"), -16777216.0)):
+        act(mat(name), src, Act.Copy, scale=s)
+
+    def shuffle(u):
+        n = lanes(u) // 4
+        for kq in range(4):
+            for h in range(4):
+                s = 160 * kq + 12 + 4 * (kq - h)
+                mm(X("SH", n * kq, n * kq + n), X("WS", s, s + 128), sf(u, h, None, 4), h == 0, h == 3)
+
+    def lists(u):
+        ts(X("SU", 256 * u, 256 * u + lanes(u)), X("SH", 0, lanes(u)), float(B), Op.add)
+
+    def repeat(q, src, l0, ks=range(4)):
+        for k in ks:
+            copy(q, X("CR", 4 * l0 + k, 4 * (l0 + src[2] - src[1]), 4), src)
+
+    ts(sf(0), X("SI", E0, E0 + LE), float(-B), Op.add)
+    shuffle(0)
+    ts(X("BG", 0, 8), X("BOF", 0, 128, 16), 16.0, Op.mult)
+    repeat("v", X("CI", E0, E0 + LE), 0)
+    lists(0)
+    ts(sf(ST), X("SI", E0 + LE, B), float(-B), Op.add)
+    shuffle(ST)
+    copy("v", mat("BOH"), mat("BOF"))
+    ts(X("DG", 0, 256), X("LM", 0, 256), X("PF", 0, 1), Op.is_equal)
+    ts(X("JB", 0, 16), X("Q16", 0, 16), X("PF", 0, 1), Op.add)
+    tt(X("RW", 0, 256), X("DG", 0, 256), X("LR", 0, 256), Op.mult)
+    ts(X("RB", 0, 256, 16), X("JB", 0, 16), float(DUMP - B), Op.add)
+    ts(X("JB", 0, 16), X("JB", 0, 16), -1.0, Op.mult, float(M), Op.add)
+    ts(X("RM", 0, 256), X("RW", 0, 256), -LOW, Op.add)
+    lists(ST)
+    act(X("MY", 0, 256), X("DG", 0, 256), Act.Identity, bias=4096.0 + W - B, scale=-4096.0)
+    act(X("MK", 0, 256), X("DG", 0, 256), Act.Identity, bias=8192.0, scale=-4096.0)
+    copy_g(X("Cw", 0, B), X("CI", 0, B), B)
     copy_g(X("Sw", E0, B), X("SI", E0, B), B - E0)
     copy_g(X("Sw", 0, E0), X("SI", 0, E0), E0)
-    iota(X("SQ", 0, 16 * M, 16), [[0, M]], 0, 0)
-    iota(X("ONB", 0, 2048), [[0, 2048]], 1, 0)
-    aff(X("BS", 0, 2048), X("ONB", 0, 2048), [[1, 16], [16, 8], [0, 16]], Op.is_equal, 0.0, 0, -1)
-    for a in range(0, 16 * M, 512):
-        zero_a(X("SP", a, min(a + 512, 16 * M)), X("ON", 0, min(512, 16 * M - a)))
-    zero_a(X("Cw", B, B + 512), X("ON", 0, 512))
-    zero_a(X("Cw", B + 512, WIN), X("ON", 0, WIN - B - 512))
-
-    copy("v", X("Cw", E0, B), X("CI", E0, B))
 
     fillers = []
-    spare = []
 
-    def pop(n=1, more=False):
+    def pop(n=1):
         for _ in range(n):
             if fillers:
                 fillers.pop(0)()
-            elif more and spare:
-                spare.pop(0)()
 
-    def ys_conv(c0, c1, src=None):
-        o = c0 - E0 if c1 <= B else c0 - 1 - E0
-        n = c1 - c0
-        s = src if src is not None else X("Sw", c0, c1)
+    def opens(u, chunks):
+        L = lanes(u)
+        for ch, (l0, n) in enumerate(chunks):
+            kp = X("KP%d" % ch, 0, 128, p=n)
+            if u % ST == 2:
+                mm(kp, X("ONK", 0, n, p=1), X("C14", 0, 128, p=1), True, False)
+                mm(kp, X("SG", l0, l0 + n), mat("BD"), False, False)
+            mm(kp, X("ONK", 0, n, p=1), X("KC", 0, 128, p=1), u % ST != 2, False)
+        a = chunks[1][0]
+        mm(X("YD", a, L), mat("IDB"), X("MY", a, L), True, False)
+        mm(X("YB", a, L), X("ONK", 0, 128, p=1), X("RH", 0, L - a, p=1), True, False)
+        mm(X("SH", 256 + a, 256 + L), X("ONK", 0, 128, p=1), X("RH", 0, L - a, p=1), True, False)
+        mm(X("KL", 0, L), mat("IDB"), X("MK", 0, L), True, False)
 
-        def second():
-            tt(X("YS", o, o + n), s, X("T2", o, o + n), Op.subtract)
-            dma("y", D("ys", o, o + n), X("YS", o, o + n))
-        return [lambda: ts(X("T2", o, o + n), s, float(B) + 0.5, Op.is_gt), second]
+    def gather(u, kq, l0, l1):
+        L = lanes(u)
+        win = X("CI", 0, B) if u == 0 else X("Cw", 0, B + M * (u - 1) if u != ST else B)
+        o = 256 * u + L // 4 * kq
+        tt(X("MG", 1024 * kq + 4 * l0, 1024 * kq + 4 * l1), IND(win, X("SU", o + l0 // 4, o + l1 // 4)),
+           X("CR", 4 * l0, 4 * l1), Op.min)
 
-    def xcols(u):
-        t, e = divmod(u, ST)
-        if e:
-            return [(0, M, N0 + M * (u - 1))]
-        r = [(0, LE, E0 + LE * t)]
-        return r + [(LE, LP, B - LP)] if t else r
+    def keys(ch, l0, n, kq):
+        for i in range(4):
+            a = 1024 * kq + 4 * l0
+            mm(X("KP%d" % ch, 4 * kq + i, 128, 16, p=n), X("MG", a + i, a + 4 * n, 4), X("BG", 0, 8), False, 4 * kq + i == 15)
 
-    def s_update(u):
-        L = sum(n for _, n, _ in xcols(u))
-        r = [lambda: tt(X("T1", 0, L), X("OS%d" % (u % 2), 0, L), X("NB", 0, L), Op.mult)]
-        for l0, n, c in xcols(u):
-            r.append(lambda l0=l0, n=n, c=c: tt(X("Sw", c, c + n), X("Sw", c, c + n), X("T1", l0, l0 + n), Op.max))
-        return r
-
-    def src_c(u, l0, l1, rep=False):
-        t, e = divmod(u, ST)
-        if e:
-            if rep:
-                return [(l0, l1, X("SP", 16 * l0, 16 * l1, 16))]
-            return [(l0, l1, X("Cw", N0 + M * (u - 1) + l0, N0 + M * (u - 1) + l1))]
-        r = []
-        if l0 < LE:
-            a = min(l1, LE)
-            r.append((l0, a, X("Cw", E0 + LE * t + l0, E0 + LE * t + a)))
-        if l1 > LE:
-            a = max(l0, LE)
-            r.append((a, l1, X("PORT", a - LE, l1 - LE)))
-        return r
-
-    def repeat(u, l0, l1, q, slot=0):
-        for a, b, s in src_c(u, l0, l1, True):
-            if q == "v":
-                d0 = 16 * a
-                if u % ST == 0:
-                    d0 = 16 * slot
-                    copy("v", X("SP", d0, d0 + 16 * (b - a), 16), s)
-                scan(X("CR", 16 * a, 16 * b), X("HM", 0, 16 * (b - a)), X("SP", d0, d0 + 16 * (b - a)), 0.0, Op.mult, Op.add)
-            elif q == "g":
-                for k in range(16):
-                    copy_g(X("CR", 16 * a + k, 16 * b, 16), s, b - a)
-            else:
-                for k in range(16):
-                    copy("a", X("CR", 16 * a + k, 16 * b, 16), s)
-
-    def gather(u, l0, l1):
-        win = X("Cw", 0, WIN) if u else X("CI", 0, B)
-        tt(X("MG", 16 * l0, 16 * l1), IND(win, X("SU%d" % u, l0, l1)), X("CR", 16 * l0, 16 * l1), Op.min)
-
-    def keys(ch, l0, n, k0=0, k1=16):
-        kp = "KP%d" % ch
-        if k0 == 0:
-            mm(X(kp, 0, 128, p=n), X("ONK", 0, n, p=1), X("KC", 0, 128, p=1), True, False)
-        for k in range(k0, k1):
-            mm(X(kp, k, 128, 16, p=n), X("MG", 16 * l0 + k, 16 * (l0 + n), 16), X("BG", 0, 8), False, k == 15)
-
-    def best(u, ch, l0, n, other):
-        kp, ff, sk, mx, oh = ["%s%d" % (b, ch) for b in ("KP", "FF", "SK", "MX", "OH")]
+    def best(u, ch, l0, n, final):
+        kp, ff, mx, oh = ["%s%d" % (b, ch) for b in ("KP", "FF", "MX", "OH")]
+        l1 = l0 + n
         scan(X(ff, 0, 128, p=n), X("RK", 0, 128, p=n), X(kp, 0, 128, p=n), T16, Op.min, Op.max)
-        pop()
-        copy("v", X(sk, 0, 128, 16, p=n), X(ff, 15, 128, 16, p=n))
-        pop()
-        scan(X(mx, 0, 128, p=n), X("HM", 0, 128, p=n), X(sk, 0, 128, p=n), 0.0, Op.mult, Op.add)
-        pop()
+        yield
+        scan(REV(mx, n), X("RK", 0, 128, p=n), REV(ff, n), T16, Op.min, Op.max)
+        yield
         tt(X(oh, 0, 128, p=n), X(kp, 0, 128, p=n), X(mx, 0, 128, p=n), Op.is_equal)
-        pop(2 if other else 1, other)
-        mm(X("OT", l0, l0 + n), X(oh, 0, 128, p=n), X("IDB", 0, n, p=n), True, True)
-        mm(X("YD", l0, l0 + n), X("DL", 0, 128, p=16), X("DC", 0, n, p=16), True, False)
-        if other:
-            other(7, 9)
-        tt(X("PT", l0, l0 + n), X("SF%d" % u, l0, l0 + n), X("OT", l0, l0 + n), Op.mult)
-        pop(2 if other else 1, other)
-        mm(X("YD", l0, l0 + n), X("BOH", 0, 128), X("PT", l0, l0 + n), False, True)
-        mm(X("YB", l0, l0 + n), X("BOH", 0, 128), X("PT", l0, l0 + n), True, True)
-        if other:
-            other(9, 16)
-        minima(X("WF", l0, l0 + n), X("YD", l0, l0 + n))
-        pop(99)
+        mm(X("OT", l0, l1), X(oh, 0, 128, p=n), X("IDB", 0, n, p=n), True, True)
+        mm(X("O2", l0, l1), X(oh, 0, 128, p=n), X("IDB", 0, n, p=n), True, True)
+        copy("a", X("OS", l0, l1), X("O2", l0, l1))
+        yield
+        tt(X("PT", l0, l1), sf(u, l0, l1), X("OT", l0, l1), Op.mult)
+        if final:
+            mm(X("YD", l0, l1), mat("IDB"), X("MY", l0, l1), True, False)
+            mm(X("YB", l0, l1), X("ONK", 0, 128, p=1), X("RH", 0, n, p=1), True, False)
+        for b, o, m in [("YD", 0, "BH")] + [("SH", 256, "BH")] * (not final) + [("YB", 0, "BH"), ("KL", 0, "BN")]:
+            mm(X(b, o + l0, o + l1), mat(m), X("OS", l0, l1), False, False)
+            mm(X(b, o + l0, o + l1), mat("BOH"), X("PT", l0, l1), False, b != "KL")
+        yield
+        scan(X("WF", l0, l1), X("RB", l0, l1), X("YD", l0, l1), 0.0, Op.max, Op.min)
+        yield
         q0 = l0 // 16 + l0 // 16 % 2
-        q1 = q0 + n // 16
-        ts(X("YW", q0, q1), X("WF", l0 + 15, l0 + n, 16), float(B), Op.add)
-        copy("a", X("OS%d" % (u % 2), l0, l0 + n), X("OT", l0, l0 + n))
-        copy("a", X("CY", l0, l0 + n), IND(X("Cw", 0, WIN), X("YW", q0, q1)))
-        copy("a", X("SY", l0, l0 + n), IND(X("Sw", 0, WIN), X("YW", q0, q1)))
+        yw = X("YW", q0, q0 + n // 16)
+        if u == 0:
+            ts(yw, X("WF", l0 + 15, l1, 16), 0.0, Op.min, float(B), Op.add)
+        else:
+            ts(yw, X("WF", l0 + 15, l1, 16), float(B), Op.add)
+        copy("a", X("CY", l0, l1), IND(X("Cw", 0, W + 8) if u else X("CI", 0, B + 8), yw))
+        copy("a", reg("SY", u, l0, l1), IND(X("Sw", 0, W + 8) if u else X("SI", 0, B + 8), yw))
+        yield
 
-    def pairs(q, c0, c1, last):
+    def pairs(q, c1, last, yb="YB", o=0):
         d = 16 * q
         e = 256 * q - d
-        ts(X("EQ", e + c0, e + c1), X("YB", c0, c1), X("WF", d + 15, d + 16), Op.is_equal)
-        if c0 == d:
-            c0 += 16
-            mm(X("KL", d, c0), X("TSB", 0, 128), X("EQ", e + d, e + c0), False, last and c0 == c1)
-        if c0 < c1:
-            mm(X("KL", c0, c1), X("BOB", 0, 128), X("EQ", e + c0, e + c1), False, last)
+        ts(X("EQ", e + d, e + c1), X(yb, o + d, o + c1), X("WF", d + 15, d + 16), Op.is_equal)
+        mm(X("KL", d, d + 16), mat("TP"), X("EQ", e + d, e + d + 16), False, last and d + 16 == c1)
+        if d + 16 < c1:
+            mm(X("KL", d + 16, c1), mat("BP"), X("EQ", e + d + 16, e + c1), False, last)
 
-    def lane_min(u, l0, n):
-        q0, q1 = l0 // 16, (l0 + n) // 16
-        act(X("WS", q0, q1), X("WF", l0 + 15, l0 + n, 16), Act.Sign)
-        act(X("WX", q0, q1), X("WS", q0, q1), Act.Square)
-        act(X("YP", q0, q1), X("WF", l0 + 15, l0 + n, 16), Act.Identity, bias=float(B))
-        for a, b, s in src_c(u, l0, l0 + n):
-            tt(X("MM", a, b), X("CY", a, b), s, Op.min)
+    def lane_min(u, l0, l1):
+        tt(reg("MM", u, l0, l1), X("CY", l0, l1), X("CR", 4 * l0, 4 * l1, 4), Op.min)
 
-    def new_succ(L, Q):
-        copy("v", IND(X("SQ", 0, SPW), X("OFM", 0, Q)), X("SY", 0, L))
+    def signs(u):
+        L = lanes(u)
+        act(X("SG", 0, L), X("KL", 0, L), Act.Sign, bias=-1500.0)
+        mm(X("O2", 256, 256 + L), X("ONK", 0, 128, p=1), X("RA", 0, L, p=1), True, False)
+        mm(X("O2", 256, 256 + L), mat("BN"), X("SG", 0, L), False, True)
 
-    SQM = X("SQ", 0, 16 * M, 16)
+    def ranks(u):
+        L = lanes(u)
+        scan(X("RS", 0, L), X("ON", 0, L), X("O2", 256, 256 + L), -(M + 0.5) * 8192.0, Op.mult, Op.add)
+
+    def inverse(u, q0, q1):
+        L = lanes(u)
+        for q in range(q0, q1):
+            act(X("JK", 256 * q, 256 * q + L - 16 * q), X("RS", 16 * q, L), Act.Sign, bias=X("JB", q, q + 1), scale=1.0 / 8192.0, acc=X("ACC", q, q + 1))
+
+    def inv_list(u, q0, q1):
+        return [lambda: tt(X("IV", q0, q1), X("ACC", q0, q1), X("Q16", q0, q1), Op.subtract),
+                lambda: ts(X("INV", 16 * u + q0, 16 * u + q1), X("IV", q0, q1), -0.5, Op.mult, lanes(u) / 2.0, Op.add)]
+
+    def close_up(out, name, u, q=M // 16):
+        copy("a", out, IND(regw(name, u), X("INV", 16 * u, 16 * u + q)))
+
+    def links(u):
+        L = lanes(u)
+        z = X("OT", 256, 256 + L)
+        act(X("RKB", 0, L), X("RS", 0, L), Act.Identity, bias=M + 0.5, scale=1.0 / 8192.0)
+        mm(z, X("CZ", 128 * u, 128 * u + 128, p=2), X("ONK", 0, L, p=2), True, False)
+        mm(z, mat("BN"), X("SG", 0, L), False, False)
+        mm(z, mat("IP"), X("OS", 0, L), False, False)
+        if u % ST == 0:
+            act(X("OV", 0, L), X("RS", 0, L), Act.Relu, bias=0.5, scale=1.0 / 8192.0)
+            mm(z, mat("IN"), X("OV", 0, L), False, False)
+        mm(z, mat("IDB"), X("RKB", 0, L), False, True)
+
+    def relink(u):
+        t, e = divmod(u, ST)
+        x = (X("Sw", E0 + LE * t, E0 + LE * t + lanes(u)), new("Sw", u - 1), reg("SY", u - 1) if e == 2 else None)[e]
+        tt(x, x, X("OT", 256, 256 + lanes(u)), Op.max)
+
+    def sub(u):
+        L = lanes(u)
+        tt(IND(X("Cw", 0, CW), X("OFY", 0, L // 16)), X("CY", 0, L), reg("MM", u), Op.subtract)
+
+    def send():
+        nxt = T.cores[(rank + 1) % len(T.cores)]
+        rid, pid, _ = topo.addr(nxt)
+        en = topo.engines(core, nxt)[0:4]
+        src, dst = X("PS", 0, LP), X("PORT", 0, LP)
+        emit("g", lambda: g.remote_dma(dst[4], src[4], T.sem["arr"], T.sem["left"], pid, rid, sum(1 << x for x in en)),
+             [dst], [src], sem="arr", n=len(en))
+
+    Q9 = M // 16
     for u in range(U):
         t, e = divmod(u, ST)
-        L = M if e else (LE + LP if t else LE)
-        Q = L // 16
-        last = u == U - 1
-        main = (0, MC if e else 128)
-        aux = (main[1], L - main[1])
-
-        def starts():
-            mm(X("KL", 0, L), X("DL", 0, 128, p=16), X("DC", 0, L, p=16), True, False)
-            mm(X("RR", 0, Q), X("IDH", 0, 128), X("LIH", 0, Q), True, False)
-
-        if u == 0:
-            repeat(u, 48, 128, "a")
-            repeat(u, 128, 208, "v", 0)
-            repeat(u, 0, 48, "v", 80)
-            ts(X("BG", 0, 8), X("BOF", 0, 128, 16), 16.0, Op.mult)
-            copy("v", X("BOH", 0, 128), X("BOF", 0, 128))
-            copy("v", X("IDH", 0, 128), X("IDF", 0, 128))
-            copy("v", X("LIH", 0, 16), X("LIF", 0, 16))
-            copy("v", X("EX", 0, 1), X("SP", 1, 2))
-            copy("v", X("SU0", 0, LE), X("SI", E0, E0 + LE))
-            gather(u, 128, 208)
-            keys(1, *aux)
-            gather(u, 0, 48)
-            gather(u, 48, 128)
-            fillers += [lambda: ts(X("SF0", 0, LE), X("SI", E0, E0 + LE), float(-B), Op.add)]
-            copy("a", X("IDB", 0, 128), X("IDF", 0, 128))
-            copy("a", X("DL", 0, 128, p=16), X("DLF", 0, 128, p=16))
-            copy("a", X("DC", 0, 256, p=16), X("DCF", 0, 256, p=16))
-            copy("a", X("BOB", 0, 128), X("BOF", 0, 128))
-            copy("a", X("TSB", 0, 128), X("TSF", 0, 128))
-            copy("a", X("TIB", 0, 128), X("TIF", 0, 128))
-            zero_a(X("Sw", B, B + 512), X("ON", 0, 512))
-            zero_a(X("Sw", B + 512, WIN), X("ON", 0, WIN - B - 512))
-            starts()
-        else:
-            starts()
-            if e:
-                repeat(u, 0, 80, "a")
-                repeat(u, 80, MC, "g")
-                repeat(u, MC, M, "v")
-                gather(u, MC, M)
-                keys(1, *aux)
-                gather(u, 0, 80)
-                gather(u, 80, MC)
-            else:
-                repeat(u, 48, 128, "a")
-                repeat(u, LE, LE + LP, "a")
-                repeat(u, 176, LE, "g")
-                repeat(u, 0, 48, "v", 0)
-                gather(u, 0, 48)
-                repeat(u, 128, 176, "v", 48)
-                gather(u, 48, 128)
-                keys(0, *main)
-                gather(u, 128, LE)
-                gather(u, LE, LE + LP)
-                new_succ(M, M // 16)
-            copy("a", X("Sw", N0 + M * (u - 1), N0 + M * u), SQM)
-            fillers += s_update(u - 1)
-            if e:
-                fillers.insert(1, lambda u=u: ts(X("SF%d" % u, 0, M), SQM, float(-B), Op.add))
-        zero_a(X("SP", 0, 16 * M, 16), X("SP", 0, 16 * M, 16))
-        if u == 1:
-            fillers += [lambda: copy("v", X("SU3", 0, LE), X("Sw", E0 + LE, E0 + 2 * LE)),
-                        lambda: copy("v", X("SU3", LE, LE + LP), X("Sw", B - LP, B))]
-        if u == 2:
-            fillers += [lambda: ts(X("SF3", 0, LE), X("Sw", E0 + LE, E0 + 2 * LE), float(-B), Op.add),
-                        lambda: ts(X("SF3", LE, LE + LP), X("Sw", B - LP, B), float(-B), Op.add)]
-            spare += ys_conv(E0, E0 + LE)
-        if u == 3:
-            spare += ys_conv(N0, N0 + M)
-        if u == 4:
-            spare += ys_conv(N0 + M, N0 + 2 * M) + ys_conv(E0 + LE, B)
-        if u == 5:
-            spare += ys_conv(N0 + 2 * M, N0 + 3 * M) + ys_conv(N0 + 3 * M, N0 + 4 * M)
-        (c1, k1), (c2, k2) = ((main, 0), (aux, 1)) if u == ST else ((aux, 1), (main, 0))
+        L, a = lanes(u), NA[u]
+        A, Bc = (0, a), (a, L - a)
         if u == ST:
-            pop(2)
-        keys(k2, c2[0], c2[1], 0, 7)
-        best(u, k1, c1[0], c1[1], lambda a, b: keys(k2, c2[0], c2[1], a, b))
+            ranks(u - 1)
+            inverse(u - 1, 0, 3)
+            opens(u, (A, Bc))
+            gather(u, 0, a, LE)
+            for f in inv_list(u - 1, 0, 3):
+                f()
+            close_up(X("PS", 0, LP), "MM", u - 1, 3)
+            send()
+            repeat("a", X("Cw", E0 + LE, E0 + LE + a), 0)
+            for kq in range(1, 4):
+                gather(u, kq, a, LE)
+            links(u - 1)
+            inverse(u - 1, 3, Q9)
+            for kq in range(3):
+                gather(u, kq, 0, a)
+                keys(0, 0, a, kq)
+            repeat("a", X("PORT", 0, LP), LE)
+            for kq in range(4):
+                gather(u, kq, LE, L)
+                keys(1, a, L - a, kq)
+            gather(u, 3, 0, a)
+            keys(0, 0, a, 3)
+        else:
+            opens(u, (A, Bc))
+            for kq in range(3):
+                gather(u, kq, 0, L)
+                keys(0, 0, a, kq)
+                keys(1, a, L - a, kq)
+                if kq == 0 and e:
+                    if e == 2:
+                        ranks(u - 1)
+                    links(u - 1)
+                    if e == 2:
+                        inverse(u - 1, 0, Q9)
+                    if u == 4:
+                        close_up(new("Cw", 2), "MM", 2)
+                        close_up(new("Sw", 1), "SY", 1)
+                        close_up(new("Sw", 2), "SY", 2)
+                        ys_out(B, B + 3 * M)
+            gather(u, 3, a, L)
+            keys(1, a, L - a, 3)
+            gather(u, 3, 0, a)
+            keys(0, 0, a, 3)
         if u:
-            zero_a(SQM, SQM)
-        for q in range(c1[0] // 16, (c1[0] + c1[1]) // 16):
-            pairs(q, 16 * q, c1[0] + c1[1], False)
-        lane_min(u, *c1)
-        while spare:
-            spare.pop(0)()
-        best(u, k2, c2[0], c2[1], None)
+            fillers.append(lambda u=u: relink(u - 1))
+        if e == 2:
+            fillers += inv_list(u - 1, 0, Q9)
+            fillers.append(lambda u=u: close_up(new("Cw", u - 1), "MM", u - 1))
         if u == ST:
-            for q in range(8):
-                pairs(q, 128, L, False)
-            for q in range(8, Q):
-                pairs(q, 16 * q, L, q == Q - 1)
-        else:
-            for q in range(c2[1] // 16):
-                pairs(q, 16 * q, L, q == c2[1] // 16 - 1)
-        lane_min(u, *c2)
-        minima(X("FK", 0, L), X("KL", 0, L))
+            fillers += inv_list(u - 1, 0, Q9)
+            fillers.append(lambda u=u: None)
+        hi, lo = best(u, 1, a, L - a, False), best(u, 0, 0, a, True)
+        next(hi)
+        pop()
+        next(hi)
+        pop()
+        next(hi)
+        pop(2)
+        next(lo)
+        next(hi)
+        next(lo)
+        next(lo)
+        next(hi)
+        next(hi)
+        next(lo)
+        for q in range(a // 16, L // 16):
+            pairs(q, L, False, "SH", 256)
+        next(lo)
+        lane_min(u, a, L)
+        next(lo)
+        if u == 1:
+            ys_out(E0, E0 + LE)
+        if u == 4:
+            ys_out(E0 + LE, B)
+        if u == 5:
+            ys_out(B + 3 * M, B + 4 * M)
+        for q in range(a // 16):
+            pairs(q, L, q == a // 16 - 1)
+        lane_min(u, 0, a)
         fk = X("FK", 15, L, 16)
-        tt(X("AW", 0, Q), fk, X("WX", 0, Q), Op.is_lt)
-        mm(X("RR", 0, Q), X("TIB", 0, 128), X("AW", 0, Q), False, False)
-        if e:
-            tt(X("CN", 0, Q), fk, X("WX", 0, Q), Op.is_ge)
-        scan(X("EX", 1, Q + 1), X("ON16", 0, Q), X("AW", 0, Q), 0.0, Op.mult, Op.add)
-        if e:
-            tt(X("TN", 0, Q), X("CN", 0, Q), X("D2", 0, Q), Op.mult)
-        tt(X("AL", 0, Q), X("AW", 0, Q), X("NLI", 0, Q), Op.mult)
-        mm(X("RR", 0, Q), X("BOB", 0, 128), X("EX", 0, Q), False, False)
-        mm(X("RR", 0, Q), X("IDH", 0, 128), X("AL", 0, Q), False, True)
-
-        places = [lambda: tt(X("TN", 0, Q), X("CN", 0, Q), X("D2", 0, Q), Op.mult),
-                  lambda: tt(X("TO", 0, Q), X("TN", 0, Q), X("YP", 0, Q), Op.max),
-                  lambda: copy("v", X("OFY", 0, Q), X("TO", 0, Q))]
-
-        def p1():
-            tt(X("P1", 0, Q), X("AW" if e else "LV", 0, Q), X("RR", 0, Q), Op.mult)
-
-        def p2():
-            if e:
-                act(X("P2", 0, Q), X("AW", 0, Q), Act.Copy, scale=float(B + M * u))
-            else:
-                ts(X("P2", 0, Q), X("LV", 0, Q), float(B + M * u), Op.mult)
-
-        def sub():
-            tt(IND(X("Cw", 0, CW), X("OFY", 0, Q)), X("CY", 0, L), X("MM", 0, L), Op.subtract)
-
-        def send():
-            nxt = T.cores[(rank + 1) % len(T.cores)]
-            rid, pid, _ = topo.addr(nxt)
-            en = topo.engines(core, nxt)[0:4]
-            src, dst = X("PS", 0, LP), X("PORT", 0, LP)
-            emit("g", lambda: g.remote_dma(dst[4], src[4], T.sem["arr"], T.sem["left"], pid, rid, sum(1 << x for x in en)),
-                 [dst], [src], sem="arr", n=len(en))
-
-        def place_m():
-            ts(X("OFM", 0, Q), X("RR", 0, Q), 16.0, Op.mult, -16.0, Op.add)
-            if not e:
-                ts(X("CN", 0, Q), X("RR", 0, Q), M + 0.5, Op.is_gt)
-            copy("v", IND(X("SP", 0, SPW), X("OFM", 0, Q)), X("MM", 0, L))
-            if u == ST - 1:
-                copy("a", X("PS", 0, LP), X("SP", 0, 16 * LP, 16))
-                send()
-            copy("a", X("Cw", N0 + M * u, N0 + M * (u + 1)), X("SP", 0, 16 * M, 16))
-
-        if not e:
-            place_m()
-            places[0]()
-            new_succ(L, Q)
-            places[1]()
-            ts(X("LV", 0, Q), X("RR", 0, Q), M + 0.5, Op.is_lt)
-            places[2]()
-            p1()
-            copy("v", X("SU%d" % (u + 1), 0, M), SQM)
-            p2()
-            sub()
+        if e == 0:
+            signs(u)
+            scan(X("FK", 0, L), X("RB", 0, L), X("KL", 0, L), 0.0, Op.max, Op.min)
+            ranks(u)
+            inverse(u, 0, Q9)
+            scan(X("RW", 0, L), X("RM", 0, L), X("RS", 0, L), -LOW, Op.max, Op.min)
+            tt(X("TO", 0, L // 16), fk, X("RW", 15, L, 16), Op.max)
+            ts(X("OFY", 0, L // 16), X("TO", 0, L // 16), float(B), Op.add)
+            sub(u)
+            for f in inv_list(u, 0, Q9):
+                f()
+            ts(sf(u + 1), IND(regw("SY", u), X("INV", 16 * u, 16 * u + Q9)), float(-B), Op.add)
+            close_up(new("Cw", u), "MM", u)
+            repeat("a", new("Cw", u), 0)
+            close_up(new("Sw", u), "SY", u)
+            shuffle(u + 1)
+            lists(u + 1)
         else:
-            places[1]()
-            places[2]()
-            if e == ST - 1:
-                sub()
-            if last:
-                dma("y", D("yc", 0, 720), X("Cw", 0, 720))
-                dma("a", D("yc", 720, 1440), X("Cw", 720, 1440))
-                dma("y", D("yc", 1440, B), X("Cw", 1440, B))
-                dma("a", D("yc", B, WIN - 1 - M), X("Cw", N0, WIN - M))
-                p1()
-                p2()
-                place_m()
-                dma("y", D("yc", WIN - 1 - M, WIN - 1), X("Cw", WIN - M, WIN))
-                new_succ(L, Q)
-            elif e == ST - 1:
-                place_m()
-                p1()
-                p2()
-            else:
-                place_m()
-                new_succ(L, Q)
-                p1()
-                copy("v", X("SU%d" % (u + 1), 0, M), SQM)
-                p2()
-                sub()
-        for i in range(16):
-            mm(X("NB", i, L, 16), X("BS", 128 * i, 128 * i + 128), X("P1", 0, Q), True, False)
-            mm(X("NB", i, L, 16), X("BS", 128 * i, 128 * i + 128), X("P2", 0, Q), False, True)
-    fillers += s_update(U - 1)
-    for f in ys_conv(N0 + 5 * M, WIN, SQM):
+            if e == 1:
+                repeat("a", reg("MM", u), 0)
+                ts(sf(u + 1), reg("SY", u), float(-B), Op.add)
+                shuffle(u + 1)
+            scan(X("FK", 0, L), X("RB", 0, L), X("KL", 0, L), 0.0, Op.max, Op.min)
+            signs(u)
+            ts(X("OFY", 0, L // 16), fk, float(B), Op.add)
+            sub(u)
+            if e == 1:
+                lists(u + 1)
+            elif u < U - 1:
+                b = NA[u + 1]
+                repeat("v", X("Cw", E0 + LE + b, E0 + 2 * LE), b, (0, 1))
+                repeat("a", X("Cw", E0 + LE + b, E0 + 2 * LE), b, (2, 3))
+    u = U - 1
+    dma("y", D("yc", 0, 880), X("Cw", 0, 880))
+    dma("y", D("yc", 880, 1760), X("Cw", 880, 1760))
+    dma("y", D("yc", 1760, W - M), X("Cw", 1760, W - M))
+    ranks(u)
+    links(u)
+    inverse(u, 0, Q9)
+    relink(u)
+    for f in inv_list(u, 0, Q9):
         f()
-    pop(99)
-    for f in ys_conv(N0 + 4 * M, N0 + 5 * M):
-        f()
+    close_up(new("Sw", u - 1), "SY", u - 1)
+    close_up(new("Sw", u), "SY", u)
+    ys_out(W - 2 * M, W)
+    close_up(new("Cw", u), "MM", u)
+    dma("a", D("yc", W - M, W), new("Cw", u))
     g.wait_ge(T.sem["left"], inc["arr"])
     for q in cnt:
         g.wait_ge(T.sem[semname(q)], cnt[q] * inc[q])

@@ -10,27 +10,30 @@ T16 = float(16 * TH)
 BIG = 33554432.0
 LOW = 2097152.0
 RG = 264
-NA = {0: 96, 1: 112, 2: 112, 3: 128, 4: 112, 5: 112}
+NA = [128, 128, 128, 128, 128, 128]
+NS = [128, 96, 96, 128, 96, 96]
+LEAVES = [2, 4, 5]
 
 f32, b16, f16, u16, i32 = "float32", "bfloat16", "float16", "uint16", "int32"
 SCRATCH = {n: ("sbuf", [128, c], d) for n, c, d in [
     ("CI", B + 8, i32), ("SI", B + 8, i32), ("Cw", CW, f32), ("Sw", W + 8, f32), ("CR", 1024, f32), ("MG", 4096, f32),
+    ("GS", 2048, f32),
     ("SF", 256 * U, f16), ("SU", 256 * U, u16), ("MM", RG * U, f32), ("SY", RG * U, f32), ("INV", 16 * U, u16),
     ("FF0", 128, f32), ("FF1", 128, f32), ("MX0", 128, f32), ("MX1", 128, f32), ("OH0", 128, b16), ("OH1", 128, b16),
-    ("OS", 256, b16), ("PT", 256, f16), ("WF", 256, f32), ("YW", 18, u16), ("EQ", 4096, b16), ("CY", 256, f32),
+    ("OS", 512, b16), ("PT", 256, f16), ("WF", 256, f32), ("YW", 18, u16), ("EQ", 4096, b16), ("CY", 256, f32),
     ("FK", 256, f32), ("OFY", 16, u16), ("SG", 256, b16), ("RS", 256, f32), ("RW", 256, f32), ("TO", 16, f32),
     ("ACC", 16, f32), ("JK", 2304, b16), ("IV", 16, f32), ("RKB", 256, b16), ("OV", 256, b16),
-    ("PORT", LP, f32), ("PS", LP, f32),
+    ("CO", 3 * M, f32), ("PORT", LP, f32), ("PM", M + 8, f32), ("PL", 4, u16), ("PO", 4, u16),
     ("ON", 512, f32), ("RK", 128, f32), ("RB", 256, f32), ("RM", 256, f32), ("DG", 256, f32), ("LM", 256, f32), ("LR", 256, f32),
     ("BOX", 128, f32), ("BOF", 128, f32), ("TSF", 128, f32), ("IDW", 160, f32), ("WS", 640, f16),
     ("PI", 2, i32), ("PR", 2, i32), ("PF", 2, f32), ("I4", 4, f32), ("MK4", 4, f32), ("Q16", 16, f32), ("JB", 16, f32),
     ("BG", 8, f32), ("BOH", 128, f16), ("IDB", 128, b16), ("IP", 128, b16), ("IN", 128, b16), ("BN", 128, b16),
     ("BP", 128, b16), ("BH", 128, b16), ("BD", 128, b16), ("TP", 128, b16), ("MY", 256, b16), ("MK", 256, b16),
     ("KC", 128, b16), ("ONK", 256, b16), ("C14", 128, b16), ("RH", 256, b16), ("RA", 256, b16), ("CZ", 128 * U, b16)]}
-for _n in ("KP0", "KP1", "OT", "O2", "YD", "YB", "KL", "SH"):
+for _n in ("KP0", "KP1", "OT", "O2", "YD", "YB", "KL", "CP"):
     SCRATCH[_n] = ("psum", [128, 512], f32)
 NDMA = 24
-SEMAPHORES = ["qv", "qt", "qa", "qg", "arr", "left"] + ["d%d" % i for i in range(NDMA)]
+SEMAPHORES = ["qv", "qt", "qa", "qg", "arm", "arl", "left"] + ["d%d" % i for i in range(NDMA)]
 
 
 def rank_program(g, core, T, topo):
@@ -55,7 +58,7 @@ def rank_program(g, core, T, topo):
     def semname(q):
         return {"v": "qv", "t": "qt", "a": "qa", "g": "qg"}.get(q, q)
 
-    def emit(q, call, outs, ins, sem=None, n=1):
+    def emit(q, call, outs, ins, sem=None, n=1, remote=False):
         acc = [(o, True) for o in outs] + [(i, False) for i in ins]
         acc += [(o[5], False) for o in list(outs) + list(ins) if o[5] is not None]
         need = {}
@@ -88,7 +91,7 @@ def rank_program(g, core, T, topo):
         for (o, w) in acc:
             hist.setdefault(o[0], []).append((me, cnt[me], o[1], o[2], o[3], w))
         inst = call()
-        if sem != "arr":
+        if not remote:
             inst.then_inc(T.sem[semname(me)], n)
 
     def act(out, in_, func, bias=None, scale=None, acc=None):
@@ -172,15 +175,20 @@ def rank_program(g, core, T, topo):
         return X("SF", 256 * u + l0, 256 * u + (lanes(u) if l1 is None else l1), step)
 
     def new(name, u):
+        if name == "Cw" and u in LEAVES:
+            return X("CO", M * LEAVES.index(u), M * LEAVES.index(u) + M)
         return X(name, B + M * u, B + M * (u + 1))
+
+    def yc_new(u, q="y"):
+        dma(q, D("yc", B + M * u, B + M * (u + 1)), new("Cw", u))
 
     def ys_out(c0, c1, q="y"):
         dma(q, D("ys", c0 - E0, c1 - E0), X("Sw", c0, c1))
 
-    dma("y", X("SI", E0, B), D("s0", E0, B))
+    dma("y", X("SI", E0, E0 + LE), D("s0", E0, E0 + LE))
     dma("a", X("CI", E0, B), D("c0", E0, B))
-    dma("y", X("CI", 0, 736), D("c0", 0, 736))
-    dma("a", X("CI", 736, E0), D("c0", 736, E0))
+    dma("y", X("CI", 0, E0), D("c0", 0, E0))
+    dma("a", X("SI", E0 + LE, B), D("s0", E0 + LE, B))
     dma("y", X("SI", 0, E0), D("s0", 0, E0))
 
     fill(X("ON", 0, 512), 1.0)
@@ -206,6 +214,8 @@ def rank_program(g, core, T, topo):
     fill(X("RA", 0, 256, p=1), 65536.0)
     fill(X("MM", 256, RG * U, RG), 0.0)
     fill(X("SY", 256, RG * U, RG), 0.0)
+    fill(X("PM", M, M + 8), 0.0)
+    fill(X("PO", 0, 4), 0)
     fill(X("CI", B, B + 8), 0)
     fill(X("SI", B, B + 8), 0)
     ts(X("PR", 0, 1), X("PI", 0, 1), 15, Op.bitwise_and)
@@ -224,27 +234,32 @@ def rank_program(g, core, T, topo):
                          ("IN", idf, -8192.0), ("BD", mat("BOF"), -16777216.0)):
         act(mat(name), src, Act.Copy, scale=s)
 
-    def shuffle(u):
+    def shuffle(u, kqs=range(4), bank=None):
         n = lanes(u) // 4
-        for kq in range(4):
+        for kq in kqs:
             for h in range(4):
                 s = 160 * kq + 12 + 4 * (kq - h)
-                mm(X("SH", n * kq, n * kq + n), X("WS", s, s + 128), sf(u, h, None, 4), h == 0, h == 3)
+                mm(X(bank or "KP%d" % (kq > 0), 128 + n * kq, 128 + n * kq + n), X("WS", s, s + 128), sf(u, h, None, 4),
+                   h == 0, h == 3)
 
-    def lists(u):
-        ts(X("SU", 256 * u, 256 * u + lanes(u)), X("SH", 0, lanes(u)), float(B), Op.add)
+    def lists(u, k0, k1, bank=None):
+        c0, c1 = k0 * lanes(u) // 4, k1 * lanes(u) // 4
+        ts(X("SU", 256 * u + c0, 256 * u + c1), X(bank or "KP%d" % (k0 > 0), 128 + c0, 128 + c1), float(B), Op.add)
 
-    def repeat(q, src, l0, ks=range(4)):
+    def repeat(q, to, src, l0, l1, ks=range(4)):
         for k in ks:
-            copy(q, X("CR", 4 * l0 + k, 4 * (l0 + src[2] - src[1]), 4), src)
+            copy(q, X(to, 4 * l0 + k, 4 * l1, 4), X(src[0], src[1] + l0, src[1] + l1))
+
+    def repeats(q, src, u):
+        repeat(q, "CR", src, min(NA[u], NS[u]), lanes(u))
+        repeat(q, "CP", src, 0, max(NA[u], NS[u]))
 
     ts(sf(0), X("SI", E0, E0 + LE), float(-B), Op.add)
     shuffle(0)
     ts(X("BG", 0, 8), X("BOF", 0, 128, 16), 16.0, Op.mult)
-    repeat("v", X("CI", E0, E0 + LE), 0)
-    lists(0)
-    ts(sf(ST), X("SI", E0 + LE, B), float(-B), Op.add)
-    shuffle(ST)
+    repeats("v", X("CI", E0, E0 + LE), 0)
+    lists(0, 0, 1)
+    lists(0, 1, 4)
     copy("v", mat("BOH"), mat("BOF"))
     ts(X("DG", 0, 256), X("LM", 0, 256), X("PF", 0, 1), Op.is_equal)
     ts(X("JB", 0, 16), X("Q16", 0, 16), X("PF", 0, 1), Op.add)
@@ -252,49 +267,59 @@ def rank_program(g, core, T, topo):
     ts(X("RB", 0, 256, 16), X("JB", 0, 16), float(DUMP - B), Op.add)
     ts(X("JB", 0, 16), X("JB", 0, 16), -1.0, Op.mult, float(M), Op.add)
     ts(X("RM", 0, 256), X("RW", 0, 256), -LOW, Op.add)
-    lists(ST)
     act(X("MY", 0, 256), X("DG", 0, 256), Act.Identity, bias=4096.0 + W - B, scale=-4096.0)
     act(X("MK", 0, 256), X("DG", 0, 256), Act.Identity, bias=8192.0, scale=-4096.0)
     copy_g(X("Cw", 0, B), X("CI", 0, B), B)
     copy_g(X("Sw", E0, B), X("SI", E0, B), B - E0)
     copy_g(X("Sw", 0, E0), X("SI", 0, E0), E0)
 
-    fillers = []
-
-    def pop(n=1):
-        for _ in range(n):
-            if fillers:
-                fillers.pop(0)()
-
-    def opens(u, chunks):
-        L = lanes(u)
-        for ch, (l0, n) in enumerate(chunks):
+    def opens(u):
+        L, a = lanes(u), NA[u]
+        for ch, (l0, n) in enumerate(((0, a), (a, L - a))):
             kp = X("KP%d" % ch, 0, 128, p=n)
             if u % ST == 2:
                 mm(kp, X("ONK", 0, n, p=1), X("C14", 0, 128, p=1), True, False)
                 mm(kp, X("SG", l0, l0 + n), mat("BD"), False, False)
             mm(kp, X("ONK", 0, n, p=1), X("KC", 0, 128, p=1), u % ST != 2, False)
-        a = chunks[1][0]
-        mm(X("YD", a, L), mat("IDB"), X("MY", a, L), True, False)
-        mm(X("YB", a, L), X("ONK", 0, 128, p=1), X("RH", 0, L - a, p=1), True, False)
-        mm(X("SH", 256 + a, 256 + L), X("ONK", 0, 128, p=1), X("RH", 0, L - a, p=1), True, False)
+        l0, l1 = (0, L) if u % ST else (0, a) if u else (a, L)
+        mm(X("YD", l0, l1), mat("IDB"), X("MY", l0, l1), True, False)
+        mm(X("YB", l0, l1), X("ONK", 0, 128, p=1), X("RH", 0, l1 - l0, p=1), True, False)
         mm(X("KL", 0, L), mat("IDB"), X("MK", 0, L), True, False)
 
-    def gather(u, kq, l0, l1):
-        L = lanes(u)
+    def counts(u, kq, l0, l1):
         win = X("CI", 0, B) if u == 0 else X("Cw", 0, B + M * (u - 1) if u != ST else B)
-        o = 256 * u + L // 4 * kq
-        tt(X("MG", 1024 * kq + 4 * l0, 1024 * kq + 4 * l1), IND(win, X("SU", o + l0 // 4, o + l1 // 4)),
-           X("CR", 4 * l0, 4 * l1), Op.min)
+        o = 256 * u + lanes(u) // 4 * kq
+        return IND(win, X("SU", o + l0 // 4, o + l1 // 4))
 
-    def keys(ch, l0, n, kq):
+    def mg(kq, l0, l1):
+        return X("MG", 1024 * kq + 4 * l0, 1024 * kq + 4 * l1)
+
+    def gather(u, kq, l0, l1):
+        tt(mg(kq, l0, l1), counts(u, kq, l0, l1), X("CR", 4 * l0, 4 * l1), Op.min)
+
+    def fetch(u, kq):
+        copy("a", X("GS", 512 * kq, 512 * kq + 4 * NS[u]), counts(u, kq, 0, NS[u]))
+
+    def smaller(u, kq):
+        tt(mg(kq, 0, NS[u]), X("GS", 512 * kq, 512 * kq + 4 * NS[u]), X("CP", 0, 4 * NS[u]), Op.min)
+
+    def keys(u, ch, kq):
+        l0, n = (0, NA[u]) if ch == 0 else (NA[u], lanes(u) - NA[u])
         for i in range(4):
             a = 1024 * kq + 4 * l0
             mm(X("KP%d" % ch, 4 * kq + i, 128, 16, p=n), X("MG", a + i, a + 4 * n, 4), X("BG", 0, 8), False, 4 * kq + i == 15)
 
-    def best(u, ch, l0, n, final):
+    def yw(u, l0, l1):
+        q0 = l0 // 16 + l0 // 16 % 2
+        return X("YW", q0, q0 + (l1 - l0) // 16)
+
+    def chosen(u, l0=0, l1=None):
+        return X("OS", 256 * (u % 2) + l0, 256 * (u % 2) + (lanes(u) if l1 is None else l1))
+
+    def best(u, ch):
         kp, ff, mx, oh = ["%s%d" % (b, ch) for b in ("KP", "FF", "MX", "OH")]
-        l1 = l0 + n
+        l0, l1 = (0, NA[u]) if ch == 0 else (NA[u], lanes(u))
+        n = l1 - l0
         scan(X(ff, 0, 128, p=n), X("RK", 0, 128, p=n), X(kp, 0, 128, p=n), T16, Op.min, Op.max)
         yield
         scan(REV(mx, n), X("RK", 0, 128, p=n), REV(ff, n), T16, Op.min, Op.max)
@@ -302,38 +327,50 @@ def rank_program(g, core, T, topo):
         tt(X(oh, 0, 128, p=n), X(kp, 0, 128, p=n), X(mx, 0, 128, p=n), Op.is_equal)
         mm(X("OT", l0, l1), X(oh, 0, 128, p=n), X("IDB", 0, n, p=n), True, True)
         mm(X("O2", l0, l1), X(oh, 0, 128, p=n), X("IDB", 0, n, p=n), True, True)
-        copy("a", X("OS", l0, l1), X("O2", l0, l1))
         yield
-        tt(X("PT", l0, l1), sf(u, l0, l1), X("OT", l0, l1), Op.mult)
-        if final:
+
+    def targets(u, l0, l1, own=None, late=False):
+        n = l1 - l0
+        os = chosen(u, l0, l1)
+        copy("a", os, X("O2", l0, l1))
+        if own:
+            own = X(own, 384, 384 + n)
+            mm(own, X("ONK", 0, 128, p=1), X("RH", 0, n, p=1), True, False)
+        if late:
             mm(X("YD", l0, l1), mat("IDB"), X("MY", l0, l1), True, False)
             mm(X("YB", l0, l1), X("ONK", 0, 128, p=1), X("RH", 0, n, p=1), True, False)
-        for b, o, m in [("YD", 0, "BH")] + [("SH", 256, "BH")] * (not final) + [("YB", 0, "BH"), ("KL", 0, "BN")]:
-            mm(X(b, o + l0, o + l1), mat(m), X("OS", l0, l1), False, False)
-            mm(X(b, o + l0, o + l1), mat("BOH"), X("PT", l0, l1), False, b != "KL")
+        tt(X("PT", l0, l1), sf(u, l0, l1), X("OT", l0, l1), Op.mult)
+        for o in [X("YD", l0, l1)] + [own] * bool(own) + [X("YB", l0, l1)]:
+            mm(o, mat("BH"), os, False, False)
+            mm(o, mat("BOH"), X("PT", l0, l1), False, True)
+        mm(X("KL", l0, l1), mat("BN"), os, False, False)
+        mm(X("KL", l0, l1), mat("BOH"), X("PT", l0, l1), False, False)
         yield
         scan(X("WF", l0, l1), X("RB", l0, l1), X("YD", l0, l1), 0.0, Op.max, Op.min)
         yield
-        q0 = l0 // 16 + l0 // 16 % 2
-        yw = X("YW", q0, q0 + n // 16)
         if u == 0:
-            ts(yw, X("WF", l0 + 15, l1, 16), 0.0, Op.min, float(B), Op.add)
+            ts(yw(u, l0, l1), X("WF", l0 + 15, l1, 16), 0.0, Op.min, float(B), Op.add)
         else:
-            ts(yw, X("WF", l0 + 15, l1, 16), float(B), Op.add)
-        copy("a", X("CY", l0, l1), IND(X("Cw", 0, W + 8) if u else X("CI", 0, B + 8), yw))
-        copy("a", reg("SY", u, l0, l1), IND(X("Sw", 0, W + 8) if u else X("SI", 0, B + 8), yw))
+            ts(yw(u, l0, l1), X("WF", l0 + 15, l1, 16), float(B), Op.add)
+        yield
+        copy("a", X("CY", l0, l1), IND(X("Cw", 0, W + 8) if u else X("CI", 0, B + 8), yw(u, l0, l1)))
         yield
 
-    def pairs(q, c1, last, yb="YB", o=0):
+    def succs(u, l0, l1):
+        copy("a", reg("SY", u, l0, l1), IND(X("Sw", 0, W + 8) if u else X("SI", 0, B + 8), yw(u, l0, l1)))
+
+    def pairs(u, q, c0, c1, last, yb="YB", o=0):
         d = 16 * q
         e = 256 * q - d
-        ts(X("EQ", e + d, e + c1), X(yb, o + d, o + c1), X("WF", d + 15, d + 16), Op.is_equal)
-        mm(X("KL", d, d + 16), mat("TP"), X("EQ", e + d, e + d + 16), False, last and d + 16 == c1)
-        if d + 16 < c1:
-            mm(X("KL", d + 16, c1), mat("BP"), X("EQ", e + d + 16, e + c1), False, last)
+        ts(X("EQ", e + c0, e + c1), X(yb, o + c0, o + c1), X("WF", d + 15, d + 16), Op.is_equal)
+        if c0 == d:
+            c0 += 16
+            mm(X("KL", d, c0), mat("TP"), X("EQ", e + d, e + c0), False, last and c0 == c1)
+        if c0 < c1:
+            mm(X("KL", c0, c1), mat("BP"), X("EQ", e + c0, e + c1), False, last)
 
-    def lane_min(u, l0, l1):
-        tt(reg("MM", u, l0, l1), X("CY", l0, l1), X("CR", 4 * l0, 4 * l1, 4), Op.min)
+    def lane_min(u, l0, l1, c):
+        tt(reg("MM", u, l0, l1), X("CY", l0, l1), X(c, 4 * l0, 4 * l1, 4), Op.min)
 
     def signs(u):
         L = lanes(u)
@@ -341,184 +378,238 @@ def rank_program(g, core, T, topo):
         mm(X("O2", 256, 256 + L), X("ONK", 0, 128, p=1), X("RA", 0, L, p=1), True, False)
         mm(X("O2", 256, 256 + L), mat("BN"), X("SG", 0, L), False, True)
 
+    def firsts(u):
+        L = lanes(u)
+        scan(X("FK", 0, L), X("RB", 0, L), X("KL", 0, L), 0.0, Op.max, Op.min)
+
     def ranks(u):
         L = lanes(u)
         scan(X("RS", 0, L), X("ON", 0, L), X("O2", 256, 256 + L), -(M + 0.5) * 8192.0, Op.mult, Op.add)
 
+    def small_ranks(u):
+        L = lanes(u)
+        act(X("RKB", 0, L), X("RS", 0, L), Act.Identity, bias=M + 0.5, scale=1.0 / 8192.0)
+        if u % ST == 0:
+            act(X("OV", 0, L), X("RS", 0, L), Act.Relu, bias=0.5, scale=1.0 / 8192.0)
+
     def inverse(u, q0, q1):
         L = lanes(u)
         for q in range(q0, q1):
-            act(X("JK", 256 * q, 256 * q + L - 16 * q), X("RS", 16 * q, L), Act.Sign, bias=X("JB", q, q + 1), scale=1.0 / 8192.0, acc=X("ACC", q, q + 1))
+            act(X("JK", 256 * q, 256 * q + L - 16 * q), X("RS", 16 * q, L), Act.Sign, bias=X("JB", q, q + 1),
+                scale=1.0 / 8192.0, acc=X("ACC", q, q + 1))
 
-    def inv_list(u, q0, q1):
-        return [lambda: tt(X("IV", q0, q1), X("ACC", q0, q1), X("Q16", q0, q1), Op.subtract),
-                lambda: ts(X("INV", 16 * u + q0, 16 * u + q1), X("IV", q0, q1), -0.5, Op.mult, lanes(u) / 2.0, Op.add)]
+    def inv_a(q1):
+        tt(X("IV", 0, q1), X("ACC", 0, q1), X("Q16", 0, q1), Op.subtract)
 
-    def close_up(out, name, u, q=M // 16):
-        copy("a", out, IND(regw(name, u), X("INV", 16 * u, 16 * u + q)))
+    def inv_b(u, q1, out=None):
+        ts(out or X("INV", 16 * u, 16 * u + q1), X("IV", 0, q1), -0.5, Op.mult, lanes(u) / 2.0, Op.add)
+
+    def close_up(name, u):
+        copy("a", new(name + "w", u), IND(regw({"C": "MM", "S": "SY"}[name], u), X("INV", 16 * u, 16 * u + Q9)))
 
     def links(u):
         L = lanes(u)
-        z = X("OT", 256, 256 + L)
-        act(X("RKB", 0, L), X("RS", 0, L), Act.Identity, bias=M + 0.5, scale=1.0 / 8192.0)
+        z = X("KP1", 128, 128 + L)
         mm(z, X("CZ", 128 * u, 128 * u + 128, p=2), X("ONK", 0, L, p=2), True, False)
+        mm(z, mat("IP"), chosen(u), False, False)
         mm(z, mat("BN"), X("SG", 0, L), False, False)
-        mm(z, mat("IP"), X("OS", 0, L), False, False)
         if u % ST == 0:
-            act(X("OV", 0, L), X("RS", 0, L), Act.Relu, bias=0.5, scale=1.0 / 8192.0)
             mm(z, mat("IN"), X("OV", 0, L), False, False)
         mm(z, mat("IDB"), X("RKB", 0, L), False, True)
 
     def relink(u):
         t, e = divmod(u, ST)
         x = (X("Sw", E0 + LE * t, E0 + LE * t + lanes(u)), new("Sw", u - 1), reg("SY", u - 1) if e == 2 else None)[e]
-        tt(x, x, X("OT", 256, 256 + lanes(u)), Op.max)
+        tt(x, x, X("KP1", 128, 128 + lanes(u)), Op.max)
 
     def sub(u):
         L = lanes(u)
         tt(IND(X("Cw", 0, CW), X("OFY", 0, L // 16)), X("CY", 0, L), reg("MM", u), Op.subtract)
 
-    def send():
+    sent = [0]
+
+    def send(dst, src, sem):
         nxt = T.cores[(rank + 1) % len(T.cores)]
         rid, pid, _ = topo.addr(nxt)
-        en = topo.engines(core, nxt)[0:4]
-        src, dst = X("PS", 0, LP), X("PORT", 0, LP)
-        emit("g", lambda: g.remote_dma(dst[4], src[4], T.sem["arr"], T.sem["left"], pid, rid, sum(1 << x for x in en)),
-             [dst], [src], sem="arr", n=len(en))
+        en = topo.engines(core, nxt)
+        sent[0] += len(en)
+        emit("g", lambda: g.remote_dma(dst[4], src[4], T.sem[sem], T.sem["left"], pid, rid, sum(1 << x for x in en)),
+             [dst], [src], sem=sem, n=len(en), remote=True)
 
     Q9 = M // 16
+    ent = X("Cw", E0 + LE, B)
     for u in range(U):
         t, e = divmod(u, ST)
-        L, a = lanes(u), NA[u]
-        A, Bc = (0, a), (a, L - a)
+        L, a, s = lanes(u), NA[u], NS[u]
         if u == ST:
-            ranks(u - 1)
-            inverse(u - 1, 0, 3)
-            opens(u, (A, Bc))
+            opens(u)
             gather(u, 0, a, LE)
-            for f in inv_list(u - 1, 0, 3):
-                f()
-            close_up(X("PS", 0, LP), "MM", u - 1, 3)
-            send()
-            repeat("a", X("Cw", E0 + LE, E0 + LE + a), 0)
-            for kq in range(1, 4):
-                gather(u, kq, a, LE)
-            links(u - 1)
-            inverse(u - 1, 3, Q9)
-            for kq in range(3):
-                gather(u, kq, 0, a)
-                keys(0, 0, a, kq)
-            repeat("a", X("PORT", 0, LP), LE)
+            inv_a(3)
+            inv_b(u - 1, 3, X("PO", 0, 3))
+            send(X("PL", 0, 4), X("PO", 0, 4), "arl")
+            repeat("a", "CP", ent, 0, a)
+            gather(u, 1, a, LE)
+            for kq in range(4):
+                fetch(u, kq)
+                if kq < 2:
+                    gather(u, kq + 2, a, LE)
+                smaller(u, kq)
+                keys(u, 0, kq)
+            copy("a", X("PORT", 0, LP), IND(X("PM", 0, M + 1), X("PL", 0, 3)))
+            repeat("a", "CR", ("PORT", -LE), LE, L)
             for kq in range(4):
                 gather(u, kq, LE, L)
-                keys(1, a, L - a, kq)
-            gather(u, 3, 0, a)
-            keys(0, 0, a, 3)
+                keys(u, 1, kq)
+            small_ranks(u - 1)
+            inverse(u - 1, 3, Q9)
+            close_up("C", 1)
         else:
-            opens(u, (A, Bc))
-            for kq in range(3):
-                gather(u, kq, 0, L)
-                keys(0, 0, a, kq)
-                keys(1, a, L - a, kq)
-                if kq == 0 and e:
-                    if e == 2:
-                        ranks(u - 1)
-                    links(u - 1)
-                    if e == 2:
-                        inverse(u - 1, 0, Q9)
-                    if u == 4:
-                        close_up(new("Cw", 2), "MM", 2)
-                        close_up(new("Sw", 1), "SY", 1)
-                        close_up(new("Sw", 2), "SY", 2)
-                        ys_out(B, B + 3 * M)
-            gather(u, 3, a, L)
-            keys(1, a, L - a, 3)
-            gather(u, 3, 0, a)
-            keys(0, 0, a, 3)
-        if u:
-            fillers.append(lambda u=u: relink(u - 1))
+            gather(u, 0, s, L)
+            if e:
+                lists(u, 1, 4)
+            opens(u)
+            for kq in range(4):
+                fetch(u, kq)
+                if kq < 3:
+                    gather(u, kq + 1, s, L)
+                if a >= s:
+                    for k2 in ((0, 1), (2,), (3,), ())[kq]:
+                        keys(u, 1, k2)
+                smaller(u, kq)
+                if a < s:
+                    keys(u, 1, kq)
+                keys(u, 0, kq)
+        hi, lo = best(u, int(u != ST)), best(u, int(u == ST))
+        if e == 1:
+            small_ranks(u - 1)
+            close_up("S", u - 1)
+        if u == 4:
+            close_up("S", 1)
         if e == 2:
-            fillers += inv_list(u - 1, 0, Q9)
-            fillers.append(lambda u=u: close_up(new("Cw", u - 1), "MM", u - 1))
-        if u == ST:
-            fillers += inv_list(u - 1, 0, Q9)
-            fillers.append(lambda u=u: None)
-        hi, lo = best(u, 1, a, L - a, False), best(u, 0, 0, a, True)
-        next(hi)
-        pop()
-        next(hi)
-        pop()
-        next(hi)
-        pop(2)
-        next(lo)
-        next(hi)
-        next(lo)
-        next(lo)
+            ranks(u - 1)
+            small_ranks(u - 1)
+            inverse(u - 1, 0, 3)
+        if u == 0:
+            ts(sf(ST), X("SI", E0 + LE, B), float(-B), Op.add)
+        mins = [(0, a, "CP"), (a, L, "CR")]
         next(hi)
         next(hi)
-        next(lo)
-        for q in range(a // 16, L // 16):
-            pairs(q, L, False, "SH", 256)
-        next(lo)
-        lane_min(u, a, L)
-        next(lo)
+        next(hi)
+        if e:
+            links(u - 1)
+            for _ in lo:
+                pass
+            if u < ST:
+                shuffle(ST, (2 * u - 2, 2 * u - 1), "KP0")
+            y = targets(u, 0, L)
+            relink(u - 1)
+            next(y)
+            if e == 2:
+                inverse(u - 1, 3, 7)
+            if u < ST:
+                lists(ST, 2 * u - 2, 2 * u, "KP0")
+            next(y)
+            next(y)
+            next(y)
+        else:
+            c1, c2 = ((0, a), (a, L)) if u else ((a, L), (0, a))
+            y1, y2 = targets(u, *c1, own="KP%d" % (u == 0)), targets(u, *c2, late=True)
+            next(lo)
+            next(y1)
+            next(lo)
+            next(lo)
+            next(y1)
+            next(y1)
+            next(y2)
+            next(y1)
+            if u:
+                links(u - 1)
+            for q in range(c1[0] // 16, c1[1] // 16):
+                pairs(u, q, 16 * q, c1[1], False, "KP%d" % (u == 0), 384 - c1[0])
+            next(y2)
+            next(y2)
+            next(y2)
+            lane_min(u, *mins.pop(u == 0))
+        if a // 16 % 2 and e == 0:
+            succs(u, 0, a)
+            succs(u, a, L)
+        else:
+            succs(u, 0, L)
         if u == 1:
             ys_out(E0, E0 + LE)
-        if u == 4:
-            ys_out(E0 + LE, B)
+        if e == 2:
+            inverse(u - 1, 7, Q9)
         if u == 5:
-            ys_out(B + 3 * M, B + 4 * M)
-        for q in range(a // 16):
-            pairs(q, L, q == a // 16 - 1)
-        lane_min(u, 0, a)
+            close_up("S", 2)
+            ys_out(E0 + LE, B + 4 * M)
+            close_up("C", 2)
+            yc_new(2)
+        blocks = range(L // 16 if u else a // 16)
+        for q in blocks:
+            pairs(u, q, max(16 * q, a) if u == ST else 16 * q, L, q == blocks[-1])
+        for m in mins:
+            lane_min(u, *m)
         fk = X("FK", 15, L, 16)
         if e == 0:
+            if u:
+                inv_a(Q9)
+                inv_b(u - 1, Q9)
             signs(u)
-            scan(X("FK", 0, L), X("RB", 0, L), X("KL", 0, L), 0.0, Op.max, Op.min)
+            firsts(u)
             ranks(u)
             inverse(u, 0, Q9)
             scan(X("RW", 0, L), X("RM", 0, L), X("RS", 0, L), -LOW, Op.max, Op.min)
             tt(X("TO", 0, L // 16), fk, X("RW", 15, L, 16), Op.max)
             ts(X("OFY", 0, L // 16), X("TO", 0, L // 16), float(B), Op.add)
             sub(u)
-            for f in inv_list(u, 0, Q9):
-                f()
+            if u:
+                relink(u - 1)
+            inv_a(Q9)
+            inv_b(u, Q9)
             ts(sf(u + 1), IND(regw("SY", u), X("INV", 16 * u, 16 * u + Q9)), float(-B), Op.add)
-            close_up(new("Cw", u), "MM", u)
-            repeat("a", new("Cw", u), 0)
-            close_up(new("Sw", u), "SY", u)
+            close_up("C", u)
+            repeat("a", "CP", new("Cw", u), 0, NA[u + 1])
+            repeat("v", "CR", new("Cw", u), NS[u + 1], M)
             shuffle(u + 1)
-            lists(u + 1)
-        else:
-            if e == 1:
-                repeat("a", reg("MM", u), 0)
-                ts(sf(u + 1), reg("SY", u), float(-B), Op.add)
-                shuffle(u + 1)
-            scan(X("FK", 0, L), X("RB", 0, L), X("KL", 0, L), 0.0, Op.max, Op.min)
+            lists(u + 1, 0, 1)
+        elif e == 1:
+            repeats("a", reg("MM", u), u + 1)
+            ts(sf(u + 1), reg("SY", u), float(-B), Op.add)
+            shuffle(u + 1)
+            firsts(u)
             signs(u)
             ts(X("OFY", 0, L // 16), fk, float(B), Op.add)
             sub(u)
-            if e == 1:
-                lists(u + 1)
-            elif u < U - 1:
-                b = NA[u + 1]
-                repeat("v", X("Cw", E0 + LE + b, E0 + 2 * LE), b, (0, 1))
-                repeat("a", X("Cw", E0 + LE + b, E0 + 2 * LE), b, (2, 3))
+            lists(u + 1, 0, 1)
+        else:
+            if u < U - 1:
+                send(X("PM", 0, M), reg("MM", u), "arm")
+            inv_a(Q9)
+            inv_b(u - 1, Q9)
+            firsts(u)
+            signs(u)
+            if u == U - 1:
+                close_up("C", u - 1)
+            ts(X("OFY", 0, L // 16), fk, float(B), Op.add)
+            sub(u)
+            ranks(u)
+            if u < U - 1:
+                inverse(u, 0, 3)
+                repeat("v", "CR", ent, NA[u + 1], LE)
     u = U - 1
-    dma("y", D("yc", 0, 880), X("Cw", 0, 880))
-    dma("y", D("yc", 880, 1760), X("Cw", 880, 1760))
-    dma("y", D("yc", 1760, W - M), X("Cw", 1760, W - M))
-    ranks(u)
+    dma("y", D("yc", 0, B + 2 * M), X("Cw", 0, B + 2 * M))
+    dma("y", D("yc", B + 3 * M, B + 4 * M), new("Cw", 3))
+    small_ranks(u)
     links(u)
     inverse(u, 0, Q9)
     relink(u)
-    for f in inv_list(u, 0, Q9):
-        f()
-    close_up(new("Sw", u - 1), "SY", u - 1)
-    close_up(new("Sw", u), "SY", u)
+    inv_a(Q9)
+    inv_b(u, Q9)
+    close_up("S", u - 1)
+    close_up("S", u)
     ys_out(W - 2 * M, W)
-    close_up(new("Cw", u), "MM", u)
-    dma("a", D("yc", W - M, W), new("Cw", u))
-    g.wait_ge(T.sem["left"], inc["arr"])
+    close_up("C", u)
+    dma("a", D("yc", W - 2 * M, W), X("CO", M, 3 * M))
+    g.wait_ge(T.sem["left"], sent[0])
     for q in cnt:
         g.wait_ge(T.sem[semname(q)], cnt[q] * inc[q])

@@ -11,7 +11,22 @@ BIG = 33554432.0
 LOW = 2097152.0
 RG = 264
 NA = [128, 128, 128, 128, 128, 128]
-NS = [128, 96, 96, 128, 96, 96]
+O0 = "gfgBBmAfgBmAfgBmAfmA"
+O1 = "gfgBBmAfgBmAfgBmAfmA"
+O3 = "rcigflgfgmAfgmAfmAmAqpBpBpBpB"
+ORDER = [O0, O1, O1, O3, O1, O1]
+N4 = [80, 88, 88, 104]
+NS = [[128] * 4, N4, N4, [128] * 4, N4, N4]
+COPIES = [2, 4, 5]
+EARLY = False
+AUTO = False
+CYC, PE, GATHER, SCATTER, WAKE, WAIT, RATE, NEAR, FAR = 0.85, 0.46, 1.56, 3.3, 165.0, 27.0, 280.0, 1350.0, 3000.0
+FIRST, PASSES, SLACK = False, 2, 20.0
+CPT = [0, 0, 4]
+SPLIT = []
+QS = 7
+SB = [96, 128]
+YAT = 0
 LEAVES = [2, 4, 5]
 
 f32, b16, f16, u16, i32 = "float32", "bfloat16", "float16", "uint16", "int32"
@@ -19,19 +34,21 @@ SCRATCH = {n: ("sbuf", [128, c], d) for n, c, d in [
     ("CI", B + 8, i32), ("SI", B + 8, i32), ("Cw", CW, f32), ("Sw", W + 8, f32), ("CR", 1024, f32), ("MG", 4096, f32),
     ("GS", 2048, f32),
     ("SF", 256 * U, f16), ("SU", 256 * U, u16), ("MM", RG * U, f32), ("SY", RG * U, f32), ("INV", 16 * U, u16),
-    ("FF0", 128, f32), ("FF1", 128, f32), ("MX0", 128, f32), ("MX1", 128, f32), ("OH0", 128, b16), ("OH1", 128, b16),
-    ("OS", 512, b16), ("PT", 256, f16), ("WF", 256, f32), ("YW", 18, u16), ("EQ", 4096, b16), ("CY", 256, f32),
+    ("FF0", 128, f32), ("FF1", 128, f32), ("OH0", 128, b16), ("OH1", 128, b16),
+    ("OS", 512, b16), ("PT", 256, f16), ("WF", 256, f32), ("YW", 18, u16), ("CY", 256, f32),
     ("FK", 256, f32), ("OFY", 16, u16), ("SG", 256, b16), ("RS", 256, f32), ("RW", 256, f32), ("TO", 16, f32),
     ("ACC", 16, f32), ("JK", 2304, b16), ("IV", 16, f32), ("RKB", 256, b16), ("OV", 256, b16),
     ("CO", 3 * M, f32), ("PORT", LP, f32), ("PM", M + 8, f32), ("PL", 4, u16), ("PO", 4, u16),
-    ("ON", 512, f32), ("RK", 128, f32), ("RB", 256, f32), ("RM", 256, f32), ("DG", 256, f32), ("LM", 256, f32), ("LR", 256, f32),
+    ("ON", 512, f32), ("RK", 256, f32), ("RB", 256, f32), ("RM", 256, f32), ("DG", 256, f32), ("LM", 256, f32), ("LR", 256, f32),
     ("BOX", 128, f32), ("BOF", 128, f32), ("TSF", 128, f32), ("IDW", 160, f32), ("WS", 640, f16),
     ("PI", 2, i32), ("PR", 2, i32), ("PF", 2, f32), ("I4", 4, f32), ("MK4", 4, f32), ("Q16", 16, f32), ("JB", 16, f32),
+    ("CC", M, f32), ("C4", 32, f32), ("CL", 32, u16), ("JT", 16, f32), ("QV", 32, f32), ("JA", 16, f32), ("JV", 256, b16),
     ("BG", 8, f32), ("BOH", 128, f16), ("IDB", 128, b16), ("IP", 128, b16), ("IN", 128, b16), ("BN", 128, b16),
-    ("BP", 128, b16), ("BH", 128, b16), ("BD", 128, b16), ("TP", 128, b16), ("MY", 256, b16), ("MK", 256, b16),
+    ("BP", 128, b16), ("BH", 128, b16), ("BD", 128, b16), ("TP", 128, b16), ("MY", 256, b16), ("M0", 256, b16), ("MK", 256, b16),
     ("KC", 128, b16), ("ONK", 256, b16), ("C14", 128, b16), ("RH", 256, b16), ("RA", 256, b16), ("CZ", 128 * U, b16)]}
 for _n in ("KP0", "KP1", "OT", "O2", "YD", "YB", "KL", "CP"):
     SCRATCH[_n] = ("psum", [128, 512], f32)
+SCRATCH["EQ"] = ("sbuf", [128, 16, 256], b16)
 NDMA = 24
 SEMAPHORES = ["qv", "qt", "qa", "qg", "arm", "arl", "left"] + ["d%d" % i for i in range(NDMA)]
 
@@ -49,8 +66,8 @@ def rank_program(g, core, T, topo):
         ap = T[name][0:p, c0:c1] if step == 1 else T[name][0:p, c0:c1:step]
         return (name, c0, c1, step, ap, None)
 
-    def REV(name, p):
-        return (name, 0, 128, 1, T[name][0:p, ::-1], None)
+    def REV(name, p, c0=0):
+        return (name, c0, c0 + 128, 1, T[name][0:p, c0 + 127:c0 - 1:-1] if c0 else T[name][0:p, 127::-1], None)
 
     def IND(x, off):
         return (x[0], x[1], x[2], 1, x[4].indirect(off[4]), off)
@@ -58,22 +75,101 @@ def rank_program(g, core, T, topo):
     def semname(q):
         return {"v": "qv", "t": "qt", "a": "qa", "g": "qg"}.get(q, q)
 
-    def emit(q, call, outs, ins, sem=None, n=1, remote=False):
+    calls, seen = [], {}
+
+    def size(x):
+        return 16 * size(x[5]) if x[5] is not None else -(-(x[2] - x[1]) // x[3])
+
+    def emit(q, call, outs, ins, sem=None, n=1, remote=False, ns=None):
         acc = [(o, True) for o in outs] + [(i, False) for i in ins]
         acc += [(o[5], False) for o in list(outs) + list(ins) if o[5] is not None]
-        need = {}
+        after, behind = set(), set()
         for (o, w) in acc:
             name, c0, c1, st = o[0:4]
-            for (q2, n2, d0, d1, s2, w2) in hist.get(name, []):
+            for (i2, q2, d0, d1, s2, w2) in seen.get(name, []):
                 if name in psum and q2 != q:
-                    pass
+                    after.add(i2)
                 elif name in psum and q == "t":
-                    continue
-                elif not (w or w2) or d1 <= c0 or c1 <= d0:
-                    continue
-                elif st == s2 and st > 1 and c0 % st != d0 % st:
-                    continue
-                need[q2] = max(need.get(q2, 0), n2)
+                    behind.add(i2)
+                elif (w or w2) and c0 < d1 and d0 < c1 and not (st == s2 and st > 1 and c0 % st != d0 % st):
+                    after.add(i2)
+        for (o, w) in acc:
+            seen.setdefault(o[0], []).append((len(calls), q, o[1], o[2], o[3], w))
+        if ns is None:
+            k = size(outs[0])
+            if outs[0][5] is not None:
+                ns = 50 + SCATTER * CYC * k
+            elif ins and ins[0][5] is not None:
+                ns = (50 if q == "v" else 65) + GATHER * CYC * k
+            else:
+                ns = CYC * max(64, k)
+        calls.append(dict(q=q, call=call, sem=sem, n=n, remote=remote, after=after, behind=behind, ns=ns,
+                          bytes=512 * size(outs[0]) if sem else 0))
+
+    def order():
+        nc = len(calls)
+        takes = [c["ns"] + (c["bytes"] / RATE + (FAR if c["remote"] else NEAR) if c["sem"] else 0) for c in calls]
+        chain = takes[:]
+        users = [[] for _ in calls]
+        for i in range(nc - 1, -1, -1):
+            for j in calls[i]["after"]:
+                chain[j] = max(chain[j], takes[j] + WAKE + chain[i])
+                users[j].append(i)
+            for j in calls[i]["behind"] - calls[i]["after"]:
+                chain[j] = max(chain[j], takes[j] + chain[i])
+                users[j].append(i)
+        holds = [c["ns"] + WAIT * bool(c["after"]) for c in calls]
+        before = [[(j, WAKE) for j in c["after"]] + [(j, 0.0) for j in c["behind"] - c["after"]] for c in calls]
+        later = [[] for _ in calls]
+        for i in range(nc):
+            for j, w in before[i]:
+                later[j].append((i, w))
+
+        def place(rank, edges, back):
+            busy = {q: [] for q in list(eng) + ["pipe"]}
+            t0, t1 = {}, {}
+
+            def gap(q, t, d):
+                for k, (a, b) in enumerate(busy[q]):
+                    if t + d <= a + SLACK and t <= a:
+                        busy[q].insert(k, (t, t + d))
+                        return t
+                    t = max(t, b)
+                busy[q].append((t, t + d))
+                return t
+            for i in rank:
+                c = calls[i]
+                t = max([t1[j] + w for j, w in edges[i]] + [0.0])
+                lag = (FAR if c["remote"] else NEAR) if c["sem"] else 0.0
+                if back:
+                    if c["sem"] and not c["remote"]:
+                        t = gap("pipe", t, c["bytes"] / RATE) + c["bytes"] / RATE
+                    t0[i] = gap(c["q"], t + lag, holds[i])
+                    t1[i] = t0[i] + holds[i]
+                else:
+                    t0[i] = gap(c["q"], t, holds[i])
+                    t1[i] = t0[i] + holds[i] + lag
+                    if c["sem"] and not c["remote"]:
+                        t1[i] = gap("pipe", t1[i], c["bytes"] / RATE) + c["bytes"] / RATE
+            return t0, t1
+
+        rank = sorted(range(nc), key=lambda i: (-chain[i], i)) if FIRST else list(range(nc))
+        best_end, best_rank = None, None
+        for _ in range(PASSES):
+            t0, t1 = place(rank, before, False)
+            rank = sorted(range(nc), key=lambda i: (t0[i], i))
+            if best_end is None or max(t1.values()) < best_end:
+                best_end, best_rank = max(t1.values()), rank
+            t0, t1 = place(sorted(range(nc), key=lambda i: (-t1[i], -i)), later, True)
+            rank = sorted(range(nc), key=lambda i: (-t1[i], i))
+        return best_rank
+
+    def issue(i):
+        q, call, sem, n, remote = [calls[i][k] for k in ("q", "call", "sem", "n", "remote")]
+        need = {}
+        for j in calls[i]["after"]:
+            q2, n2 = calls[j]["mark"]
+            need[q2] = max(need.get(q2, 0), n2)
         kn = known[q]
         todo = [(q2, n2) for q2, n2 in need.items() if kn.get(q2, 0) < n2]
         todo = [(q2, n2) for q2, n2 in todo
@@ -88,8 +184,7 @@ def rank_program(g, core, T, topo):
         c = dict(kn)
         c[me] = cnt[me]
         clock[(me, cnt[me])] = c
-        for (o, w) in acc:
-            hist.setdefault(o[0], []).append((me, cnt[me], o[1], o[2], o[3], w))
+        calls[i]["mark"] = (me, cnt[me])
         inst = call()
         if not remote:
             inst.then_inc(T.sem[semname(me)], n)
@@ -113,7 +208,9 @@ def rank_program(g, core, T, topo):
             act(out, in_, Act.Copy)
 
     def tt(out, a, b, op):
-        emit("v", lambda: g.vector.tensor_tensor(out[4], a[4], b[4], op), [out], [a, b])
+        slow = out[5] is None and a[5] is None and a[0] not in psum and b[0] not in psum
+        emit("v", lambda: g.vector.tensor_tensor(out[4], a[4], b[4], op), [out], [a, b],
+             ns=CYC * max(64, 2 * size(out)) if slow else None)
 
     def ts(out, a, s1, op0, s2=None, op1=None):
         col = isinstance(s1, tuple)
@@ -134,26 +231,28 @@ def rank_program(g, core, T, topo):
         act(out, X("ON", 0, out[2] - out[1]), Act.Copy, scale=0.0)
 
     def mm(out, lhsT, rhs, start, stop):
-        emit("t", lambda: g.tensor.matmul(out[4], lhsT[4], rhs[4], start, stop), [out], [lhsT, rhs])
+        emit("t", lambda: g.tensor.matmul(out[4], lhsT[4], rhs[4], start, stop), [out], [lhsT, rhs],
+             ns=PE * max(min(64, size(lhsT)), size(rhs)) * (4 if SCRATCH[rhs[0]][2] == f32 else 1))
 
     def aff(out, in_, pattern, op, f, base, cm):
-        emit("g", lambda: g.affine_select(out[4], in_[4], pattern, op, f, base, cm), [out], [in_])
+        emit("g", lambda: g.affine_select(out[4], in_[4], pattern, op, f, base, cm), [out], [in_], ns=170 + 2 * CYC * size(out))
 
     def copy_g(out, in_, n):
         aff(out, in_, [[0, n]], Op.is_gt, 0.0, 1, 0)
 
     def iota(out, pattern, base, cm, whole=False):
         if whole:
-            emit("g", lambda: g.iota(out[4], pattern, base, cm), [out], [])
+            emit("g", lambda: g.iota(out[4], pattern, base, cm), [out], [], ns=130 + 2 * CYC * size(out))
         else:
-            emit("g", lambda: g.iota(out[4], pattern, base, cm, allow_small_or_imprecise_dtypes=True), [out], [])
+            emit("g", lambda: g.iota(out[4], pattern, base, cm, allow_small_or_imprecise_dtypes=True), [out], [],
+                 ns=130 + 2 * CYC * size(out))
 
     ndma = [0]
 
     def dma(q, out, in_):
         s = "d%d" % ndma[0]
         ndma[0] += 1
-        emit(q, lambda: eng[q].dma_start(out[4], in_[4]), [out], [in_], sem=s, n=16)
+        emit(q, lambda: eng[q].dma_start(out[4], in_[4]), [out], [in_], sem=s, n=16, ns=60)
 
     def D(name, c0, c1):
         return (name, c0, c1, 1, T[name][:, c0:c1], None)
@@ -197,20 +296,26 @@ def rank_program(g, core, T, topo):
     aff(X("IDW", 0, 160), X("ON", 0, 160), [[-1, 160]], Op.is_equal, 0.0, 12, 1)
     aff(mat("BOX"), mat("ON"), [[-16, 8], [0, 16]], Op.is_ge, 0.0, 0, 1)
     aff(mat("BOF"), mat("BOX"), [[16, 8], [0, 16]], Op.is_ge, 0.0, 15, -1)
-    iota(X("KC", 0, 128, p=1), [[0, 8], [-1, 16]], 15, 0)
     iota(X("LM", 0, 256), [[0, 16], [1, 16]], 0, 0)
     iota(X("Q16", 0, 16), [[16, 16]], 0, 0)
     iota(X("LR", 0, 256), [[1, 256]], DUMP - B + int(LOW), 0)
+    iota(X("C4", 0, 32), [[4, 32]], 0, 0)
     aff(mat("TSF"), mat("BOF"), [[1, 128]], Op.is_gt, 0.0, 0, -1)
+    iota(X("KC", 0, 128, p=1), [[0, 8], [-1, 16]], 15, 0)
     for u in range(U):
         c = B - 1 + M * u - 8192 + 14 * 4096
         iota(X("CZ", 128 * u, 128 * u + 128, p=2), [[0, 128]], c - c % 256, c % 256 - (c - c % 256))
-    fill(mat("RK"), BIG)
+    ts(X("PR", 0, 1), X("PI", 0, 1), 15, Op.bitwise_and)
+    fill(X("RK", 0, 256), BIG)
+    ts(X("PR", 1, 2), X("PR", 0, 1), 2, Op.arith_shift_right)
     fill(X("RB", 0, 256), -LOW)
+    copy("v", X("PF", 0, 2), X("PR", 0, 2))
     fill(X("ONK", 0, 256, p=2), 1.0)
-    fill(X("RK", 0, 128, 16), T16)
-    fill(X("C14", 0, 128, p=1), 14.0 * 16777216.0)
     fill(X("RH", 0, 256, p=1), float(W - B))
+    ts(X("MK4", 0, 4), X("I4", 0, 4), X("PF", 1, 2), Op.is_equal)
+    fill(X("RK", 0, 128, 16), T16 - 0.5)
+    fill(X("RK", 128, 256, 16), T16 - 0.25)
+    fill(X("C14", 0, 128, p=1), 14.0 * 16777216.0)
     fill(X("RA", 0, 256, p=1), 65536.0)
     fill(X("MM", 256, RG * U, RG), 0.0)
     fill(X("SY", 256, RG * U, RG), 0.0)
@@ -218,10 +323,6 @@ def rank_program(g, core, T, topo):
     fill(X("PO", 0, 4), 0)
     fill(X("CI", B, B + 8), 0)
     fill(X("SI", B, B + 8), 0)
-    ts(X("PR", 0, 1), X("PI", 0, 1), 15, Op.bitwise_and)
-    ts(X("PR", 1, 2), X("PR", 0, 1), 2, Op.arith_shift_right)
-    copy("v", X("PF", 0, 2), X("PR", 0, 2))
-    ts(X("MK4", 0, 4), X("I4", 0, 4), X("PF", 1, 2), Op.is_equal)
     for kq in range(4):
         ts(X("WS", 160 * kq, 160 * kq + 160), X("IDW", 0, 160), X("MK4", kq, kq + 1), Op.mult)
     zero_a(X("Cw", B, B + 512))
@@ -250,25 +351,38 @@ def rank_program(g, core, T, topo):
         for k in ks:
             copy(q, X(to, 4 * l0 + k, 4 * l1, 4), X(src[0], src[1] + l0, src[1] + l1))
 
-    def repeats(q, src, u):
-        repeat(q, "CR", src, min(NA[u], NS[u]), lanes(u))
-        repeat(q, "CP", src, 0, max(NA[u], NS[u]))
+    def spread(src, l0, l1):
+        copy("a", X("CR", 4 * l0, 4 * l1), IND(X(src[0], src[1] + l0, src[1] + l1), X("CL", 0, (l1 - l0) // 4)))
+
+    def spread_t(src, ks):
+        for k in ks:
+            mm(X("CP", k, 512, 4), idf, X(src[0], src[1], src[1] + 128), True, True)
 
     ts(sf(0), X("SI", E0, E0 + LE), float(-B), Op.add)
     shuffle(0)
     ts(X("BG", 0, 8), X("BOF", 0, 128, 16), 16.0, Op.mult)
-    repeats("v", X("CI", E0, E0 + LE), 0)
+    ts(X("DG", 0, 256), X("LM", 0, 256), X("PF", 0, 1), Op.is_equal)
+    ts(X("JA", 0, 16), X("Q16", 0, 16), X("PF", 0, 1), Op.add)
+    copy("v", mat("BOH"), mat("BOF"))
+    repeat("v", "CR", X("CI", E0, E0 + LE), 128, LE)
+    repeat("v", "CP", X("CI", E0, E0 + LE), 0, 128)
     lists(0, 0, 1)
     lists(0, 1, 4)
-    copy("v", mat("BOH"), mat("BOF"))
-    ts(X("DG", 0, 256), X("LM", 0, 256), X("PF", 0, 1), Op.is_equal)
-    ts(X("JB", 0, 16), X("Q16", 0, 16), X("PF", 0, 1), Op.add)
     tt(X("RW", 0, 256), X("DG", 0, 256), X("LR", 0, 256), Op.mult)
-    ts(X("RB", 0, 256, 16), X("JB", 0, 16), float(DUMP - B), Op.add)
-    ts(X("JB", 0, 16), X("JB", 0, 16), -1.0, Op.mult, float(M), Op.add)
-    ts(X("RM", 0, 256), X("RW", 0, 256), -LOW, Op.add)
-    act(X("MY", 0, 256), X("DG", 0, 256), Act.Identity, bias=4096.0 + W - B, scale=-4096.0)
+    ts(X("RB", 0, 256, 16), X("JA", 0, 16), float(DUMP - B), Op.add)
+    ts(X("CL", 0, 32), X("C4", 0, 32), X("PF", 1, 2), Op.add)
+    act(X("M0", 0, 256), X("DG", 0, 256), Act.Identity, bias=4096.0, scale=-4096.0)
     act(X("MK", 0, 256), X("DG", 0, 256), Act.Identity, bias=8192.0, scale=-4096.0)
+    act(X("MY", 0, 256), X("DG", 0, 256), Act.Identity, bias=4096.0 + W - B, scale=-4096.0)
+
+    def late_constants():
+        act(X("JB", 0, 16), X("JA", 0, 16), Act.Identity, bias=float(M), scale=-1.0)
+        act(X("JT", 0, 16), X("JA", 0, 16), Act.Identity, bias=-8192.0 * M, scale=8192.0)
+        for t in range(RO):
+            copy("a", X("QV", 16 * t, 16 * t + QS), X("Q16", 0, QS))
+            act(X("QV", 16 * t + QS, 16 * t + 16), X("Q16", QS, 16), Act.Identity, bias=float(lanes(ST * t)), scale=0.0)
+        act(X("RM", 0, 256), X("RW", 0, 256), Act.Identity, bias=-LOW)
+
     copy_g(X("Cw", 0, B), X("CI", 0, B), B)
     copy_g(X("Sw", E0, B), X("SI", E0, B), B - E0)
     copy_g(X("Sw", 0, E0), X("SI", 0, E0), E0)
@@ -281,9 +395,10 @@ def rank_program(g, core, T, topo):
                 mm(kp, X("ONK", 0, n, p=1), X("C14", 0, 128, p=1), True, False)
                 mm(kp, X("SG", l0, l0 + n), mat("BD"), False, False)
             mm(kp, X("ONK", 0, n, p=1), X("KC", 0, 128, p=1), u % ST != 2, False)
-        l0, l1 = (0, L) if u % ST else (0, a) if u else (a, L)
-        mm(X("YD", l0, l1), mat("IDB"), X("MY", l0, l1), True, False)
-        mm(X("YB", l0, l1), X("ONK", 0, 128, p=1), X("RH", 0, l1 - l0, p=1), True, False)
+        l0, l1 = (0, L) if u % ST else (0, a) if u and not EARLY else (a, L)
+        mm(X("YD", l0, l1), mat("IDB"), X("MY" if u in COPIES else "M0", l0, l1), True, False)
+        if u in COPIES:
+            mm(X("YB", l0, l1), X("ONK", 0, 128, p=1), X("RH", 0, l1 - l0, p=1), True, False)
         mm(X("KL", 0, L), mat("IDB"), X("MK", 0, L), True, False)
 
     def counts(u, kq, l0, l1):
@@ -298,10 +413,17 @@ def rank_program(g, core, T, topo):
         tt(mg(kq, l0, l1), counts(u, kq, l0, l1), X("CR", 4 * l0, 4 * l1), Op.min)
 
     def fetch(u, kq):
-        copy("a", X("GS", 512 * kq, 512 * kq + 4 * NS[u]), counts(u, kq, 0, NS[u]))
+        s = NS[u][kq]
+        copy("a", X("GS", 512 * kq, 512 * kq + 4 * s), counts(u, kq, 0, s))
 
     def smaller(u, kq):
-        tt(mg(kq, 0, NS[u]), X("GS", 512 * kq, 512 * kq + 4 * NS[u]), X("CP", 0, 4 * NS[u]), Op.min)
+        s = NS[u][kq]
+        if kq in SPLIT:
+            for i in range(4):
+                tt(X("MG", 1024 * kq + i, 1024 * kq + 4 * s, 4), X("GS", 512 * kq + i, 512 * kq + 4 * s, 4),
+                   X("CP", i, 4 * s, 4), Op.min)
+        else:
+            tt(mg(kq, 0, s), X("GS", 512 * kq, 512 * kq + 4 * s), X("CP", 0, 4 * s), Op.min)
 
     def keys(u, ch, kq):
         l0, n = (0, NA[u]) if ch == 0 else (NA[u], lanes(u) - NA[u])
@@ -317,14 +439,13 @@ def rank_program(g, core, T, topo):
         return X("OS", 256 * (u % 2) + l0, 256 * (u % 2) + (lanes(u) if l1 is None else l1))
 
     def best(u, ch):
-        kp, ff, mx, oh = ["%s%d" % (b, ch) for b in ("KP", "FF", "MX", "OH")]
+        kp, ff, oh = ["%s%d" % (b, ch) for b in ("KP", "FF", "OH")]
         l0, l1 = (0, NA[u]) if ch == 0 else (NA[u], lanes(u))
         n = l1 - l0
-        scan(X(ff, 0, 128, p=n), X("RK", 0, 128, p=n), X(kp, 0, 128, p=n), T16, Op.min, Op.max)
+        scan(X(ff, 0, 128, p=n), X("RK", 0, 128, p=n), X(kp, 0, 128, p=n), T16 - 0.5, Op.min, Op.max)
+        scan(REV(kp, n, 128), X("RK", 128, 256, p=n), REV(kp, n), T16 - 0.25, Op.min, Op.max)
         yield
-        scan(REV(mx, n), X("RK", 0, 128, p=n), REV(ff, n), T16, Op.min, Op.max)
-        yield
-        tt(X(oh, 0, 128, p=n), X(kp, 0, 128, p=n), X(mx, 0, 128, p=n), Op.is_equal)
+        tt(X(oh, 0, 128, p=n), X(ff, 0, 128, p=n), X(kp, 128, 256, p=n), Op.is_equal)
         mm(X("OT", l0, l1), X(oh, 0, 128, p=n), X("IDB", 0, n, p=n), True, True)
         mm(X("O2", l0, l1), X(oh, 0, 128, p=n), X("IDB", 0, n, p=n), True, True)
         yield
@@ -333,25 +454,19 @@ def rank_program(g, core, T, topo):
         n = l1 - l0
         os = chosen(u, l0, l1)
         copy("a", os, X("O2", l0, l1))
-        if own:
-            own = X(own, 384, 384 + n)
-            mm(own, X("ONK", 0, 128, p=1), X("RH", 0, n, p=1), True, False)
         if late:
-            mm(X("YD", l0, l1), mat("IDB"), X("MY", l0, l1), True, False)
-            mm(X("YB", l0, l1), X("ONK", 0, 128, p=1), X("RH", 0, n, p=1), True, False)
+            mm(X("YD", l0, l1), mat("IDB"), X("M0", l0, l1), True, False)
         tt(X("PT", l0, l1), sf(u, l0, l1), X("OT", l0, l1), Op.mult)
-        for o in [X("YD", l0, l1)] + [own] * bool(own) + [X("YB", l0, l1)]:
-            mm(o, mat("BH"), os, False, False)
-            mm(o, mat("BOH"), X("PT", l0, l1), False, True)
-        mm(X("KL", l0, l1), mat("BN"), os, False, False)
+        for o in [X("YD", l0, l1)] + ([X(own, 384, 384 + n)] if own else []) + [X("YB", l0, l1)]:
+            if u in COPIES:
+                mm(o, mat("BH"), os, False, False)
+            mm(o, mat("BOH"), X("PT", l0, l1), o[0] != "YD" and u not in COPIES, True)
         mm(X("KL", l0, l1), mat("BOH"), X("PT", l0, l1), False, False)
+        mm(X("KL", l0, l1), mat("BN"), os, False, False)
         yield
         scan(X("WF", l0, l1), X("RB", l0, l1), X("YD", l0, l1), 0.0, Op.max, Op.min)
         yield
-        if u == 0:
-            ts(yw(u, l0, l1), X("WF", l0 + 15, l1, 16), 0.0, Op.min, float(B), Op.add)
-        else:
-            ts(yw(u, l0, l1), X("WF", l0 + 15, l1, 16), float(B), Op.add)
+        ts(yw(u, l0, l1), X("WF", l0 + 15, l1, 16), float(B), Op.add)
         yield
         copy("a", X("CY", l0, l1), IND(X("Cw", 0, W + 8) if u else X("CI", 0, B + 8), yw(u, l0, l1)))
         yield
@@ -361,13 +476,16 @@ def rank_program(g, core, T, topo):
 
     def pairs(u, q, c0, c1, last, yb="YB", o=0):
         d = 16 * q
-        e = 256 * q - d
-        ts(X("EQ", e + c0, e + c1), X(yb, o + c0, o + c1), X("WF", d + 15, d + 16), Op.is_equal)
-        if c0 == d:
-            c0 += 16
-            mm(X("KL", d, c0), mat("TP"), X("EQ", e + d, e + c0), False, last and c0 == c1)
+        ts(eq(q, c0 - d, c1 - d), X(yb, o + c0, o + c1), X("WF", d + 15, d + 16), Op.is_equal)
+        c0 = max(c0, d + 16)
         if c0 < c1:
-            mm(X("KL", c0, c1), mat("BP"), X("EQ", e + c0, e + c1), False, last)
+            mm(X("KL", c0, c1), mat("BP"), eq(q, c0 - d, c1 - d), False, last)
+
+    def eq(q, c0, c1):
+        return ("EQ", 256 * q + c0, 256 * q + c1, 1, T["EQ"][:, q, c0:c1], None)
+
+    def within(q0, q1, last):
+        mm(X("KL", 16 * q0, 16 * q1), mat("TP"), ("EQ", 256 * q0, 256 * q1 - 240, 1, T["EQ"][:, q0:q1, 0:16], None), False, last)
 
     def lane_min(u, l0, l1, c):
         tt(reg("MM", u, l0, l1), X("CY", l0, l1), X(c, 4 * l0, 4 * l1, 4), Op.min)
@@ -398,8 +516,16 @@ def rank_program(g, core, T, topo):
             act(X("JK", 256 * q, 256 * q + L - 16 * q), X("RS", 16 * q, L), Act.Sign, bias=X("JB", q, q + 1),
                 scale=1.0 / 8192.0, acc=X("ACC", q, q + 1))
 
-    def inv_a(q1):
-        tt(X("IV", 0, q1), X("ACC", 0, q1), X("Q16", 0, q1), Op.subtract)
+    def inverse_v(u, q):
+        L = lanes(u)
+        ts(X("JV", 16 * q, L), X("RS", 16 * q, L), X("JT", q, q + 1), Op.is_gt, 2.0, Op.mult)
+        yield
+        emit("v", lambda: g.vector.tensor_reduce(T["ACC"][:, q:q + 1], T["JV"][:, 16 * q:L], AxisListType.X, Op.add),
+             [X("ACC", q, q + 1)], [X("JV", 16 * q, L)], ns=CYC * (L - 16 * q))
+        yield
+
+    def inv_a(q1, t=None):
+        tt(X("IV", 0, q1), X("ACC", 0, q1), X("Q16", 0, q1) if t is None else X("QV", 16 * t, 16 * t + q1), Op.subtract)
 
     def inv_b(u, q1, out=None):
         ts(out or X("INV", 16 * u, 16 * u + q1), X("IV", 0, q1), -0.5, Op.mult, lanes(u) / 2.0, Op.add)
@@ -422,77 +548,75 @@ def rank_program(g, core, T, topo):
         x = (X("Sw", E0 + LE * t, E0 + LE * t + lanes(u)), new("Sw", u - 1), reg("SY", u - 1) if e == 2 else None)[e]
         tt(x, x, X("KP1", 128, 128 + lanes(u)), Op.max)
 
-    def sub(u):
-        L = lanes(u)
-        tt(IND(X("Cw", 0, CW), X("OFY", 0, L // 16)), X("CY", 0, L), reg("MM", u), Op.subtract)
+    def sub(u, l0=0, l1=None):
+        l1 = lanes(u) if l1 is None else l1
+        if l0 < l1:
+            tt(IND(X("Cw", 0, CW), X("OFY", l0 // 16, l1 // 16)), X("CY", l0, l1), reg("MM", u, l0, l1), Op.subtract)
 
     sent = [0]
 
     def send(dst, src, sem):
         nxt = T.cores[(rank + 1) % len(T.cores)]
         rid, pid, _ = topo.addr(nxt)
-        en = topo.engines(core, nxt)
+        en = topo.engines(core, nxt)[0::2]
         sent[0] += len(en)
         emit("g", lambda: g.remote_dma(dst[4], src[4], T.sem[sem], T.sem["left"], pid, rid, sum(1 << x for x in en)),
-             [dst], [src], sem=sem, n=len(en), remote=True)
+             [dst], [src], sem=sem, n=len(en), remote=True, ns=500)
 
     Q9 = M // 16
     ent = X("Cw", E0 + LE, B)
     for u in range(U):
         t, e = divmod(u, ST)
         L, a, s = lanes(u), NA[u], NS[u]
-        if u == ST:
-            opens(u)
-            gather(u, 0, a, LE)
-            inv_a(3)
-            inv_b(u - 1, 3, X("PO", 0, 3))
-            send(X("PL", 0, 4), X("PO", 0, 4), "arl")
-            repeat("a", "CP", ent, 0, a)
-            gather(u, 1, a, LE)
-            for kq in range(4):
+        nxt = {c: 0 for c in "fgmpABirlcq"}
+        for c in ORDER[u]:
+            kq = nxt[c]
+            nxt[c] += 1
+            if c == "f":
                 fetch(u, kq)
-                if kq < 2:
-                    gather(u, kq + 2, a, LE)
+            elif c == "g":
+                if kq == 0:
+                    if e:
+                        lists(u, 1, 4)
+                    opens(u)
+                gather(u, kq, s[kq], LE if u == ST else L)
+            elif c == "m":
                 smaller(u, kq)
-                keys(u, 0, kq)
-            copy("a", X("PORT", 0, LP), IND(X("PM", 0, M + 1), X("PL", 0, 3)))
-            repeat("a", "CR", ("PORT", -LE), LE, L)
-            for kq in range(4):
+            elif c == "p":
                 gather(u, kq, LE, L)
-                keys(u, 1, kq)
+            elif c in "AB":
+                keys(u, "AB".index(c), kq)
+            elif c == "i":
+                inverse(u - 1, 0, 3)
+            elif c == "r":
+                repeat("v", "CR", ent, a, LE)
+            elif c == "l":
+                inv_a(3)
+                inv_b(u - 1, 3, X("PO", 0, 3))
+                send(X("PL", 0, 4), X("PO", 0, 4), "arl")
+            elif c == "c":
+                spread_t(ent, range(CPT[2]))
+                repeat("a", "CP", ent, 0, 128, range(CPT[2], 4))
+            else:
+                copy("a", X("PORT", 0, LP), IND(X("PM", 0, M + 1), X("PL", 0, 3)))
+                spread(("PORT", -LE), LE, L)
+        if u == ST:
             small_ranks(u - 1)
             inverse(u - 1, 3, Q9)
             close_up("C", 1)
-        else:
-            gather(u, 0, s, L)
-            if e:
-                lists(u, 1, 4)
-            opens(u)
-            for kq in range(4):
-                fetch(u, kq)
-                if kq < 3:
-                    gather(u, kq + 1, s, L)
-                if a >= s:
-                    for k2 in ((0, 1), (2,), (3,), ())[kq]:
-                        keys(u, 1, k2)
-                smaller(u, kq)
-                if a < s:
-                    keys(u, 1, kq)
-                keys(u, 0, kq)
-        hi, lo = best(u, int(u != ST)), best(u, int(u == ST))
+        up = u != ST or EARLY
+        hi, lo = best(u, int(up)), best(u, int(not up))
         if e == 1:
             small_ranks(u - 1)
             close_up("S", u - 1)
-        if u == 4:
-            close_up("S", 1)
         if e == 2:
             ranks(u - 1)
             small_ranks(u - 1)
             inverse(u - 1, 0, 3)
         if u == 0:
+            late_constants()
             ts(sf(ST), X("SI", E0 + LE, B), float(-B), Op.add)
         mins = [(0, a, "CP"), (a, L, "CR")]
-        next(hi)
         next(hi)
         next(hi)
         if e:
@@ -508,94 +632,102 @@ def rank_program(g, core, T, topo):
                 inverse(u - 1, 3, 7)
             if u < ST:
                 lists(ST, 2 * u - 2, 2 * u, "KP0")
-            next(y)
-            next(y)
+            if e == 1:
+                copy("a", new("Cw", u - 1), X("CC", 0, M))
+            if u == 4:
+                close_up("S", 1)
+                close_up("S", 2)
+                close_up("C", 2)
+                yc_new(2)
+            if u == 5:
+                ys_out(B + 2 * M, B + 4 * M)
             next(y)
         else:
-            c1, c2 = ((0, a), (a, L)) if u else ((a, L), (0, a))
-            y1, y2 = targets(u, *c1, own="KP%d" % (u == 0)), targets(u, *c2, late=True)
+            c1, c2 = ((a, L), (0, a)) if up else ((0, a), (a, L))
+            y1, y2 = targets(u, *c1, own="KP%d" % up), targets(u, *c2, late=True)
             next(lo)
             next(y1)
-            next(lo)
             next(lo)
             next(y1)
             next(y1)
             next(y2)
             next(y1)
+            for q in range(c1[0] // 16, c1[1] // 16):
+                pairs(u, q, 16 * q, c1[1], False, "KP%d" % up, 384 - c1[0])
+            within(c1[0] // 16, c1[1] // 16, False)
             if u:
                 links(u - 1)
-            for q in range(c1[0] // 16, c1[1] // 16):
-                pairs(u, q, 16 * q, c1[1], False, "KP%d" % (u == 0), 384 - c1[0])
             next(y2)
-            next(y2)
-            next(y2)
-            lane_min(u, *mins.pop(u == 0))
-        if a // 16 % 2 and e == 0:
-            succs(u, 0, a)
-            succs(u, a, L)
-        else:
-            succs(u, 0, L)
+            y = y2
         if u == 1:
             ys_out(E0, E0 + LE)
         if e == 2:
             inverse(u - 1, 7, Q9)
-        if u == 5:
-            close_up("S", 2)
-            ys_out(E0 + LE, B + 4 * M)
-            close_up("C", 2)
-            yc_new(2)
-        blocks = range(L // 16 if u else a // 16)
+        if u == 4:
+            ys_out(E0 + LE, B + 2 * M)
+        blocks = range(L // 16 if e or not up else a // 16)
+        for _ in y:
+            pass
+        succs(u, 0, L)
         for q in blocks:
-            pairs(u, q, max(16 * q, a) if u == ST else 16 * q, L, q == blocks[-1])
+            pairs(u, q, 16 * q if up else max(16 * q, a), L, False)
+        within(0 if up else a // 16, blocks[-1] + 1, True)
         for m in mins:
             lane_min(u, *m)
         fk = X("FK", 15, L, 16)
         if e == 0:
             if u:
                 inv_a(Q9)
+                relink(u - 1)
                 inv_b(u - 1, Q9)
             signs(u)
             firsts(u)
             ranks(u)
-            inverse(u, 0, Q9)
+            inverse(u, 0, QS)
+            share = (x for q in range(QS, Q9) for x in inverse_v(u, q))
+            next(share, 0)
             scan(X("RW", 0, L), X("RM", 0, L), X("RS", 0, L), -LOW, Op.max, Op.min)
+            next(share, 0)
             tt(X("TO", 0, L // 16), fk, X("RW", 15, L, 16), Op.max)
+            next(share, 0)
             ts(X("OFY", 0, L // 16), X("TO", 0, L // 16), float(B), Op.add)
-            sub(u)
-            if u:
-                relink(u - 1)
-            inv_a(Q9)
+            for _ in share:
+                pass
+            sub(u, 0, SB[t])
+            inv_a(Q9, t)
             inv_b(u, Q9)
             ts(sf(u + 1), IND(regw("SY", u), X("INV", 16 * u, 16 * u + Q9)), float(-B), Op.add)
-            close_up("C", u)
-            repeat("a", "CP", new("Cw", u), 0, NA[u + 1])
-            repeat("v", "CR", new("Cw", u), NS[u + 1], M)
+            copy("a", X("CC", 0, M), IND(regw("MM", u), X("INV", 16 * u, 16 * u + Q9)))
+            spread(X("CC", 0, M), min(NS[u + 1]), M)
             shuffle(u + 1)
+            spread_t(X("CC", 0, M), range(CPT[0]))
+            repeat("a", "CP", X("CC", 0, M), 0, 128, range(CPT[0], 4))
+            sub(u, SB[t])
             lists(u + 1, 0, 1)
         elif e == 1:
-            repeats("a", reg("MM", u), u + 1)
+            spread(reg("MM", u), min(NS[u + 1]), M)
             ts(sf(u + 1), reg("SY", u), float(-B), Op.add)
             shuffle(u + 1)
             firsts(u)
             signs(u)
+            spread_t(reg("MM", u), range(CPT[1]))
+            repeat("a", "CP", reg("MM", u), 0, 128, range(CPT[1], 4))
             ts(X("OFY", 0, L // 16), fk, float(B), Op.add)
-            sub(u)
             lists(u + 1, 0, 1)
+            sub(u)
         else:
             if u < U - 1:
                 send(X("PM", 0, M), reg("MM", u), "arm")
             inv_a(Q9)
             inv_b(u - 1, Q9)
             firsts(u)
-            signs(u)
             if u == U - 1:
                 close_up("C", u - 1)
+                yc_new(u - 1)
+            signs(u)
             ts(X("OFY", 0, L // 16), fk, float(B), Op.add)
             sub(u)
             ranks(u)
-            if u < U - 1:
-                inverse(u, 0, 3)
-                repeat("v", "CR", ent, NA[u + 1], LE)
     u = U - 1
     dma("y", D("yc", 0, B + 2 * M), X("Cw", 0, B + 2 * M))
     dma("y", D("yc", B + 3 * M, B + 4 * M), new("Cw", 3))
@@ -609,7 +741,9 @@ def rank_program(g, core, T, topo):
     close_up("S", u)
     ys_out(W - 2 * M, W)
     close_up("C", u)
-    dma("a", D("yc", W - 2 * M, W), X("CO", M, 3 * M))
+    yc_new(u, "a")
+    for i in (order() if AUTO else range(len(calls))):
+        issue(i)
     g.wait_ge(T.sem["left"], sent[0])
     for q in cnt:
         g.wait_ge(T.sem[semname(q)], cnt[q] * inc[q])

@@ -13,36 +13,38 @@ RG = 264
 NA = [128, 128, 128, 128, 128, 128]
 O0 = "gfgBBmAfgBmAfgBmAfmA"
 O1 = "gfgBBmAfgBmAfgBmAfmA"
-O3 = "rcigflgfgmAfgmAfmAmAqpBpBpBpB"
+O3 = "ircgBlfgmfBgfmfABgAmBmFbAAqFppPPFFabapPpyPykeeyydedeeezeeeeezeezz"
 ORDER = [O0, O1, O1, O3, O1, O1]
-N4 = [80, 88, 88, 104]
+N4 = [80, 96, 96, 96]
 NS = [[128] * 4, N4, N4, [128] * 4, N4, N4]
 COPIES = [2, 4, 5]
-EARLY = False
+JOINT = False
+INORDER = False
 AUTO = False
 CYC, PE, GATHER, SCATTER, WAKE, WAIT, RATE, NEAR, FAR = 0.85, 0.46, 1.56, 3.3, 165.0, 27.0, 280.0, 1350.0, 3000.0
 FIRST, PASSES, SLACK = False, 2, 20.0
 CPT = [0, 0, 4]
 SPLIT = []
-QS = 7
-SB = [96, 128]
-YAT = 0
+COUNTED = [0, 3, 5]
+QS = [6, 6, 5]
+SB = [0, 0]
+SHORT = 0
 LEAVES = [2, 4, 5]
 
 f32, b16, f16, u16, i32 = "float32", "bfloat16", "float16", "uint16", "int32"
 SCRATCH = {n: ("sbuf", [128, c], d) for n, c, d in [
     ("CI", B + 8, i32), ("SI", B + 8, i32), ("Cw", CW, f32), ("Sw", W + 8, f32), ("CR", 1024, f32), ("MG", 4096, f32),
-    ("GS", 2048, f32),
+    ("GS", 2048, f32), ("GP", 16 * LP, f32),
     ("SF", 256 * U, f16), ("SU", 256 * U, u16), ("MM", RG * U, f32), ("SY", RG * U, f32), ("INV", 16 * U, u16),
-    ("FF0", 128, f32), ("FF1", 128, f32), ("OH0", 128, b16), ("OH1", 128, b16),
+    ("FF0", 128, f32), ("FF1", 128, f32), ("FF2", 128, f32), ("OH2", 128, b16), ("OH0", 128, b16), ("OH1", 128, b16),
     ("OS", 512, b16), ("PT", 256, f16), ("WF", 256, f32), ("YW", 18, u16), ("CY", 256, f32),
     ("FK", 256, f32), ("OFY", 16, u16), ("SG", 256, b16), ("RS", 256, f32), ("RW", 256, f32), ("TO", 16, f32),
     ("ACC", 16, f32), ("JK", 2304, b16), ("IV", 16, f32), ("RKB", 256, b16), ("OV", 256, b16),
     ("CO", 3 * M, f32), ("PORT", LP, f32), ("PM", M + 8, f32), ("PL", 4, u16), ("PO", 4, u16),
-    ("ON", 512, f32), ("RK", 256, f32), ("RB", 256, f32), ("RM", 256, f32), ("DG", 256, f32), ("LM", 256, f32), ("LR", 256, f32),
+    ("ON", 256, f32), ("RK", 256, f32), ("RB", 256, f32), ("RM", 256, f32), ("DG", 256, f32), ("LM", 256, f32), ("LR", 256, f32),
     ("BOX", 128, f32), ("BOF", 128, f32), ("TSF", 128, f32), ("IDW", 160, f32), ("WS", 640, f16),
     ("PI", 2, i32), ("PR", 2, i32), ("PF", 2, f32), ("I4", 4, f32), ("MK4", 4, f32), ("Q16", 16, f32), ("JB", 16, f32),
-    ("CC", M, f32), ("C4", 32, f32), ("CL", 32, u16), ("JT", 16, f32), ("QV", 32, f32), ("JA", 16, f32), ("JV", 256, b16),
+    ("CC", M, f32), ("C4", 32, f32), ("CL", 32, u16), ("JT", 16, f32), ("QV", 48, f32), ("JA", 16, f32),
     ("BG", 8, f32), ("BOH", 128, f16), ("IDB", 128, b16), ("IP", 128, b16), ("IN", 128, b16), ("BN", 128, b16),
     ("BP", 128, b16), ("BH", 128, b16), ("BD", 128, b16), ("TP", 128, b16), ("MY", 256, b16), ("M0", 256, b16), ("MK", 256, b16),
     ("KC", 128, b16), ("ONK", 256, b16), ("C14", 128, b16), ("RH", 256, b16), ("RA", 256, b16), ("CZ", 128 * U, b16)]}
@@ -90,6 +92,8 @@ def rank_program(g, core, T, topo):
                 if name in psum and q2 != q:
                     after.add(i2)
                 elif name in psum and q == "t":
+                    behind.add(i2)
+                elif INORDER and w and q2 == q and sem is None and calls[i2]["sem"] is None:
                     behind.add(i2)
                 elif (w or w2) and c0 < d1 and d0 < c1 and not (st == s2 and st > 1 and c0 % st != d0 % st):
                     after.add(i2)
@@ -290,50 +294,51 @@ def rank_program(g, core, T, topo):
     dma("a", X("SI", E0 + LE, B), D("s0", E0 + LE, B))
     dma("y", X("SI", 0, E0), D("s0", 0, E0))
 
-    fill(X("ON", 0, 512), 1.0)
+    fill(X("ON", 0, 256), 1.0)
     iota(X("PI", 0, 1), [[0, 1]], 0, 1, True)
     iota(X("I4", 0, 4), [[1, 4]], 0, 0)
     aff(X("IDW", 0, 160), X("ON", 0, 160), [[-1, 160]], Op.is_equal, 0.0, 12, 1)
-    aff(mat("BOX"), mat("ON"), [[-16, 8], [0, 16]], Op.is_ge, 0.0, 0, 1)
-    aff(mat("BOF"), mat("BOX"), [[16, 8], [0, 16]], Op.is_ge, 0.0, 15, -1)
     iota(X("LM", 0, 256), [[0, 16], [1, 16]], 0, 0)
-    iota(X("Q16", 0, 16), [[16, 16]], 0, 0)
     iota(X("LR", 0, 256), [[1, 256]], DUMP - B + int(LOW), 0)
-    iota(X("C4", 0, 32), [[4, 32]], 0, 0)
-    aff(mat("TSF"), mat("BOF"), [[1, 128]], Op.is_gt, 0.0, 0, -1)
+    aff(mat("BOX"), mat("ON"), [[-16, 8], [0, 16]], Op.is_ge, 0.0, 0, 1)
+    iota(X("Q16", 0, 16), [[16, 16]], 0, 0)
+    aff(mat("BOF"), mat("BOX"), [[16, 8], [0, 16]], Op.is_ge, 0.0, 15, -1)
     iota(X("KC", 0, 128, p=1), [[0, 8], [-1, 16]], 15, 0)
-    for u in range(U):
-        c = B - 1 + M * u - 8192 + 14 * 4096
-        iota(X("CZ", 128 * u, 128 * u + 128, p=2), [[0, 128]], c - c % 256, c % 256 - (c - c % 256))
+    aff(mat("TSF"), mat("BOF"), [[1, 128]], Op.is_gt, 0.0, 0, -1)
+    iota(X("C4", 0, 32), [[4, 32]], 0, 0)
     ts(X("PR", 0, 1), X("PI", 0, 1), 15, Op.bitwise_and)
-    fill(X("RK", 0, 256), BIG)
-    ts(X("PR", 1, 2), X("PR", 0, 1), 2, Op.arith_shift_right)
-    fill(X("RB", 0, 256), -LOW)
-    copy("v", X("PF", 0, 2), X("PR", 0, 2))
     fill(X("ONK", 0, 256, p=2), 1.0)
-    fill(X("RH", 0, 256, p=1), float(W - B))
+    fill(X("MM", 256, RG * U, RG), 0.0)
+    ts(X("PR", 1, 2), X("PR", 0, 1), 2, Op.arith_shift_right)
+    fill(X("SY", 256, RG * U, RG), 0.0)
+    fill(X("CI", B, B + 8), 0)
+    fill(X("SI", B, B + 8), 0)
+    copy("v", X("PF", 0, 2), X("PR", 0, 2))
+    fill(X("RK", 0, 256), BIG)
     ts(X("MK4", 0, 4), X("I4", 0, 4), X("PF", 1, 2), Op.is_equal)
     fill(X("RK", 0, 128, 16), T16 - 0.5)
     fill(X("RK", 128, 256, 16), T16 - 0.25)
-    fill(X("C14", 0, 128, p=1), 14.0 * 16777216.0)
-    fill(X("RA", 0, 256, p=1), 65536.0)
-    fill(X("MM", 256, RG * U, RG), 0.0)
-    fill(X("SY", 256, RG * U, RG), 0.0)
-    fill(X("PM", M, M + 8), 0.0)
-    fill(X("PO", 0, 4), 0)
-    fill(X("CI", B, B + 8), 0)
-    fill(X("SI", B, B + 8), 0)
     for kq in range(4):
         ts(X("WS", 160 * kq, 160 * kq + 160), X("IDW", 0, 160), X("MK4", kq, kq + 1), Op.mult)
-    zero_a(X("Cw", B, B + 512))
-    zero_a(X("Cw", B + 512, W + 8))
-    zero_a(X("Sw", B, B + 512))
-    zero_a(X("Sw", B + 512, W + 8))
+    ts(X("DG", 0, 256), X("LM", 0, 256), X("PF", 0, 1), Op.is_equal)
+    tt(X("RW", 0, 256), X("DG", 0, 256), X("LR", 0, 256), Op.mult)
+    act(X("RB", 0, 256), X("ON", 0, 256), Act.Copy, scale=-LOW)
+    for name in ("Cw", "Sw"):
+        for c in range(B, W + 8, 256):
+            zero_a(X(name, c, min(c + 256, W + 8)))
     idf = X("IDW", 12, 140)
-    for name, src, s in (("IDB", idf, 1.0), ("BH", mat("BOF"), float(B - W)), ("BN", mat("BOF"), -4096.0),
-                         ("BP", mat("BOF"), 4096.0), ("TP", mat("TSF"), 4096.0), ("IP", idf, 8192.0),
-                         ("IN", idf, -8192.0), ("BD", mat("BOF"), -16777216.0)):
-        act(mat(name), src, Act.Copy, scale=s)
+
+    def scaled(*names):
+        for name in names:
+            src, s = {"IDB": (idf, 1.0), "BH": (mat("BOF"), float(B - W)), "BN": (mat("BOF"), -4096.0), "BP": (mat("BOF"), 4096.0),
+                      "TP": (mat("TSF"), 4096.0), "IP": (idf, 8192.0), "IN": (idf, -8192.0), "BD": (mat("BOF"), -16777216.0)}[name]
+            act(mat(name), src, Act.Copy, scale=s)
+
+    scaled("IDB", "IP", "IN")
+    act(X("M0", 0, 256), X("DG", 0, 256), Act.Identity, bias=4096.0, scale=-4096.0)
+    act(X("MK", 0, 256), X("DG", 0, 256), Act.Identity, bias=8192.0, scale=-4096.0)
+    act(X("MY", 0, 256), X("DG", 0, 256), Act.Identity, bias=4096.0 + W - B, scale=-4096.0)
+
 
     def shuffle(u, kqs=range(4), bank=None):
         n = lanes(u) // 4
@@ -360,42 +365,48 @@ def rank_program(g, core, T, topo):
 
     ts(sf(0), X("SI", E0, E0 + LE), float(-B), Op.add)
     shuffle(0)
-    ts(X("BG", 0, 8), X("BOF", 0, 128, 16), 16.0, Op.mult)
-    ts(X("DG", 0, 256), X("LM", 0, 256), X("PF", 0, 1), Op.is_equal)
-    ts(X("JA", 0, 16), X("Q16", 0, 16), X("PF", 0, 1), Op.add)
-    copy("v", mat("BOH"), mat("BOF"))
-    repeat("v", "CR", X("CI", E0, E0 + LE), 128, LE)
+    repeat("v", "CR", X("CI", E0, E0 + LE), min(NS[0]), LE)
     repeat("v", "CP", X("CI", E0, E0 + LE), 0, 128)
     lists(0, 0, 1)
     lists(0, 1, 4)
-    tt(X("RW", 0, 256), X("DG", 0, 256), X("LR", 0, 256), Op.mult)
-    ts(X("RB", 0, 256, 16), X("JA", 0, 16), float(DUMP - B), Op.add)
-    ts(X("CL", 0, 32), X("C4", 0, 32), X("PF", 1, 2), Op.add)
-    act(X("M0", 0, 256), X("DG", 0, 256), Act.Identity, bias=4096.0, scale=-4096.0)
-    act(X("MK", 0, 256), X("DG", 0, 256), Act.Identity, bias=8192.0, scale=-4096.0)
-    act(X("MY", 0, 256), X("DG", 0, 256), Act.Identity, bias=4096.0 + W - B, scale=-4096.0)
+    act(X("JA", 0, 16), X("Q16", 0, 16), Act.Identity, bias=X("PF", 0, 1))
+    act(X("BG", 0, 8), X("BOF", 0, 128, 16), Act.Copy, scale=16.0)
 
     def late_constants():
+        scaled("BN", "BP", "TP", "BH", "BD")
+        act(X("RB", 0, 256, 16), X("JA", 0, 16), Act.Identity, bias=float(DUMP - B))
         act(X("JB", 0, 16), X("JA", 0, 16), Act.Identity, bias=float(M), scale=-1.0)
         act(X("JT", 0, 16), X("JA", 0, 16), Act.Identity, bias=-8192.0 * M, scale=8192.0)
-        for t in range(RO):
-            copy("a", X("QV", 16 * t, 16 * t + QS), X("Q16", 0, QS))
-            act(X("QV", 16 * t + QS, 16 * t + 16), X("Q16", QS, 16), Act.Identity, bias=float(lanes(ST * t)), scale=0.0)
+        for t, u in enumerate(COUNTED):
+            copy("a", X("QV", 16 * t, 16 * t + QS[t]), X("Q16", 0, QS[t]))
+            act(X("QV", 16 * t + QS[t], 16 * t + 16), X("Q16", QS[t], 16), Act.Identity, bias=float(lanes(u)), scale=0.0)
+        for name, c in (("C14", 14.0 * 16777216.0), ("RH", float(W - B)), ("RA", 65536.0)):
+            n = SCRATCH[name][1][1]
+            act(X(name, 0, n, p=1), X("ON", 0, n, p=1), Act.Copy, scale=c)
+        zero_a(X("PM", M, M + 8))
+        copy("v", mat("BOH"), mat("BOF"))
         act(X("RM", 0, 256), X("RW", 0, 256), Act.Identity, bias=-LOW)
 
     copy_g(X("Cw", 0, B), X("CI", 0, B), B)
+    for u in range(U):
+        c = B - 1 + M * u - 8192 + 14 * 4096
+        iota(X("CZ", 128 * u, 128 * u + 128, p=2), [[0, 128]], c - c % 256, c % 256 - (c - c % 256))
     copy_g(X("Sw", E0, B), X("SI", E0, B), B - E0)
     copy_g(X("Sw", 0, E0), X("SI", 0, E0), E0)
 
+    def chunk(u, ch):
+        return ((0, NA[u]), (NA[u], min(lanes(u), LE)), (LE, lanes(u)))[ch]
+
     def opens(u):
         L, a = lanes(u), NA[u]
-        for ch, (l0, n) in enumerate(((0, a), (a, L - a))):
+        for ch in range(2):
+            l0, n = chunk(u, ch)[0], chunk(u, ch)[1] - chunk(u, ch)[0]
             kp = X("KP%d" % ch, 0, 128, p=n)
             if u % ST == 2:
                 mm(kp, X("ONK", 0, n, p=1), X("C14", 0, 128, p=1), True, False)
                 mm(kp, X("SG", l0, l0 + n), mat("BD"), False, False)
             mm(kp, X("ONK", 0, n, p=1), X("KC", 0, 128, p=1), u % ST != 2, False)
-        l0, l1 = (0, L) if u % ST else (0, a) if u and not EARLY else (a, L)
+        l0, l1 = (0, min(L, LE)) if u or JOINT else (a, L)
         mm(X("YD", l0, l1), mat("IDB"), X("MY" if u in COPIES else "M0", l0, l1), True, False)
         if u in COPIES:
             mm(X("YB", l0, l1), X("ONK", 0, 128, p=1), X("RH", 0, l1 - l0, p=1), True, False)
@@ -426,10 +437,10 @@ def rank_program(g, core, T, topo):
             tt(mg(kq, 0, s), X("GS", 512 * kq, 512 * kq + 4 * s), X("CP", 0, 4 * s), Op.min)
 
     def keys(u, ch, kq):
-        l0, n = (0, NA[u]) if ch == 0 else (NA[u], lanes(u) - NA[u])
+        l0, l1 = chunk(u, ch)
         for i in range(4):
-            a = 1024 * kq + 4 * l0
-            mm(X("KP%d" % ch, 4 * kq + i, 128, 16, p=n), X("MG", a + i, a + 4 * n, 4), X("BG", 0, 8), False, 4 * kq + i == 15)
+            mm(X(("KP0", "KP1", "CP")[ch], 4 * kq + i, 128, 16, p=l1 - l0), X("MG", 1024 * kq + 4 * l0 + i, 1024 * kq + 4 * l1, 4),
+               X("BG", 0, 8), False, 4 * kq + i == 15)
 
     def yw(u, l0, l1):
         q0 = l0 // 16 + l0 // 16 % 2
@@ -439,8 +450,8 @@ def rank_program(g, core, T, topo):
         return X("OS", 256 * (u % 2) + l0, 256 * (u % 2) + (lanes(u) if l1 is None else l1))
 
     def best(u, ch):
-        kp, ff, oh = ["%s%d" % (b, ch) for b in ("KP", "FF", "OH")]
-        l0, l1 = (0, NA[u]) if ch == 0 else (NA[u], lanes(u))
+        kp, ff, oh = ("KP0", "KP1", "CP")[ch], "FF%d" % ch, "OH%d" % ch
+        l0, l1 = chunk(u, ch)
         n = l1 - l0
         scan(X(ff, 0, 128, p=n), X("RK", 0, 128, p=n), X(kp, 0, 128, p=n), T16 - 0.5, Op.min, Op.max)
         scan(REV(kp, n, 128), X("RK", 128, 256, p=n), REV(kp, n), T16 - 0.25, Op.min, Op.max)
@@ -450,17 +461,17 @@ def rank_program(g, core, T, topo):
         mm(X("O2", l0, l1), X(oh, 0, 128, p=n), X("IDB", 0, n, p=n), True, True)
         yield
 
-    def targets(u, l0, l1, own=None, late=False):
+    def targets(u, l0, l1, own=None, late=False, both=False):
         n = l1 - l0
         os = chosen(u, l0, l1)
         copy("a", os, X("O2", l0, l1))
         if late:
             mm(X("YD", l0, l1), mat("IDB"), X("M0", l0, l1), True, False)
         tt(X("PT", l0, l1), sf(u, l0, l1), X("OT", l0, l1), Op.mult)
-        for o in [X("YD", l0, l1)] + ([X(own, 384, 384 + n)] if own else []) + [X("YB", l0, l1)]:
+        for o in [X("YD", l0, l1)] + ([X(own, 384, 384 + n)] if own else []) + [X("YB", l0, l1)] * (both or not own):
+            mm(o, mat("BOH"), X("PT", l0, l1), o[0] != "YD" and u not in COPIES, u not in COPIES)
             if u in COPIES:
-                mm(o, mat("BH"), os, False, False)
-            mm(o, mat("BOH"), X("PT", l0, l1), o[0] != "YD" and u not in COPIES, True)
+                mm(o, mat("BH"), os, False, True)
         mm(X("KL", l0, l1), mat("BOH"), X("PT", l0, l1), False, False)
         mm(X("KL", l0, l1), mat("BN"), os, False, False)
         yield
@@ -479,13 +490,15 @@ def rank_program(g, core, T, topo):
         ts(eq(q, c0 - d, c1 - d), X(yb, o + c0, o + c1), X("WF", d + 15, d + 16), Op.is_equal)
         c0 = max(c0, d + 16)
         if c0 < c1:
-            mm(X("KL", c0, c1), mat("BP"), eq(q, c0 - d, c1 - d), False, last)
+            mm(X("KL", c0, c1), mat("BP"), eq(q, c0 - d, c1 - d), False, False)
 
     def eq(q, c0, c1):
         return ("EQ", 256 * q + c0, 256 * q + c1, 1, T["EQ"][:, q, c0:c1], None)
 
     def within(q0, q1, last):
-        mm(X("KL", 16 * q0, 16 * q1), mat("TP"), ("EQ", 256 * q0, 256 * q1 - 240, 1, T["EQ"][:, q0:q1, 0:16], None), False, last)
+        out = X("KL", 16 * q0, 16 * q1)
+        emit("t", lambda: g.tensor.matmul(out[4], T["TP"][:, :], T["EQ"][:, q0:q1, 0:16], False, last), [out],
+             [mat("TP")] + [eq(q, 0, 16) for q in range(q0, q1)], ns=60)
 
     def lane_min(u, l0, l1, c):
         tt(reg("MM", u, l0, l1), X("CY", l0, l1), X(c, 4 * l0, 4 * l1, 4), Op.min)
@@ -512,16 +525,18 @@ def rank_program(g, core, T, topo):
 
     def inverse(u, q0, q1):
         L = lanes(u)
-        for q in range(q0, q1):
-            act(X("JK", 256 * q, 256 * q + L - 16 * q), X("RS", 16 * q, L), Act.Sign, bias=X("JB", q, q + 1),
+        for q in (range(q1 - 1, q0 - 1, -1) if u in COUNTED else range(q0, q1)):
+            p0 = 0 if u in COUNTED and q < 2 else 16 * q
+            act(X("JK", 256 * q, 256 * q + L - p0), X("RS", p0, L), Act.Sign, bias=X("JB", q, q + 1),
                 scale=1.0 / 8192.0, acc=X("ACC", q, q + 1))
 
     def inverse_v(u, q):
         L = lanes(u)
-        ts(X("JV", 16 * q, L), X("RS", 16 * q, L), X("JT", q, q + 1), Op.is_gt, 2.0, Op.mult)
+        jv = X("JK", 256 * q, 256 * q + L - 16 * q)
+        ts(jv, X("RS", 16 * q, L), X("JT", q, q + 1), Op.is_gt, 2.0, Op.mult)
         yield
-        emit("v", lambda: g.vector.tensor_reduce(T["ACC"][:, q:q + 1], T["JV"][:, 16 * q:L], AxisListType.X, Op.add),
-             [X("ACC", q, q + 1)], [X("JV", 16 * q, L)], ns=CYC * (L - 16 * q))
+        emit("v", lambda: g.vector.tensor_reduce(T["ACC"][:, q:q + 1], jv[4], AxisListType.X, Op.add),
+             [X("ACC", q, q + 1)], [jv], ns=CYC * (L - 16 * q))
         yield
 
     def inv_a(q1, t=None):
@@ -568,7 +583,9 @@ def rank_program(g, core, T, topo):
     for u in range(U):
         t, e = divmod(u, ST)
         L, a, s = lanes(u), NA[u], NS[u]
-        nxt = {c: 0 for c in "fgmpABirlcq"}
+        nxt = {c: 0 for c in "fFgmpABPirlcqabdyzenk"}
+        stages = {"a": best(u, 0), "b": best(u, 1), "d": best(u, 2), "y": targets(u, 0, LE),
+                  "z": targets(u, LE, L, own="KP1", late=True)}
         for c in ORDER[u]:
             kq = nxt[c]
             nxt[c] += 1
@@ -582,10 +599,26 @@ def rank_program(g, core, T, topo):
                 gather(u, kq, s[kq], LE if u == ST else L)
             elif c == "m":
                 smaller(u, kq)
+            elif c == "F":
+                copy("a", X("GP", 4 * LP * kq, 4 * LP * (kq + 1)), counts(u, kq, LE, L))
             elif c == "p":
-                gather(u, kq, LE, L)
-            elif c in "AB":
-                keys(u, "AB".index(c), kq)
+                tt(mg(kq, LE, L), X("GP", 4 * LP * kq, 4 * LP * (kq + 1)), X("YB", 256, 256 + 4 * LP), Op.min)
+            elif c in "ABP":
+                if c == "P" and kq == 0:
+                    mm(X("CP", 0, 128, p=LP), X("ONK", 0, LP, p=1), X("KC", 0, 128, p=1), True, False)
+                keys(u, "ABP".index(c), kq)
+            elif c in stages:
+                next(stages[c])
+                if c == "y" and kq == 3:
+                    succs(u, 0, LE)
+            elif c == "e":
+                pairs(u, kq, 16 * kq, LE, False)
+                if kq == LE // 16 - 1:
+                    within(0, LE // 16, False)
+            elif c == "k":
+                small_ranks(u - 1)
+                inverse(u - 1, 3, Q9)
+                links(u - 1)
             elif c == "i":
                 inverse(u - 1, 0, 3)
             elif c == "r":
@@ -599,13 +632,8 @@ def rank_program(g, core, T, topo):
                 repeat("a", "CP", ent, 0, 128, range(CPT[2], 4))
             else:
                 copy("a", X("PORT", 0, LP), IND(X("PM", 0, M + 1), X("PL", 0, 3)))
-                spread(("PORT", -LE), LE, L)
-        if u == ST:
-            small_ranks(u - 1)
-            inverse(u - 1, 3, Q9)
-            close_up("C", 1)
-        up = u != ST or EARLY
-        hi, lo = best(u, int(up)), best(u, int(not up))
+                repeat("a", "YB", ("PORT", -64), 64, 64 + LP)
+        hi, lo = best(u, 1), best(u, 0)
         if e == 1:
             small_ranks(u - 1)
             close_up("S", u - 1)
@@ -615,22 +643,24 @@ def rank_program(g, core, T, topo):
             inverse(u - 1, 0, 3)
         if u == 0:
             late_constants()
-            ts(sf(ST), X("SI", E0 + LE, B), float(-B), Op.add)
         mins = [(0, a, "CP"), (a, L, "CR")]
-        next(hi)
-        next(hi)
-        if e:
-            links(u - 1)
+        if u != ST:
+            next(hi)
+            next(hi)
+        if e or JOINT and u == 0:
+            if u:
+                links(u - 1)
             for _ in lo:
                 pass
-            if u < ST:
+            if 0 < u < ST:
                 shuffle(ST, (2 * u - 2, 2 * u - 1), "KP0")
             y = targets(u, 0, L)
-            relink(u - 1)
+            if u:
+                relink(u - 1)
             next(y)
             if e == 2:
                 inverse(u - 1, 3, 7)
-            if u < ST:
+            if 0 < u < ST:
                 lists(ST, 2 * u - 2, 2 * u, "KP0")
             if e == 1:
                 copy("a", new("Cw", u - 1), X("CC", 0, M))
@@ -642,9 +672,9 @@ def rank_program(g, core, T, topo):
             if u == 5:
                 ys_out(B + 2 * M, B + 4 * M)
             next(y)
-        else:
-            c1, c2 = ((a, L), (0, a)) if up else ((0, a), (a, L))
-            y1, y2 = targets(u, *c1, own="KP%d" % up), targets(u, *c2, late=True)
+        elif u == 0:
+            c1, c2 = (a, L), (0, a)
+            y1, y2 = targets(u, *c1, own="KP1", both=True), targets(u, *c2, late=True)
             next(lo)
             next(y1)
             next(lo)
@@ -653,10 +683,8 @@ def rank_program(g, core, T, topo):
             next(y2)
             next(y1)
             for q in range(c1[0] // 16, c1[1] // 16):
-                pairs(u, q, 16 * q, c1[1], False, "KP%d" % up, 384 - c1[0])
+                pairs(u, q, 16 * q, c1[1], False, "KP1", 384 - c1[0])
             within(c1[0] // 16, c1[1] // 16, False)
-            if u:
-                links(u - 1)
             next(y2)
             y = y2
         if u == 1:
@@ -665,37 +693,56 @@ def rank_program(g, core, T, topo):
             inverse(u - 1, 7, Q9)
         if u == 4:
             ys_out(E0 + LE, B + 2 * M)
-        blocks = range(L // 16 if e or not up else a // 16)
-        for _ in y:
-            pass
-        succs(u, 0, L)
-        for q in blocks:
-            pairs(u, q, 16 * q if up else max(16 * q, a), L, False)
-        within(0 if up else a // 16, blocks[-1] + 1, True)
-        for m in mins:
-            lane_min(u, *m)
+        if u == ST:
+            succs(u, LE, L)
+            close_up("C", 1)
+            for q in range(L // 16):
+                pairs(u, q, max(16 * q, LE), L, False, "KP1", 384 - LE)
+            within(LE // 16, L // 16, True)
+            tt(reg("MM", u, 0, LE), X("CY", 0, LE), X("Cw", E0 + LE, E0 + 2 * LE), Op.min)
+            tt(reg("MM", u, LE, L), X("CY", LE, L), X("PORT", 0, LP), Op.min)
+        else:
+            blocks = range(L // 16 if e or JOINT else a // 16)
+            for q in blocks:
+                if q == (e == 2):
+                    for _ in y:
+                        pass
+                    succs(u, 0, L)
+                pairs(u, q, 16 * q, L, False)
+            within(0, blocks[-1] + 1, True)
+            for m in mins:
+                lane_min(u, *m)
         fk = X("FK", 15, L, 16)
         if e == 0:
             if u:
                 inv_a(Q9)
-                relink(u - 1)
-                inv_b(u - 1, Q9)
+            else:
+                ts(X("CL", 0, 32), X("C4", 0, 32), X("PF", 1, 2), Op.add)
+                fill(X("PO", 0, 4), 0)
+                ts(sf(ST), X("SI", E0 + LE, B), float(-B), Op.add)
             signs(u)
+            if u:
+                inv_b(u - 1, Q9)
             firsts(u)
             ranks(u)
-            inverse(u, 0, QS)
-            share = (x for q in range(QS, Q9) for x in inverse_v(u, q))
-            next(share, 0)
+            if u:
+                relink(u - 1)
+            inverse(u, 0, QS[t])
+            share = [inverse_v(u, q) for q in range(QS[t], Q9)]
+            for x in share:
+                next(x)
             scan(X("RW", 0, L), X("RM", 0, L), X("RS", 0, L), -LOW, Op.max, Op.min)
-            next(share, 0)
+            for x in share:
+                next(x)
             tt(X("TO", 0, L // 16), fk, X("RW", 15, L, 16), Op.max)
-            next(share, 0)
-            ts(X("OFY", 0, L // 16), X("TO", 0, L // 16), float(B), Op.add)
-            for _ in share:
-                pass
+            if SB[t]:
+                ts(X("OFY", 0, L // 16), X("TO", 0, L // 16), float(B), Op.add)
+            tt(X("IV", 2, Q9), X("ACC", 2, Q9), X("QV", 16 * t + 2, 16 * t + Q9), Op.subtract)
+            if not SB[t]:
+                ts(X("OFY", 0, L // 16), X("TO", 0, L // 16), float(B), Op.add)
             sub(u, 0, SB[t])
-            inv_a(Q9, t)
-            inv_b(u, Q9)
+            ts(X("INV", 16 * u + 2, 16 * u + Q9), X("IV", 2, Q9), -0.5, Op.mult, L / 2.0, Op.add)
+            ts(X("INV", 16 * u, 16 * u + 2), X("ACC", 0, 2), -0.5, Op.mult, L / 2.0, Op.add)
             ts(sf(u + 1), IND(regw("SY", u), X("INV", 16 * u, 16 * u + Q9)), float(-B), Op.add)
             copy("a", X("CC", 0, M), IND(regw("MM", u), X("INV", 16 * u, 16 * u + Q9)))
             spread(X("CC", 0, M), min(NS[u + 1]), M)
@@ -719,12 +766,12 @@ def rank_program(g, core, T, topo):
             if u < U - 1:
                 send(X("PM", 0, M), reg("MM", u), "arm")
             inv_a(Q9)
-            inv_b(u - 1, Q9)
             firsts(u)
+            inv_b(u - 1, Q9)
+            signs(u)
             if u == U - 1:
                 close_up("C", u - 1)
                 yc_new(u - 1)
-            signs(u)
             ts(X("OFY", 0, L // 16), fk, float(B), Op.add)
             sub(u)
             ranks(u)
@@ -733,12 +780,17 @@ def rank_program(g, core, T, topo):
     dma("y", D("yc", B + 3 * M, B + 4 * M), new("Cw", 3))
     small_ranks(u)
     links(u)
-    inverse(u, 0, Q9)
+    inverse(u, 0, QS[2])
+    share = [inverse_v(u, q) for q in range(QS[2], Q9)]
+    for _ in range(2):
+        for x in share:
+            next(x)
     relink(u)
-    inv_a(Q9)
-    inv_b(u, Q9)
-    close_up("S", u - 1)
-    close_up("S", u)
+    tt(X("IV", 2, Q9), X("ACC", 2, Q9), X("QV", 32 + 2, 32 + Q9), Op.subtract)
+    copy("v", new("Sw", u - 1), IND(regw("SY", u - 1), X("INV", 16 * (u - 1), 16 * (u - 1) + Q9)))
+    ts(X("INV", 16 * u + 2, 16 * u + Q9), X("IV", 2, Q9), -0.5, Op.mult, M / 2.0, Op.add)
+    ts(X("INV", 16 * u, 16 * u + 2), X("ACC", 0, 2), -0.5, Op.mult, M / 2.0, Op.add)
+    copy("v", new("Sw", u), IND(regw("SY", u), X("INV", 16 * u, 16 * u + Q9)))
     ys_out(W - 2 * M, W)
     close_up("C", u)
     yc_new(u, "a")

from concourse.mybir import dt, AluOpType, AxisListType, ActivationFunctionType

B, LE, LP, M, ST, RO, TH = 1920, 208, 48, 144, 3, 2, 49152
U = RO * ST
E0 = B - RO * LE - LP
W = B + U * M
DUMP = W + 8
CW = DUMP + 256
T16 = float(16 * TH)
BIG = 33554432.0
LOW = 2097152.0
RG = 264
NA = [128, 128, 128, 128, 128, 128]
O0 = "gfgBBmAfgBmAfgBmAfmA"
O1 = "gfgBBmAfgBmAfgBmAfmA"
O3 = "ircgBlfgmfBgfmfABgAmBmFbAAqFppPPFFabapPpyPykeeyydedeeezeeeeezeezz"
ORDER = [O0, O1, O1, O3, O1, O1]
N4 = [80, 96, 96, 96]
NS = [[128] * 4, N4, N4, [128] * 4, N4, N4]
COPIES = [2, 4, 5]
JOINT = False
INORDER = False
AUTO = False
CYC, PE, GATHER, SCATTER, WAKE, WAIT, RATE, NEAR, FAR = 0.85, 0.46, 1.56, 3.3, 165.0, 27.0, 280.0, 1350.0, 3000.0
FIRST, PASSES, SLACK = False, 2, 20.0
CPT = [0, 0, 4]
SPLIT = []
COUNTED = [0, 3, 5]
QS = [6, 6, 5]
SB = [0, 0]
SHORT = 0
LEAVES = [2, 4, 5]

f32, b16, f16, u16, i32 = "float32", "bfloat16", "float16", "uint16", "int32"
SCRATCH = {n: ("sbuf", [128, c], d) for n, c, d in [
    ("CI", B + 8, i32), ("SI", B + 8, i32), ("Cw", CW, f32), ("Sw", W + 8, f32), ("CR", 1024, f32), ("MG", 4096, f32),
    ("GS", 2048, f32), ("GP", 16 * LP, f32),
    ("SF", 256 * U, f16), ("SU", 256 * U, u16), ("MM", RG * U, f32), ("SY", RG * U, f32), ("INV", 16 * U, u16),
    ("FF0", 128, f32), ("FF1", 128, f32), ("FF2", 128, f32), ("OH2", 128, b16), ("OH0", 128, b16), ("OH1", 128, b16),
    ("OS", 512, b16), ("PT", 256, f16), ("WF", 256, f32), ("YW", 18, u16), ("CY", 256, f32),
    ("FK", 256, f32), ("OFY", 16, u16), ("SG", 256, b16), ("RS", 256, f32), ("RW", 256, f32), ("TO", 16, f32),
    ("ACC", 16, f32), ("JK", 2304, b16), ("IV", 16, f32), ("RKB", 256, b16), ("OV", 256, b16),
    ("CO", 3 * M, f32), ("PORT", LP, f32), ("PM", M + 8, f32), ("PL", 4, u16), ("PO", 4, u16),
    ("ON", 256, f32), ("RK", 256, f32), ("RB", 256, f32), ("RM", 256, f32), ("DG", 256, f32), ("LM", 256, f32), ("LR", 256, f32),
    ("BOX", 128, f32), ("BOF", 128, f32), ("TSF", 128, f32), ("IDW", 160, f32), ("WS", 640, f16),
    ("PI", 2, i32), ("PR", 2, i32), ("PF", 2, f32), ("I4", 4, f32), ("MK4", 4, f32), ("Q16", 16, f32), ("JB", 16, f32),
    ("CC", M, f32), ("C4", 32, f32), ("CL", 32, u16), ("JT", 16, f32), ("QV", 48, f32), ("JA", 16, f32),
    ("BG", 8, f32), ("BOH", 128, f16), ("IDB", 128, b16), ("IP", 128, b16), ("IN", 128, b16), ("BN", 128, b16),
    ("BP", 128, b16), ("BH", 128, b16), ("BD", 128, b16), ("TP", 128, b16), ("MY", 256, b16), ("M0", 256, b16), ("MK", 256, b16),
    ("KC", 128, b16), ("ONK", 256, b16), ("C14", 128, b16), ("RH", 256, b16), ("RA", 256, b16), ("CZ", 128 * U, b16)]}
for _n in ("KP0", "KP1", "OT", "O2", "YD", "YB", "KL", "CP"):
    SCRATCH[_n] = ("psum", [128, 512], f32)
SCRATCH["EQ"] = ("sbuf", [128, 16, 256], b16)
NDMA = 24
SEMAPHORES = ["qv", "qt", "qa", "qg", "arm", "arl", "left"] + ["d%d" % i for i in range(NDMA)]


def rank_program(g, core, T, topo):
    rank = T.rank_of(core)
    if rank is None:
        return
    Op, Act = AluOpType, ActivationFunctionType
    eng = {"v": g.vector, "t": g.tensor, "a": g.scalar, "g": g, "y": g.sync}
    cnt, known, clock, hist, inc = {}, {q: {} for q in eng}, {}, {}, {}
    psum = {n for n in SCRATCH if SCRATCH[n][0] == "psum"}

    def X(name, c0, c1, step=1, p=128):
        ap = T[name][0:p, c0:c1] if step == 1 else T[name][0:p, c0:c1:step]
        return (name, c0, c1, step, ap, None)

    def REV(name, p, c0=0):
        return (name, c0, c0 + 128, 1, T[name][0:p, c0 + 127:c0 - 1:-1] if c0 else T[name][0:p, 127::-1], None)

    def IND(x, off):
        return (x[0], x[1], x[2], 1, x[4].indirect(off[4]), off)

    def semname(q):
        return {"v": "qv", "t": "qt", "a": "qa", "g": "qg"}.get(q, q)

    calls, seen = [], {}

    def size(x):
        return 16 * size(x[5]) if x[5] is not None else -(-(x[2] - x[1]) // x[3])

    def emit(q, call, outs, ins, sem=None, n=1, remote=False, ns=None):
        acc = [(o, True) for o in outs] + [(i, False) for i in ins]
        acc += [(o[5], False) for o in list(outs) + list(ins) if o[5] is not None]
        after, behind = set(), set()
        for (o, w) in acc:
            name, c0, c1, st = o[0:4]
            for (i2, q2, d0, d1, s2, w2) in seen.get(name, []):
                if name in psum and q2 != q:
                    after.add(i2)
                elif name in psum and q == "t":
                    behind.add(i2)
                elif INORDER and w and q2 == q and sem is None and calls[i2]["sem"] is None:
                    behind.add(i2)
                elif (w or w2) and c0 < d1 and d0 < c1 and not (st == s2 and st > 1 and c0 % st != d0 % st):
                    after.add(i2)
        for (o, w) in acc:
            seen.setdefault(o[0], []).append((len(calls), q, o[1], o[2], o[3], w))
        if ns is None:
            k = size(outs[0])
            if outs[0][5] is not None:
                ns = 50 + SCATTER * CYC * k
            elif ins and ins[0][5] is not None:
                ns = (50 if q == "v" else 65) + GATHER * CYC * k
            else:
                ns = CYC * max(64, k)
        calls.append(dict(q=q, call=call, sem=sem, n=n, remote=remote, after=after, behind=behind, ns=ns,
                          bytes=512 * size(outs[0]) if sem else 0))

    def order():
        nc = len(calls)
        takes = [c["ns"] + (c["bytes"] / RATE + (FAR if c["remote"] else NEAR) if c["sem"] else 0) for c in calls]
        chain = takes[:]
        users = [[] for _ in calls]
        for i in range(nc - 1, -1, -1):
            for j in calls[i]["after"]:
                chain[j] = max(chain[j], takes[j] + WAKE + chain[i])
                users[j].append(i)
            for j in calls[i]["behind"] - calls[i]["after"]:
                chain[j] = max(chain[j], takes[j] + chain[i])
                users[j].append(i)
        holds = [c["ns"] + WAIT * bool(c["after"]) for c in calls]
        before = [[(j, WAKE) for j in c["after"]] + [(j, 0.0) for j in c["behind"] - c["after"]] for c in calls]
        later = [[] for _ in calls]
        for i in range(nc):
            for j, w in before[i]:
                later[j].append((i, w))

        def place(rank, edges, back):
            busy = {q: [] for q in list(eng) + ["pipe"]}
            t0, t1 = {}, {}

            def gap(q, t, d):
                for k, (a, b) in enumerate(busy[q]):
                    if t + d <= a + SLACK and t <= a:
                        busy[q].insert(k, (t, t + d))
                        return t
                    t = max(t, b)
                busy[q].append((t, t + d))
                return t
            for i in rank:
                c = calls[i]
                t = max([t1[j] + w for j, w in edges[i]] + [0.0])
                lag = (FAR if c["remote"] else NEAR) if c["sem"] else 0.0
                if back:
                    if c["sem"] and not c["remote"]:
                        t = gap("pipe", t, c["bytes"] / RATE) + c["bytes"] / RATE
                    t0[i] = gap(c["q"], t + lag, holds[i])
                    t1[i] = t0[i] + holds[i]
                else:
                    t0[i] = gap(c["q"], t, holds[i])
                    t1[i] = t0[i] + holds[i] + lag
                    if c["sem"] and not c["remote"]:
                        t1[i] = gap("pipe", t1[i], c["bytes"] / RATE) + c["bytes"] / RATE
            return t0, t1

        rank = sorted(range(nc), key=lambda i: (-chain[i], i)) if FIRST else list(range(nc))
        best_end, best_rank = None, None
        for _ in range(PASSES):
            t0, t1 = place(rank, before, False)
            rank = sorted(range(nc), key=lambda i: (t0[i], i))
            if best_end is None or max(t1.values()) < best_end:
                best_end, best_rank = max(t1.values()), rank
            t0, t1 = place(sorted(range(nc), key=lambda i: (-t1[i], -i)), later, True)
            rank = sorted(range(nc), key=lambda i: (-t1[i], i))
        return best_rank

    def issue(i):
        q, call, sem, n, remote = [calls[i][k] for k in ("q", "call", "sem", "n", "remote")]
        need = {}
        for j in calls[i]["after"]:
            q2, n2 = calls[j]["mark"]
            need[q2] = max(need.get(q2, 0), n2)
        kn = known[q]
        todo = [(q2, n2) for q2, n2 in need.items() if kn.get(q2, 0) < n2]
        todo = [(q2, n2) for q2, n2 in todo
                if not any((q3, n3) != (q2, n2) and clock[(q3, n3)].get(q2, 0) >= n2 for q3, n3 in todo)]
        for q2, n2 in todo:
            eng[q].wait_ge(T.sem[semname(q2)], n2 * inc[q2])
            for k, v in clock[(q2, n2)].items():
                kn[k] = max(kn.get(k, 0), v)
        me = q if sem is None else sem
        cnt[me] = cnt.get(me, 0) + 1
        inc[me] = n
        c = dict(kn)
        c[me] = cnt[me]
        clock[(me, cnt[me])] = c
        calls[i]["mark"] = (me, cnt[me])
        inst = call()
        if not remote:
            inst.then_inc(T.sem[semname(me)], n)

    def act(out, in_, func, bias=None, scale=None, acc=None):
        kw, ins, outs = {}, [in_], [out]
        if bias is not None:
            kw["bias"] = bias[4] if isinstance(bias, tuple) else bias
            ins += [bias] if isinstance(bias, tuple) else []
        if scale is not None:
            kw["scale"] = scale
        if acc is not None:
            kw["accum_out"] = acc[4]
            outs.append(acc)
        emit("a", lambda: g.scalar.activation(out[4], in_[4], func, **kw), outs, ins)

    def copy(q, out, in_):
        if q == "v":
            emit("v", lambda: g.vector.tensor_copy(out[4], in_[4]), [out], [in_])
        else:
            act(out, in_, Act.Copy)

    def tt(out, a, b, op):
        slow = out[5] is None and a[5] is None and a[0] not in psum and b[0] not in psum
        emit("v", lambda: g.vector.tensor_tensor(out[4], a[4], b[4], op), [out], [a, b],
             ns=CYC * max(64, 2 * size(out)) if slow else None)

    def ts(out, a, s1, op0, s2=None, op1=None):
        col = isinstance(s1, tuple)
        k = s1[4] if col else s1
        ins = [a, s1] if col else [a]
        if op1 is None:
            emit("v", lambda: g.vector.tensor_scalar(out[4], a[4], k, None, op0), [out], ins)
        else:
            emit("v", lambda: g.vector.tensor_scalar(out[4], a[4], k, s2, op0, op1), [out], ins)

    def scan(out, d0, d1, init, op0, op1):
        emit("v", lambda: g.vector.tensor_tensor_scan(out[4], d0[4], d1[4], init, op0, op1), [out], [d0, d1])

    def fill(out, c):
        emit("v", lambda: g.vector.memset(out[4], c), [out], [])

    def zero_a(out):
        act(out, X("ON", 0, out[2] - out[1]), Act.Copy, scale=0.0)

    def mm(out, lhsT, rhs, start, stop):
        emit("t", lambda: g.tensor.matmul(out[4], lhsT[4], rhs[4], start, stop), [out], [lhsT, rhs],
             ns=PE * max(min(64, size(lhsT)), size(rhs)) * (4 if SCRATCH[rhs[0]][2] == f32 else 1))

    def aff(out, in_, pattern, op, f, base, cm):
        emit("g", lambda: g.affine_select(out[4], in_[4], pattern, op, f, base, cm), [out], [in_], ns=170 + 2 * CYC * size(out))

    def copy_g(out, in_, n):
        aff(out, in_, [[0, n]], Op.is_gt, 0.0, 1, 0)

    def iota(out, pattern, base, cm, whole=False):
        if whole:
            emit("g", lambda: g.iota(out[4], pattern, base, cm), [out], [], ns=130 + 2 * CYC * size(out))
        else:
            emit("g", lambda: g.iota(out[4], pattern, base, cm, allow_small_or_imprecise_dtypes=True), [out], [],
                 ns=130 + 2 * CYC * size(out))

    ndma = [0]

    def dma(q, out, in_):
        s = "d%d" % ndma[0]
        ndma[0] += 1
        emit(q, lambda: eng[q].dma_start(out[4], in_[4]), [out], [in_], sem=s, n=16, ns=60)

    def D(name, c0, c1):
        return (name, c0, c1, 1, T[name][:, c0:c1], None)

    def mat(name):
        return X(name, 0, 128)

    def lanes(u):
        return M if u % ST else (LE + LP if u else LE)

    def reg(name, u, l0=0, l1=None):
        a = RG * u + 256 - lanes(u)
        return X(name, a + l0, a + (lanes(u) if l1 is None else l1))

    def regw(name, u):
        return reg(name, u, 0, lanes(u) + 1)

    def sf(u, l0=0, l1=None, step=1):
        return X("SF", 256 * u + l0, 256 * u + (lanes(u) if l1 is None else l1), step)

    def new(name, u):
        if name == "Cw" and u in LEAVES:
            return X("CO", M * LEAVES.index(u), M * LEAVES.index(u) + M)
        return X(name, B + M * u, B + M * (u + 1))

    def yc_new(u, q="y"):
        dma(q, D("yc", B + M * u, B + M * (u + 1)), new("Cw", u))

    def ys_out(c0, c1, q="y"):
        dma(q, D("ys", c0 - E0, c1 - E0), X("Sw", c0, c1))

    dma("y", X("SI", E0, E0 + LE), D("s0", E0, E0 + LE))
    dma("a", X("CI", E0, B), D("c0", E0, B))
    dma("y", X("CI", 0, E0), D("c0", 0, E0))
    dma("a", X("SI", E0 + LE, B), D("s0", E0 + LE, B))
    dma("y", X("SI", 0, E0), D("s0", 0, E0))

    fill(X("ON", 0, 256), 1.0)
    iota(X("PI", 0, 1), [[0, 1]], 0, 1, True)
    iota(X("I4", 0, 4), [[1, 4]], 0, 0)
    aff(X("IDW", 0, 160), X("ON", 0, 160), [[-1, 160]], Op.is_equal, 0.0, 12, 1)
    iota(X("LM", 0, 256), [[0, 16], [1, 16]], 0, 0)
    iota(X("LR", 0, 256), [[1, 256]], DUMP - B + int(LOW), 0)
    aff(mat("BOX"), mat("ON"), [[-16, 8], [0, 16]], Op.is_ge, 0.0, 0, 1)
    iota(X("Q16", 0, 16), [[16, 16]], 0, 0)
    aff(mat("BOF"), mat("BOX"), [[16, 8], [0, 16]], Op.is_ge, 0.0, 15, -1)
    iota(X("KC", 0, 128, p=1), [[0, 8], [-1, 16]], 15, 0)
    aff(mat("TSF"), mat("BOF"), [[1, 128]], Op.is_gt, 0.0, 0, -1)
    iota(X("C4", 0, 32), [[4, 32]], 0, 0)
    ts(X("PR", 0, 1), X("PI", 0, 1), 15, Op.bitwise_and)
    fill(X("ONK", 0, 256, p=2), 1.0)
    fill(X("MM", 256, RG * U, RG), 0.0)
    ts(X("PR", 1, 2), X("PR", 0, 1), 2, Op.arith_shift_right)
    fill(X("SY", 256, RG * U, RG), 0.0)
    fill(X("CI", B, B + 8), 0)
    fill(X("SI", B, B + 8), 0)
    copy("v", X("PF", 0, 2), X("PR", 0, 2))
    fill(X("RK", 0, 256), BIG)
    ts(X("MK4", 0, 4), X("I4", 0, 4), X("PF", 1, 2), Op.is_equal)
    fill(X("RK", 0, 128, 16), T16 - 0.5)
    fill(X("RK", 128, 256, 16), T16 - 0.25)
    for kq in range(4):
        ts(X("WS", 160 * kq, 160 * kq + 160), X("IDW", 0, 160), X("MK4", kq, kq + 1), Op.mult)
    ts(X("DG", 0, 256), X("LM", 0, 256), X("PF", 0, 1), Op.is_equal)
    tt(X("RW", 0, 256), X("DG", 0, 256), X("LR", 0, 256), Op.mult)
    act(X("RB", 0, 256), X("ON", 0, 256), Act.Copy, scale=-LOW)
    for name in ("Cw", "Sw"):
        for c in range(B, W + 8, 256):
            zero_a(X(name, c, min(c + 256, W + 8)))
    idf = X("IDW", 12, 140)

    def scaled(*names):
        for name in names:
            src, s = {"IDB": (idf, 1.0), "BH": (mat("BOF"), float(B - W)), "BN": (mat("BOF"), -4096.0), "BP": (mat("BOF"), 4096.0),
                      "TP": (mat("TSF"), 4096.0), "IP": (idf, 8192.0), "IN": (idf, -8192.0), "BD": (mat("BOF"), -16777216.0)}[name]
            act(mat(name), src, Act.Copy, scale=s)

    scaled("IDB", "IP", "IN")
    act(X("M0", 0, 256), X("DG", 0, 256), Act.Identity, bias=4096.0, scale=-4096.0)
    act(X("MK", 0, 256), X("DG", 0, 256), Act.Identity, bias=8192.0, scale=-4096.0)
    act(X("MY", 0, 256), X("DG", 0, 256), Act.Identity, bias=4096.0 + W - B, scale=-4096.0)


    def shuffle(u, kqs=range(4), bank=None):
        n = lanes(u) // 4
        for kq in kqs:
            for h in range(4):
                s = 160 * kq + 12 + 4 * (kq - h)
                mm(X(bank or "KP%d" % (kq > 0), 128 + n * kq, 128 + n * kq + n), X("WS", s, s + 128), sf(u, h, None, 4),
                   h == 0, h == 3)

    def lists(u, k0, k1, bank=None):
        c0, c1 = k0 * lanes(u) // 4, k1 * lanes(u) // 4
        ts(X("SU", 256 * u + c0, 256 * u + c1), X(bank or "KP%d" % (k0 > 0), 128 + c0, 128 + c1), float(B), Op.add)

    def repeat(q, to, src, l0, l1, ks=range(4)):
        for k in ks:
            copy(q, X(to, 4 * l0 + k, 4 * l1, 4), X(src[0], src[1] + l0, src[1] + l1))

    def spread(src, l0, l1):
        copy("a", X("CR", 4 * l0, 4 * l1), IND(X(src[0], src[1] + l0, src[1] + l1), X("CL", 0, (l1 - l0) // 4)))

    def spread_t(src, ks):
        for k in ks:
            mm(X("CP", k, 512, 4), idf, X(src[0], src[1], src[1] + 128), True, True)

    ts(sf(0), X("SI", E0, E0 + LE), float(-B), Op.add)
    shuffle(0)
    repeat("v", "CR", X("CI", E0, E0 + LE), min(NS[0]), LE)
    repeat("v", "CP", X("CI", E0, E0 + LE), 0, 128)
    lists(0, 0, 1)
    lists(0, 1, 4)
    act(X("JA", 0, 16), X("Q16", 0, 16), Act.Identity, bias=X("PF", 0, 1))
    act(X("BG", 0, 8), X("BOF", 0, 128, 16), Act.Copy, scale=16.0)

    def late_constants():
        scaled("BN", "BP", "TP", "BH", "BD")
        act(X("RB", 0, 256, 16), X("JA", 0, 16), Act.Identity, bias=float(DUMP - B))
        act(X("JB", 0, 16), X("JA", 0, 16), Act.Identity, bias=float(M), scale=-1.0)
        act(X("JT", 0, 16), X("JA", 0, 16), Act.Identity, bias=-8192.0 * M, scale=8192.0)
        for t, u in enumerate(COUNTED):
            copy("a", X("QV", 16 * t, 16 * t + QS[t]), X("Q16", 0, QS[t]))
            act(X("QV", 16 * t + QS[t], 16 * t + 16), X("Q16", QS[t], 16), Act.Identity, bias=float(lanes(u)), scale=0.0)
        for name, c in (("C14", 14.0 * 16777216.0), ("RH", float(W - B)), ("RA", 65536.0)):
            n = SCRATCH[name][1][1]
            act(X(name, 0, n, p=1), X("ON", 0, n, p=1), Act.Copy, scale=c)
        zero_a(X("PM", M, M + 8))
        copy("v", mat("BOH"), mat("BOF"))
        act(X("RM", 0, 256), X("RW", 0, 256), Act.Identity, bias=-LOW)

    copy_g(X("Cw", 0, B), X("CI", 0, B), B)
    for u in range(U):
        c = B - 1 + M * u - 8192 + 14 * 4096
        iota(X("CZ", 128 * u, 128 * u + 128, p=2), [[0, 128]], c - c % 256, c % 256 - (c - c % 256))
    copy_g(X("Sw", E0, B), X("SI", E0, B), B - E0)
    copy_g(X("Sw", 0, E0), X("SI", 0, E0), E0)

    def chunk(u, ch):
        return ((0, NA[u]), (NA[u], min(lanes(u), LE)), (LE, lanes(u)))[ch]

    def opens(u):
        L, a = lanes(u), NA[u]
        for ch in range(2):
            l0, n = chunk(u, ch)[0], chunk(u, ch)[1] - chunk(u, ch)[0]
            kp = X("KP%d" % ch, 0, 128, p=n)
            if u % ST == 2:
                mm(kp, X("ONK", 0, n, p=1), X("C14", 0, 128, p=1), True, False)
                mm(kp, X("SG", l0, l0 + n), mat("BD"), False, False)
            mm(kp, X("ONK", 0, n, p=1), X("KC", 0, 128, p=1), u % ST != 2, False)
        l0, l1 = (0, min(L, LE)) if u or JOINT else (a, L)
        mm(X("YD", l0, l1), mat("IDB"), X("MY" if u in COPIES else "M0", l0, l1), True, False)
        if u in COPIES:
            mm(X("YB", l0, l1), X("ONK", 0, 128, p=1), X("RH", 0, l1 - l0, p=1), True, False)
        mm(X("KL", 0, L), mat("IDB"), X("MK", 0, L), True, False)

    def counts(u, kq, l0, l1):
        win = X("CI", 0, B) if u == 0 else X("Cw", 0, B + M * (u - 1) if u != ST else B)
        o = 256 * u + lanes(u) // 4 * kq
        return IND(win, X("SU", o + l0 // 4, o + l1 // 4))

    def mg(kq, l0, l1):
        return X("MG", 1024 * kq + 4 * l0, 1024 * kq + 4 * l1)

    def gather(u, kq, l0, l1):
        tt(mg(kq, l0, l1), counts(u, kq, l0, l1), X("CR", 4 * l0, 4 * l1), Op.min)

    def fetch(u, kq):
        s = NS[u][kq]
        copy("a", X("GS", 512 * kq, 512 * kq + 4 * s), counts(u, kq, 0, s))

    def smaller(u, kq):
        s = NS[u][kq]
        if kq in SPLIT:
            for i in range(4):
                tt(X("MG", 1024 * kq + i, 1024 * kq + 4 * s, 4), X("GS", 512 * kq + i, 512 * kq + 4 * s, 4),
                   X("CP", i, 4 * s, 4), Op.min)
        else:
            tt(mg(kq, 0, s), X("GS", 512 * kq, 512 * kq + 4 * s), X("CP", 0, 4 * s), Op.min)

    def keys(u, ch, kq):
        l0, l1 = chunk(u, ch)
        for i in range(4):
            mm(X(("KP0", "KP1", "CP")[ch], 4 * kq + i, 128, 16, p=l1 - l0), X("MG", 1024 * kq + 4 * l0 + i, 1024 * kq + 4 * l1, 4),
               X("BG", 0, 8), False, 4 * kq + i == 15)

    def yw(u, l0, l1):
        q0 = l0 // 16 + l0 // 16 % 2
        return X("YW", q0, q0 + (l1 - l0) // 16)

    def chosen(u, l0=0, l1=None):
        return X("OS", 256 * (u % 2) + l0, 256 * (u % 2) + (lanes(u) if l1 is None else l1))

    def best(u, ch):
        kp, ff, oh = ("KP0", "KP1", "CP")[ch], "FF%d" % ch, "OH%d" % ch
        l0, l1 = chunk(u, ch)
        n = l1 - l0
        scan(X(ff, 0, 128, p=n), X("RK", 0, 128, p=n), X(kp, 0, 128, p=n), T16 - 0.5, Op.min, Op.max)
        scan(REV(kp, n, 128), X("RK", 128, 256, p=n), REV(kp, n), T16 - 0.25, Op.min, Op.max)
        yield
        tt(X(oh, 0, 128, p=n), X(ff, 0, 128, p=n), X(kp, 128, 256, p=n), Op.is_equal)
        mm(X("OT", l0, l1), X(oh, 0, 128, p=n), X("IDB", 0, n, p=n), True, True)
        mm(X("O2", l0, l1), X(oh, 0, 128, p=n), X("IDB", 0, n, p=n), True, True)
        yield

    def targets(u, l0, l1, own=None, late=False, both=False):
        n = l1 - l0
        os = chosen(u, l0, l1)
        copy("a", os, X("O2", l0, l1))
        if late:
            mm(X("YD", l0, l1), mat("IDB"), X("M0", l0, l1), True, False)
        tt(X("PT", l0, l1), sf(u, l0, l1), X("OT", l0, l1), Op.mult)
        for o in [X("YD", l0, l1)] + ([X(own, 384, 384 + n)] if own else []) + [X("YB", l0, l1)] * (both or not own):
            mm(o, mat("BOH"), X("PT", l0, l1), o[0] != "YD" and u not in COPIES, u not in COPIES)
            if u in COPIES:
                mm(o, mat("BH"), os, False, True)
        mm(X("KL", l0, l1), mat("BOH"), X("PT", l0, l1), False, False)
        mm(X("KL", l0, l1), mat("BN"), os, False, False)
        yield
        scan(X("WF", l0, l1), X("RB", l0, l1), X("YD", l0, l1), 0.0, Op.max, Op.min)
        yield
        ts(yw(u, l0, l1), X("WF", l0 + 15, l1, 16), float(B), Op.add)
        yield
        copy("a", X("CY", l0, l1), IND(X("Cw", 0, W + 8) if u else X("CI", 0, B + 8), yw(u, l0, l1)))
        yield

    def succs(u, l0, l1):
        copy("a", reg("SY", u, l0, l1), IND(X("Sw", 0, W + 8) if u else X("SI", 0, B + 8), yw(u, l0, l1)))

    def pairs(u, q, c0, c1, last, yb="YB", o=0):
        d = 16 * q
        ts(eq(q, c0 - d, c1 - d), X(yb, o + c0, o + c1), X("WF", d + 15, d + 16), Op.is_equal)
        c0 = max(c0, d + 16)
        if c0 < c1:
            mm(X("KL", c0, c1), mat("BP"), eq(q, c0 - d, c1 - d), False, False)

    def eq(q, c0, c1):
        return ("EQ", 256 * q + c0, 256 * q + c1, 1, T["EQ"][:, q, c0:c1], None)

    def within(q0, q1, last):
        out = X("KL", 16 * q0, 16 * q1)
        emit("t", lambda: g.tensor.matmul(out[4], T["TP"][:, :], T["EQ"][:, q0:q1, 0:16], False, last), [out],
             [mat("TP")] + [eq(q, 0, 16) for q in range(q0, q1)], ns=60)

    def lane_min(u, l0, l1, c):
        tt(reg("MM", u, l0, l1), X("CY", l0, l1), X(c, 4 * l0, 4 * l1, 4), Op.min)

    def signs(u):
        L = lanes(u)
        act(X("SG", 0, L), X("KL", 0, L), Act.Sign, bias=-1500.0)
        mm(X("O2", 256, 256 + L), X("ONK", 0, 128, p=1), X("RA", 0, L, p=1), True, False)
        mm(X("O2", 256, 256 + L), mat("BN"), X("SG", 0, L), False, True)

    def firsts(u):
        L = lanes(u)
        scan(X("FK", 0, L), X("RB", 0, L), X("KL", 0, L), 0.0, Op.max, Op.min)

    def ranks(u):
        L = lanes(u)
        scan(X("RS", 0, L), X("ON", 0, L), X("O2", 256, 256 + L), -(M + 0.5) * 8192.0, Op.mult, Op.add)

    def small_ranks(u):
        L = lanes(u)
        act(X("RKB", 0, L), X("RS", 0, L), Act.Identity, bias=M + 0.5, scale=1.0 / 8192.0)
        if u % ST == 0:
            act(X("OV", 0, L), X("RS", 0, L), Act.Relu, bias=0.5, scale=1.0 / 8192.0)

    def inverse(u, q0, q1):
        L = lanes(u)
        for q in (range(q1 - 1, q0 - 1, -1) if u in COUNTED else range(q0, q1)):
            p0 = 0 if u in COUNTED and q < 2 else 16 * q
            act(X("JK", 256 * q, 256 * q + L - p0), X("RS", p0, L), Act.Sign, bias=X("JB", q, q + 1),
                scale=1.0 / 8192.0, acc=X("ACC", q, q + 1))

    def inverse_v(u, q):
        L = lanes(u)
        jv = X("JK", 256 * q, 256 * q + L - 16 * q)
        ts(jv, X("RS", 16 * q, L), X("JT", q, q + 1), Op.is_gt, 2.0, Op.mult)
        yield
        emit("v", lambda: g.vector.tensor_reduce(T["ACC"][:, q:q + 1], jv[4], AxisListType.X, Op.add),
             [X("ACC", q, q + 1)], [jv], ns=CYC * (L - 16 * q))
        yield

    def inv_a(q1, t=None):
        tt(X("IV", 0, q1), X("ACC", 0, q1), X("Q16", 0, q1) if t is None else X("QV", 16 * t, 16 * t + q1), Op.subtract)

    def inv_b(u, q1, out=None):
        ts(out or X("INV", 16 * u, 16 * u + q1), X("IV", 0, q1), -0.5, Op.mult, lanes(u) / 2.0, Op.add)

    def close_up(name, u):
        copy("a", new(name + "w", u), IND(regw({"C": "MM", "S": "SY"}[name], u), X("INV", 16 * u, 16 * u + Q9)))

    def links(u):
        L = lanes(u)
        z = X("KP1", 128, 128 + L)
        mm(z, X("CZ", 128 * u, 128 * u + 128, p=2), X("ONK", 0, L, p=2), True, False)
        mm(z, mat("IP"), chosen(u), False, False)
        mm(z, mat("BN"), X("SG", 0, L), False, False)
        if u % ST == 0:
            mm(z, mat("IN"), X("OV", 0, L), False, False)
        mm(z, mat("IDB"), X("RKB", 0, L), False, True)

    def relink(u):
        t, e = divmod(u, ST)
        x = (X("Sw", E0 + LE * t, E0 + LE * t + lanes(u)), new("Sw", u - 1), reg("SY", u - 1) if e == 2 else None)[e]
        tt(x, x, X("KP1", 128, 128 + lanes(u)), Op.max)

    def sub(u, l0=0, l1=None):
        l1 = lanes(u) if l1 is None else l1
        if l0 < l1:
            tt(IND(X("Cw", 0, CW), X("OFY", l0 // 16, l1 // 16)), X("CY", l0, l1), reg("MM", u, l0, l1), Op.subtract)

    sent = [0]

    def send(dst, src, sem):
        nxt = T.cores[(rank + 1) % len(T.cores)]
        rid, pid, _ = topo.addr(nxt)
        en = topo.engines(core, nxt)[0::2]
        sent[0] += len(en)
        emit("g", lambda: g.remote_dma(dst[4], src[4], T.sem[sem], T.sem["left"], pid, rid, sum(1 << x for x in en)),
             [dst], [src], sem=sem, n=len(en), remote=True, ns=500)

    Q9 = M // 16
    ent = X("Cw", E0 + LE, B)
    for u in range(U):
        t, e = divmod(u, ST)
        L, a, s = lanes(u), NA[u], NS[u]
        nxt = {c: 0 for c in "fFgmpABPirlcqabdyzenk"}
        stages = {"a": best(u, 0), "b": best(u, 1), "d": best(u, 2), "y": targets(u, 0, LE),
                  "z": targets(u, LE, L, own="KP1", late=True)}
        for c in ORDER[u]:
            kq = nxt[c]
            nxt[c] += 1
            if c == "f":
                fetch(u, kq)
            elif c == "g":
                if kq == 0:
                    if e:
                        lists(u, 1, 4)
                    opens(u)
                gather(u, kq, s[kq], LE if u == ST else L)
            elif c == "m":
                smaller(u, kq)
            elif c == "F":
                copy("a", X("GP", 4 * LP * kq, 4 * LP * (kq + 1)), counts(u, kq, LE, L))
            elif c == "p":
                tt(mg(kq, LE, L), X("GP", 4 * LP * kq, 4 * LP * (kq + 1)), X("YB", 256, 256 + 4 * LP), Op.min)
            elif c in "ABP":
                if c == "P" and kq == 0:
                    mm(X("CP", 0, 128, p=LP), X("ONK", 0, LP, p=1), X("KC", 0, 128, p=1), True, False)
                keys(u, "ABP".index(c), kq)
            elif c in stages:
                next(stages[c])
                if c == "y" and kq == 3:
                    succs(u, 0, LE)
            elif c == "e":
                pairs(u, kq, 16 * kq, LE, False)
                if kq == LE // 16 - 1:
                    within(0, LE // 16, False)
            elif c == "k":
                small_ranks(u - 1)
                inverse(u - 1, 3, Q9)
                links(u - 1)
            elif c == "i":
                inverse(u - 1, 0, 3)
            elif c == "r":
                repeat("v", "CR", ent, a, LE)
            elif c == "l":
                inv_a(3)
                inv_b(u - 1, 3, X("PO", 0, 3))
                send(X("PL", 0, 4), X("PO", 0, 4), "arl")
            elif c == "c":
                spread_t(ent, range(CPT[2]))
                repeat("a", "CP", ent, 0, 128, range(CPT[2], 4))
            else:
                copy("a", X("PORT", 0, LP), IND(X("PM", 0, M + 1), X("PL", 0, 3)))
                repeat("a", "YB", ("PORT", -64), 64, 64 + LP)
        hi, lo = best(u, 1), best(u, 0)
        if e == 1:
            small_ranks(u - 1)
            close_up("S", u - 1)
        if e == 2:
            ranks(u - 1)
            small_ranks(u - 1)
            inverse(u - 1, 0, 3)
        if u == 0:
            late_constants()
        mins = [(0, a, "CP"), (a, L, "CR")]
        if u != ST:
            next(hi)
            next(hi)
        if e or JOINT and u == 0:
            if u:
                links(u - 1)
            for _ in lo:
                pass
            if 0 < u < ST:
                shuffle(ST, (2 * u - 2, 2 * u - 1), "KP0")
            y = targets(u, 0, L)
            if u:
                relink(u - 1)
            next(y)
            if e == 2:
                inverse(u - 1, 3, 7)
            if 0 < u < ST:
                lists(ST, 2 * u - 2, 2 * u, "KP0")
            if e == 1:
                copy("a", new("Cw", u - 1), X("CC", 0, M))
            if u == 4:
                close_up("S", 1)
                close_up("S", 2)
                close_up("C", 2)
                yc_new(2)
            if u == 5:
                ys_out(B + 2 * M, B + 4 * M)
            next(y)
        elif u == 0:
            c1, c2 = (a, L), (0, a)
            y1, y2 = targets(u, *c1, own="KP1", both=True), targets(u, *c2, late=True)
            next(lo)
            next(y1)
            next(lo)
            next(y1)
            next(y1)
            next(y2)
            next(y1)
            for q in range(c1[0] // 16, c1[1] // 16):
                pairs(u, q, 16 * q, c1[1], False, "KP1", 384 - c1[0])
            within(c1[0] // 16, c1[1] // 16, False)
            next(y2)
            y = y2
        if u == 1:
            ys_out(E0, E0 + LE)
        if e == 2:
            inverse(u - 1, 7, Q9)
        if u == 4:
            ys_out(E0 + LE, B + 2 * M)
        if u == ST:
            succs(u, LE, L)
            close_up("C", 1)
            for q in range(L // 16):
                pairs(u, q, max(16 * q, LE), L, False, "KP1", 384 - LE)
            within(LE // 16, L // 16, True)
            tt(reg("MM", u, 0, LE), X("CY", 0, LE), X("Cw", E0 + LE, E0 + 2 * LE), Op.min)
            tt(reg("MM", u, LE, L), X("CY", LE, L), X("PORT", 0, LP), Op.min)
        else:
            blocks = range(L // 16 if e or JOINT else a // 16)
            for q in blocks:
                if q == (e == 2):
                    for _ in y:
                        pass
                    succs(u, 0, L)
                pairs(u, q, 16 * q, L, False)
            within(0, blocks[-1] + 1, True)
            for m in mins:
                lane_min(u, *m)
        fk = X("FK", 15, L, 16)
        if e == 0:
            if u:
                inv_a(Q9)
            else:
                ts(X("CL", 0, 32), X("C4", 0, 32), X("PF", 1, 2), Op.add)
                fill(X("PO", 0, 4), 0)
                ts(sf(ST), X("SI", E0 + LE, B), float(-B), Op.add)
            signs(u)
            if u:
                inv_b(u - 1, Q9)
            firsts(u)
            ranks(u)
            if u:
                relink(u - 1)
            inverse(u, 0, QS[t])
            share = [inverse_v(u, q) for q in range(QS[t], Q9)]
            for x in share:
                next(x)
            scan(X("RW", 0, L), X("RM", 0, L), X("RS", 0, L), -LOW, Op.max, Op.min)
            for x in share:
                next(x)
            tt(X("TO", 0, L // 16), fk, X("RW", 15, L, 16), Op.max)
            if SB[t]:
                ts(X("OFY", 0, L // 16), X("TO", 0, L // 16), float(B), Op.add)
            tt(X("IV", 2, Q9), X("ACC", 2, Q9), X("QV", 16 * t + 2, 16 * t + Q9), Op.subtract)
            if not SB[t]:
                ts(X("OFY", 0, L // 16), X("TO", 0, L // 16), float(B), Op.add)
            sub(u, 0, SB[t])
            ts(X("INV", 16 * u + 2, 16 * u + Q9), X("IV", 2, Q9), -0.5, Op.mult, L / 2.0, Op.add)
            ts(X("INV", 16 * u, 16 * u + 2), X("ACC", 0, 2), -0.5, Op.mult, L / 2.0, Op.add)
            ts(sf(u + 1), IND(regw("SY", u), X("INV", 16 * u, 16 * u + Q9)), float(-B), Op.add)
            copy("a", X("CC", 0, M), IND(regw("MM", u), X("INV", 16 * u, 16 * u + Q9)))
            spread(X("CC", 0, M), min(NS[u + 1]), M)
            shuffle(u + 1)
            spread_t(X("CC", 0, M), range(CPT[0]))
            repeat("a", "CP", X("CC", 0, M), 0, 128, range(CPT[0], 4))
            sub(u, SB[t])
            lists(u + 1, 0, 1)
        elif e == 1:
            spread(reg("MM", u), min(NS[u + 1]), M)
            ts(sf(u + 1), reg("SY", u), float(-B), Op.add)
            shuffle(u + 1)
            firsts(u)
            signs(u)
            spread_t(reg("MM", u), range(CPT[1]))
            repeat("a", "CP", reg("MM", u), 0, 128, range(CPT[1], 4))
            ts(X("OFY", 0, L // 16), fk, float(B), Op.add)
            lists(u + 1, 0, 1)
            sub(u)
        else:
            if u < U - 1:
                send(X("PM", 0, M), reg("MM", u), "arm")
            inv_a(Q9)
            firsts(u)
            inv_b(u - 1, Q9)
            signs(u)
            if u == U - 1:
                close_up("C", u - 1)
                yc_new(u - 1)
            ts(X("OFY", 0, L // 16), fk, float(B), Op.add)
            sub(u)
            ranks(u)
    u = U - 1
    dma("y", D("yc", 0, B + 2 * M), X("Cw", 0, B + 2 * M))
    dma("y", D("yc", B + 3 * M, B + 4 * M), new("Cw", 3))
    small_ranks(u)
    links(u)
    inverse(u, 0, QS[2])
    share = [inverse_v(u, q) for q in range(QS[2], Q9)]
    for _ in range(2):
        for x in share:
            next(x)
    relink(u)
    tt(X("IV", 2, Q9), X("ACC", 2, Q9), X("QV", 32 + 2, 32 + Q9), Op.subtract)
    copy("v", new("Sw", u - 1), IND(regw("SY", u - 1), X("INV", 16 * (u - 1), 16 * (u - 1) + Q9)))
    ts(X("INV", 16 * u + 2, 16 * u + Q9), X("IV", 2, Q9), -0.5, Op.mult, M / 2.0, Op.add)
    ts(X("INV", 16 * u, 16 * u + 2), X("ACC", 0, 2), -0.5, Op.mult, M / 2.0, Op.add)
    copy("v", new("Sw", u), IND(regw("SY", u), X("INV", 16 * u, 16 * u + Q9)))
    ys_out(W - 2 * M, W)
    close_up("C", u)
    yc_new(u, "a")
    for i in (order() if AUTO else range(len(calls))):
        issue(i)
    g.wait_ge(T.sem["left"], sent[0])
    for q in cnt:
        g.wait_ge(T.sem[semname(q)], cnt[q] * inc[q])
